import numpy as np, ml_dtypes
CORES = [83,85,87,115,117,119]
N = 6
BF = ml_dtypes.bfloat16
def gentries(a):
    return np.ascontiguousarray(a.reshape(8, 16, -1).transpose(0, 2, 1)).reshape(8, -1)
def gtable(e):
    e = np.asarray(e); return np.ascontiguousarray(e.reshape(8, -1, 16).transpose(0, 2, 1)).reshape(128, -1).astype(np.int32)
PL, D, P, T, H, S, Q4 = 2048, 1024, 256, 4, 2, 8, 512
def entry(rng, *shape):
    return np.where(rng.random(shape) < 0.5, rng.integers(0, PL, shape), PL + rng.integers(0, D, shape))
def parts(rng):
    x = rng.integers(0, 64, (N, 8, 16, PL)); a = entry(rng, N, 8, 16, D); b = entry(rng, N, 8, 16, D); z = rng.integers(0, 64, (N, 8, 16, P))
    v = rng.integers(0, D, (N, 8, P)); p = rng.integers(0, D, (N, 8, P)); w = rng.integers(0, 256, (N, 8, 16)); h = rng.integers(100, 401, (N, 8, 16))
    return x, a, b, z, v, p, w, h
def pack(x, a, b, z, v, p, w, h):
    return {"xl": np.reshape(x, (N, 128, PL)).astype(np.float32).astype(BF), "vdir": np.reshape(a, (N, 128, D)).astype(np.int32), "pdir": np.reshape(b, (N, 128, D)).astype(np.int32),
            "z": np.reshape(z, (N, 128, P)).astype(np.float32).astype(BF), "vn": np.stack([gtable(e) for e in v]), "pn": np.stack([gtable(e) for e in p]),
            "wt": np.reshape(w, (N, 128, 1)).astype(np.int32), "th": np.reshape(h, (N, 128, 1)).astype(np.int32)}
def setup_inputs(rng):
    return pack(*parts(rng))
def setup_inputs_spread(rng):
    x, a, b, z, v, p, w, h = parts(rng)
    x = (np.exp2(6 * rng.random((N, 8, 1, PL))) * rng.random((N, 8, 16, PL))).astype(np.int64); z = (np.exp2(6 * rng.random((N, 8, 1, P))) * rng.random((N, 8, 16, P))).astype(np.int64)
    x = np.minimum(x, 63); z = np.minimum(z, 63)
    def uneven(n, *shape):
        r = rng.random(shape) ** 3
        return np.minimum((n * np.where(rng.random(shape) < 0.5, r, 1 - r)).astype(np.int64), n - 1)
    a = uneven(PL + D, N, 8, 16, D); b = uneven(PL + D, N, 8, 16, D); v = uneven(D, N, 8, P); p = uneven(D, N, 8, P)
    w = np.minimum((np.exp2(8 * rng.random((N, 8, 16))) * rng.random((N, 8, 16))).astype(np.int64), 255)
    h = np.minimum(np.exp2(10 * rng.random((N, 8, 16))).astype(np.int64) - 1, 1008); h[:, :, 3] = 1008; w[:, :, 3] = 255
    return pack(x, a, b, z, v, p, w, h)
def tips(rng, shape, hi, inner):
    e = hi * rng.integers(0, 2, shape); o = np.where(rng.random(shape) < 0.5, rng.choice(np.array(inner), shape), rng.integers(0, hi + 1, shape))
    return np.where(rng.random(shape) < 0.8, e, o)
def setup_inputs_ends(rng):
    m = rng.integers(0, 3, (N, 8, 1, PL)); x = 63 * np.where(m == 2, rng.integers(0, 2, (N, 8, 16, PL)), m)
    m = rng.integers(0, 3, (N, 8, 1, P)); z = 63 * np.where(m == 2, rng.integers(0, 2, (N, 8, 16, P)), m)
    top = PL + D - 1; w = 255 * rng.integers(0, 2, (N, 8, 16)); h = 1008 * rng.integers(0, 2, (N, 8, 16))
    a = tips(rng, (N, 8, 16, D), top, [PL - 1, PL, 1]); b = tips(rng, (N, 8, 16, D), top, [PL - 1, PL, 1])
    v = tips(rng, (N, 8, P), D - 1, [1, D - 2]); p = tips(rng, (N, 8, P), D - 1, [1, D - 2])
    for g in (0, 7):
        w[:, g] = 255; h[:, g, 0] = 0; h[:, g, 1] = 1008; h[:, g, 14] = 0; h[:, g, 15] = 1008
        for c in (0, D - 1):
            x[:, g, :, c] = 0; a[:, g, :, c] = top * rng.integers(0, 2, (N, 16)); b[:, g, :, c] = top * rng.integers(0, 2, (N, 16))
        for c in (Q4 - 2, 2 * Q4 - 2, 3 * Q4 - 2, PL - 2, PL - 1): x[:, g, :, c] = 63
        for i in (0, 1, P - 1): z[:, g, :, i] = 63
        for i in (2, P - 2): z[:, g, :, i] = 0
        for i, c in ((0, D - 1), (1, 0), (2, D - 1), (P - 2, 0), (P - 1, D - 1)): v[:, g, i] = c; p[:, g, i] = c
    return pack(x, a, b, z, v, p, w, h)
def setup_inputs_corners(rng):
    x, a, b, z, v, p, w, h = parts(rng); own = np.arange(D)[None, :]
    h = np.where(rng.random(h.shape) < 0.6, rng.choice(np.array([0, 1, 1007, 1008]), h.shape), h); w = np.where(rng.random(w.shape) < 0.5, rng.choice(np.array([0, 1, 255]), w.shape), w)
    for q in range(N):
        o = rng.permutation(8)
        for g in range(8):
            c = int(o[g])
            if c == 0:
                a[q, g] = rng.integers(0, PL, (16, D)); b[q, g] = rng.integers(0, PL, (16, D))
                k = rng.choice(np.array([0, 15]), P); e = a[q, g][k, v[q, g]]; m = np.arange(P) % 3 == 0
                z[q, g] = np.where(m[None, :], x[q, g][:, e], z[q, g])
            elif c == 1: a[q, g] = PL + rng.integers(0, D, (16, D)); b[q, g] = PL + rng.integers(0, D, (16, D))
            elif c == 2: a[q, g] = PL + rng.integers(0, D, (16, D)); b[q, g] = rng.integers(0, PL, (16, D))
            elif c == 3:
                a[q, g] = np.where(own % 2 == 0, PL + rng.integers(0, D, (16, D)), rng.integers(0, PL, (16, D)))
                b[q, g] = PL + 2 * rng.integers(0, D // 2, (16, D)) + 1; v[q, g] = 2 * rng.integers(0, D // 2, P)
            elif c == 4:
                a[q, g] = PL + own; b[q, g] = PL + own; b[q, g, 8:] = PL + (own + 1) % D
            elif c == 5:
                a[q, g] = rng.choice(np.array([0, PL - 1, PL, PL + D - 1]), (16, D)); b[q, g] = rng.choice(np.array([0, PL - 1, PL, PL + D - 1]), (16, D)); w[q, g] = 0
            elif c == 6:
                a[q, g] = PL + (D - 1) * rng.integers(0, 2, (16, D)); w[q, g] = 255
            else:
                p[q, g] = v[q, g]; v[q, g, 0] = 0; v[q, g, P - 1] = D - 1; p[q, g, 0] = D - 1; p[q, g, P - 1] = 0
    return pack(x, a, b, z, v, p, w, h)
def setup_inputs_crowd(rng):
    x, a, b, z, v, p, w, h = parts(rng)
    for q in range(N):
        for g in range(8):
            c, e = rng.permutation(D)[:P], rng.permutation(D)[:P]; s, t = int(rng.integers(0, D)), int(rng.integers(0, D))
            if g == 0: c[:] = s
            elif g == 1: e[:] = s
            elif g == 2: c[:] = s; e[:] = t
            elif g == 3: c[:] = s; c[P - 1] = (s + 1) % D
            elif g == 4: e[:] = s; e[0] = (s + 1) % D
            elif g == 5: c = rng.choice(np.array([0, D - 1]), P); e = rng.choice(np.array([0, D - 1]), P)
            elif g == 6 and q < N - 1:
                if q % 2 == 0: e[P - 1] = e[0]
                else: c[P - 1] = c[0]
            elif g == 7: c[:] = s; e[:] = t; z[q, g] = z[q, g, :, :1]
            v[q, g] = c; p[q, g] = e
    h[0] = 0; h[N - 1] = 0; h[N - 1, 6, 15] = 1
    x[1] = 56 + (x[1] >> 3); z[1] = 56 + (z[1] >> 3); h[1] = rng.integers(630, 801, (8, 16))
    x[2] = x[2] >> 3; z[2] = 30 * z[2] >> 6; h[2] = rng.integers(480, 761, (8, 16))
    m = 2 * int(rng.integers(10, 20)) + 1; j = rng.permutation(P)[:m]; k = rng.permutation(16)
    z[2, 5][:, j] = rng.integers(45, 52, (16, m)); h[2, 5, k[:5]] = rng.integers(480, 609, 5); h[2, 5, k[5:]] = rng.integers(820, 1009, 11)
    x[N - 1, 6, 0] = 63; z[N - 1, 6, 0] = rng.integers(0, 63, P); n = int(rng.integers(0, PL))
    a[N - 1, 6, 15, v[N - 1, 6, P - 1]] = n; z[N - 1, 6, :, P - 1] = x[N - 1, 6, :, n]
    return pack(x, a, b, z, v, p, w, h)
def setup_inputs_ties(rng):
    x, a, b, z, v, p, w, h = parts(rng)
    for q in range(N):
        few = q in (1, 3)
        for g in range(8):
            if g % 2 == 0:
                y = rng.integers(21 if few else 0, 41, (16, 1)); x[q, g] = y + 3 * rng.integers(0, 6, (1, PL)); z[q, g] = y + 3 * rng.integers(0, 8, (1, P))
                h[q, g] = rng.choice(np.array([0, 1, 48, 49, 96, 97, 144, 145]), 16)
                if few: h[q, g] = np.sum(y) + 48 * rng.integers(1, 6, 16) - rng.permutation(16) // 6
            else:
                x[q, g] = rng.integers(0, 64, (16, 8))[:, rng.integers(0, 8, PL)]
                v[q, g] = rng.permutation(D)[:P]; p[q, g] = rng.permutation(D)[:P]
                if g % 4 == 1: v[q, g, P - 1] = v[q, g, 0]
                else: p[q, g, P - 1] = p[q, g, 0]
                if few: x[q, g] = x[q, g] >> 2; z[q, g] = z[q, g] >> 2; h[q, g] = rng.integers(241, 301, 16)
    m = rng.permutation(3) + 1
    for i, q in ((0, 1), (1, 3)):
        z[q, 7, :, P - 1] = 62; k = rng.permutation(16)[int(m[i]):]; h[q, 7, k] = 1008
    return pack(x, a, b, z, v, p, w, h)
def check_inputs(d):
    bad = []
    for k, hi in (("xl", 63), ("vdir", PL + D - 1), ("pdir", PL + D - 1), ("z", 63), ("vn", D - 1), ("pn", D - 1), ("wt", 255), ("th", 1008)):
        e = np.asarray(d[k]).astype(np.float64)
        if not (np.min(e) >= 0 and np.max(e) <= hi): bad.append("range of " + k)
        elif not np.all(e == np.floor(e)): bad.append("whole numbers in " + k)
    return bad
def reference(xl, vdir, pdir, z, vn, pn, wt, th):
    X = xl.astype(np.float32).astype(np.int64).reshape(N, 8, 16, PL); Z = z.astype(np.float32).astype(np.int64).reshape(N, 8, 16, P)
    VD = vdir.astype(np.int64).reshape(N, 8, 16, D); PD = pdir.astype(np.int64).reshape(N, 8, 16, D)
    w = wt.astype(np.int64).reshape(N, 8, 16, 1); h = th.astype(np.int64).reshape(N, 8, 16, 1)
    v = np.stack([gentries(a) for a in vn]).astype(np.int64); p = np.stack([gentries(a) for a in pn]).astype(np.int64)
    A = np.zeros(N, np.int64); lower = np.tri(P, P, -1, dtype=bool)
    for t in range(T):
        if t > 0: v, p, Z = np.roll(v, 1, axis=0), np.roll(p, 1, axis=0), np.roll(Z, 1, axis=0)
        e = np.take_along_axis(VD, v[:, :, None, :], 3)
        for i in range(H):
            e = np.where(e >= PL, np.take_along_axis(PD if i % 2 == 0 else VD, np.maximum(e - PL, 0), 3), e)
        e = np.where(e >= PL, e - PL, e)
        x = np.take_along_axis(X, e.reshape(N, 8, 1, 16 * P), 3).reshape(N, 8, 16, 16, P)
        d = np.add.reduce(np.abs(x - Z[:, :, :, None, :]), axis=2)
        ks = np.argmin(d, axis=2)[:, :, None, :]
        xs = np.take_along_axis(x, ks[:, :, None], 3)[:, :, :, 0]
        u = np.add.reduce(w * Z, axis=2) & 4095
        n = S * np.arange(P) + (u & (S - 1))
        near = d < h + (A & 255)[:, None, None, None]
        np.put_along_axis(e, ks, n[:, :, None, :], 2)
        np.put_along_axis(X, n[:, :, None, :], (xs + Z) >> 1, 3)
        same = (v[..., :, None] == v[..., None, :]) | (p[..., :, None] == p[..., None, :])
        edits = ~np.any(same & lower, axis=-1)
        tov = np.where(near, e, PL + p[:, :, None, :]); top = np.where(near, PL + v[:, :, None, :], e)
        for q in range(N):
            for g in range(8):
                m = edits[q, g]
                VD[q, g][:, v[q, g][m]] = tov[q, g][:, m]; PD[q, g][:, p[q, g][m]] = top[q, g][:, m]
        A = np.add.reduce((1 - near.astype(np.int64)).reshape(N, -1), axis=1)
        p, v = v, ((u * u >> 5) + 37 * v) & (D - 1)
        Z = np.abs(Z - xs)
    yx = X[..., :Q4] + 64 * X[..., Q4:2 * Q4] + 4096 * X[..., 2 * Q4:3 * Q4] + 262144 * X[..., 3 * Q4:]
    return {"yx": yx.reshape(N, 128, Q4).astype(np.float32), "yvd": VD.reshape(N, 128, D).astype(np.float32), "ypd": PD.reshape(N, 128, D).astype(np.float32),
            "yz": Z.reshape(N, 128, P).astype(np.float32).astype(BF), "yvp": (D * p + v).astype(np.float32)}

@@ -1,0 +1,615 @@
+import numpy as np
+from concourse.mybir import AluOpType as A, AxisListType, ActivationFunctionType as F
+
+NV = 4
+ACT_Q = {2: (0, 2), 3: (0, 2)}
+ACT_H = {2: (), 3: ()}
+LOOKS = [(2, 0), (2, 1), (2, 2), (2, 3), (3, 0), (3, 1), (3, 2), (3, 3)]
+DVE_X = (3, 6, 7)
+DVE_ABS = ((1, 1),)
+DVE_KEY = ()
+AHEAD = True
+DIFF_BANKS = ((2, 3, 2, 3), (0, 2, 3, 0))
+DIFF_LAST = DIFF_BANKS
+KEY_BANKS = (4, 1)
+YB = 4
+BETA = 1.7
+TRIES = 3500
+SEED = 1
+REMOTE_ENGINES = 4
+
+f32, bf, f16, i32, u16 = "float32", "bfloat16", "float16", "int32", "uint16"
+SCRATCH = {}
+for _n, _c, _d in [
+    ("svd", 1024, i32), ("spd", 1024, i32), ("w2", 3328, f32), ("w3", 3328, f32), ("xw", 3072, bf),
+    ("vpi", 32, i32), ("wti", 16, i32), ("z0", 272, bf), ("pb0", 256, f16),
+    ("e1", 256, u16), ("e2", 256, u16), ("e3", 256, u16), ("ef", 256, f16), ("hi", 256, f16),
+    ("wd0", 1024, f16), ("wd1", 1024, f16), ("wd2", 1024, f16), ("wf", 2048, f32),
+    ("xg", 4096, bf), ("ab", 4096, bf), ("pm", 256, f32), ("st", 288, bf), ("sg", 256, bf), ("acc", 8, f32),
+    ("a2", 768, f32), ("ep", 256, f32), ("sl", 256, bf), ("ku", 16, u16), ("xs", 256, bf), ("nl", 256, bf),
+    ("rb", 256, bf), ("mt", 2176, bf), ("fl", 256, bf), ("vpf", 64, f32),
+    ("ui", 16, i32), ("um", 16, i32), ("ri", 16, i32), ("ru", 16, u16), ("nf", 16, f32), ("nu", 16, u16),
+    ("sq", 16, i32), ("sh", 16, i32), ("v37", 16, f32), ("sm", 16, i32), ("vi", 16, i32),
+    ("dm", 16, f32), ("dd", 16, f32), ("of", 32, f32), ("ou", 32, u16), ("ai", 8, i32), ("aj", 8, i32), ("abias", 8, f32),
+    ("yv", 256, f32), ("yt", 256, f32), ("yxs", 512, f32),
+    ("pi", 8, i32), ("pj", 8, i32), ("col", 16, f32), ("row", 256, f32), ("m16", 16, f32), ("idb", 128, bf), ("idn", 128, bf),
+    ("idh", 128, f16), ("idq", 128, bf), ("ip2", 128, bf), ("in2", 128, bf), ("i64", 128, bf), ("i4k", 128, bf), ("i18", 128, bf),
+    ("bk", 144, bf), ("ky", 256, f32), ("dh", 2048, f16), ("bn", 144, bf), ("bw", 144, bf), ("blk", 128, f32), ("wb", 128, bf),
+    ("sel", 48, bf), ("idf", 128, f32), ("et", 256, f16),
+    ("b8", 128, f32), ("par", 128, f32), ("pair", 64, f16), ("n8", 128, f16), ("t8", 1024, bf), ("th2", 256, bf), ("oneh", 128, f16), ("onef", 128, f32), ("kc", 256, f16), ("rst", 128, f32),
+    ("mix", 8, u16), ("jl", 16, f32), ("dt", 16, f32), ("j8r", 16, f32), ("jc", 16, f16), ("j8c", 256, bf),
+    ("m128", 128, bf), ("pw", 64, f32),
+]:
+    SCRATCH[_n] = ("sbuf", [128, _c], _d)
+for _t in range(NV):
+    SCRATCH["zo%d" % _t] = ("sbuf", [128, 272], bf)
+    SCRATCH["po%d" % _t] = ("sbuf", [128, 32], u16)
+    SCRATCH["vb%d" % _t] = ("sbuf", [128, 256], f16)
+    SCRATCH["pl%d" % _t] = ("sbuf", [128, 32], u16)
+    if _t:
+        SCRATCH["z%d" % _t] = ("sbuf", [128, 272], bf)
+        SCRATCH["pb%d" % _t] = ("sbuf", [128, 256], f16)
+for _b in range(8):
+    SCRATCH["ps%d" % _b] = ("psum", [128, 512], f32)
+
+ENG = ("pe", "dve", "act", "pool", "sp")
+SEMAPHORES = ["q_" + e for e in ENG[:4]] + ["d%d" % i for i in range(24)] + ["sent"] + \
+             ["r%s%d" % (k, t) for k in "pqbz" for t in range(1, NV)]
+
+MODELS = [dict(cy=1.04, g=1.56, s=3.8, pe=0.52), dict(cy=1.04, g=1.1, s=2.0, pe=0.52), dict(cy=1.04, g=2.0, s=5.5, pe=0.52)]
+HOP = 90.0
+
+
+def build_ops(g, T, topo, core):
+    ops = []
+    V, S, P = g.vector, g.scalar, g.tensor
+    ps = [T["ps%d" % b] for b in range(8)]
+    nxt = T.cores[(T.rank_of(core) + 1) % len(T.cores)]
+    rid, pid, _ = topo.addr(nxt)
+    mask = sum(1 << e for e in topo.engines(core, nxt)[:REMOTE_ENGINES])
+    ndma = [0, -1]
+
+    def op(eng, fn, cost, r, w, kind="c", sem=None):
+        ops.append(dict(eng=eng, fn=fn, cost=cost, r=list(r), w=list(w), kind=kind, sem=sem, visit=ndma[1]))
+
+    def ts(out, in0, s1, o0, n, r, w, s2=None, o1=None, cost="v"):
+        if o1 is None:
+            op("dve", lambda: V.tensor_scalar(out, in0, s1, None, o0), (cost, n), r, w)
+        else:
+            op("dve", lambda: V.tensor_scalar(out, in0, s1, s2, o0, o1), (cost, n), r, w)
+
+    def tt(out, in0, in1, o, n, r, w, cost="v"):
+        op("dve", lambda: V.tensor_tensor(out, in0, in1, o), (cost, n), r, w)
+
+    def cp(out, in_, n, r, w, cost="v"):
+        op("dve", lambda: V.tensor_copy(out, in_), (cost, n), r, w)
+
+    def ms(out, val, n, w):
+        op("dve", lambda: V.memset(out, val), ("v", n), [], w)
+
+    def act(out, in_, func, n, r, w, cost="v", **kw):
+        op("act", lambda: S.activation(out, in_, func, **kw), (cost, n), r, w)
+
+    def many(eng, fns, n, r, w):
+        def fn():
+            last = None
+            for f in fns:
+                last = f()
+            return last
+        op(eng, fn, ("v", n), r, w)
+
+    def pe(mms, r, w):
+        def fn():
+            last = None
+            for o, l, x, s0, s1, c in mms:
+                last = P.matmul(o, l, x, s0, s1)
+            return last
+        op("pe", fn, ("p", sum(m[5] for m in mms)), r, w)
+
+    def iota(out, pattern, base, cm, n, w, flag=True):
+        if flag:
+            op("pool", lambda: g.iota(out, pattern, base, cm, allow_small_or_imprecise_dtypes=True), ("i", n), [], w)
+        else:
+            op("pool", lambda: g.iota(out, pattern, base, cm), ("i", n), [], w)
+
+    def dma(eng, out, in_, nbytes, r, w):
+        q = g.sync if eng == "sp" else g.scalar
+        op(eng, lambda: q.dma_start(out, in_), ("d", nbytes), r, w, kind="dma", sem="d%d" % ndma[0])
+        ndma[0] += 1
+
+    def send(dst, src, sem, nbytes, r, w):
+        op("pool", lambda: g.remote_dma(dst, src, T.sem[sem], T.sem.sent, pid, rid, mask), ("r", nbytes), r, w, kind="send", sem=sem)
+
+    dma("sp", T.vpi[:, 0:16], T.vn[:], 8192, [], ["vpi0"])
+    dma("sp", T.svd[:], T.vdir[:], 524288, [], ["svd"])
+    dma("sp", T.spd[:, 0:512], T.pdir[:, 0:512], 262144, [], ["spd0"])
+    dma("sp", T.spd[:, 512:1024], T.pdir[:, 512:1024], 262144, [], ["spd1"])
+    dma("act", T.vpi[:, 16:32], T.pn[:], 8192, [], ["vpi1"])
+    dma("act", T.wti[:, 0:1], T.wt[:], 512, [], ["wti0"])
+    dma("act", T.wti[:, 8:9], T.th[:], 512, [], ["wti1"])
+    dma("act", T.z0[:, 0:256], T.z[:], 65536, [], ["z0"])
+    dma("sp", T.xw[:, 0:2048], T.xl[:], 524288, [], ["x0", "x1"])
+    dma("sp", T.xw[:, 2048:3072], T.xl[:, 0:1024], 262144, [], ["xd"])
+
+    col = lambda c: T.col[:, c:c + 1]
+    iota(T.pi[:, 0:1], [[0, 1]], 0, 1, 1, ["pi"], flag=False)
+    iota(T.row[:], [[1, 256]], 0, 0, 256, ["row"])
+    iota(T.w2[:, 0:512], [[1, 512]], 0, 0, 512, ["w2a"])
+    iota(T.blk[:], [[16, 8], [0, 16]], 0, 0, 128, ["blk"])
+    iota(T.w3[:, 0:1024], [[1, 1024]], 0, 0, 1024, ["w3a"])
+    iota(T.w3[:, 1024:2048], [[1, 1024]], 1024, 0, 1024, ["w3b"])
+    act(T.w2[:, 512:1024], T.w2[:, 0:512], F.Identity, 512, ["w2a"], ["w2b"], bias=512.0)
+    act(T.w2[:, 1024:2048], T.w2[:, 0:1024], F.Identity, 1024, ["w2a", "w2b"], ["w2c"], bias=1024.0)
+    ts(T.pj[:, 0:1], T.pi[:, 0:1], 15, A.bitwise_and, 1, ["pi"], ["pj0"])
+    ts(T.pj[:, 1:2], T.pi[:, 0:1], 112, A.bitwise_and, 1, ["pi"], ["pj1"])
+    cp(T.col[:, 0:2], T.pj[:, 0:2], 2, ["pj0", "pj1"], ["c01"])
+    cp(col(2), T.pi[:, 0:1], 1, ["pi"], ["c2"])
+    ts(T.m16[:], T.row[:, 0:16], col(0), A.is_equal, 16, ["row", "c01"], ["m16"])
+    ts(T.idb[:], T.row[:, 0:128], col(2), A.is_equal, 128, ["row", "c2"], ["idb"])
+    cp(T.idh[:], T.idb[:], 64, ["idb"], ["idh"])
+    for a in range(4):
+        many("dve", [(lambda k=k: V.tensor_scalar(T.dh[:, 128 * k:128 * k + 128], T.idb[:], T.m16[:, k:k + 1], None, A.mult))
+                     for k in range(4 * a, 4 * a + 4)], 256, ["idb", "m16"], ["dh%d" % a])
+    DH = ["dh%d" % a for a in range(4)]
+    act(T.idf[:], T.idb[:], F.Identity, 128, ["idb"], ["idf"])
+    if ACT_Q[2] or ACT_Q[3]:
+        ts(T.pj[:, 2:3], T.pi[:, 0:1], 1, A.bitwise_and, 1, ["pi"], ["pj2"])
+        ts(T.pj[:, 3:4], T.pi[:, 0:1], 126, A.bitwise_and, 1, ["pi"], ["pj3"])
+        cp(T.col[:, 5:7], T.pj[:, 2:4], 2, ["pj2", "pj3"], ["c56"])
+        iota(T.b8[:], [[0, 8], [1, 2], [0, 8]], 0, 0, 128, ["b8"])
+        ts(T.par[:], T.b8[:], col(5), A.is_equal, 128, ["b8", "c56"], ["par"])
+        ts(T.pair[:], T.row[:, 0:128:2], col(6), A.is_equal, 64, ["row", "c56"], ["pair"])
+        ts(T.n8[:], T.row[:, 0:128], 0.0, A.mult, 128, ["row"], ["n8"], -8.0, A.add)
+    iota(T.t8[:], [[0, 128], [1, 8]], 0, 0, 1024, ["t8"])
+    for name, val in (("idn", -1.0), ("idq", 0.5), ("ip2", 2048.0), ("in2", -2048.0), ("i64", 64.0), ("i4k", 4096.0), ("i18", 262144.0)):
+        act(T[name][:], T.idb[:], F.Identity, 128, ["idb"], [name], scale=val)
+    ts(col(3), col(1), 15.0, A.add, 1, ["c01"], ["c3"])
+    cp(T.col[:, 7:9], T.wti[:, 0:9:8], 2, ["wti0", "wti1"], ["c7", "c8"])
+    ts(T.bn[:], T.row[:, 0:144], col(3), A.is_equal, 144, ["row", "c3"], ["bn"])
+    act(T.bw[:], T.bn[:], F.Identity, 144, ["bn", "c7"], ["bw"], scale=col(7))
+    act(T.bk[:], T.bn[:], F.Identity, 144, ["bn", "c01"], ["bk"], scale=col(0))
+    ms(T.pw[:, 0:16], 1.0 / BETA, 16, ["pw0"])
+    ms(T.pw[:, 16:32], 0.0, 16, ["pw1"])
+    op("dve", lambda: V.tensor_tensor_scan(T.pw[:, 32:48], T.pw[:, 0:16], T.pw[:, 16:32], BETA ** 9, A.mult, A.add), ("v", 16), ["pw0", "pw1"], ["pw2"])
+    tt(T.pw[:, 48:64], T.pw[:, 32:48], T.m16[:], A.mult, 32, ["pw2", "m16"], ["pw3"])
+    op("dve", lambda: V.tensor_reduce(col(4), T.pw[:, 48:64], AxisListType.X, A.add), ("v", 16), ["pw3"], ["c4"])
+    ts(T.wb[:], T.blk[:], col(1), A.is_equal, 128, ["blk", "c01", "c4"], ["wb"], col(4), A.mult)
+    ts(T.sel[:, 8:16], T.blk[:, 0:128:16], col(1), A.is_equal, 8, ["blk", "c01"], ["sel1"])
+    act(T.sel[:, 0:8], T.sel[:, 8:16], F.Identity, 8, ["sel1"], ["sel0"], scale=16.0)
+    if DVE_ABS:
+        act(T.sel[:, 16:32], T.sel[:, 0:16], F.Identity, 16, ["sel0", "sel1"], ["sel2"], scale=2.0)
+        act(T.sel[:, 32:48], T.sel[:, 0:16], F.Identity, 16, ["sel0", "sel1"], ["sel3"], scale=-1.0)
+    scale = [2.0 ** (97 - 13 * jh) for jh in range(16)]
+    many("act", [(lambda jh=jh: S.activation(T.th2[:, 16 * jh:16 * jh + 16], T.m16[:], F.Identity, scale=-2.56 * scale[jh]))
+                 for jh in range(16)], 1024, ["m16"], ["th2"])
+    ms(T.onef[:], 1.0, 128, ["onef"])
+    cp(T.oneh[:], T.onef[:], 128, ["onef"], ["oneh"])
+    ts(T.kc[:, 0:128], T.idb[:], col(0), A.mult, 64, ["idb", "c01"], ["kc0"])
+    ts(T.kc[:, 128:256], T.idb[:], col(8), A.mult, 64, ["idb", "c8"], ["kc1"], -1.0, A.mult)
+    ms(T.rst[:], 0.0, 128, ["rst"])
+    ms(T.rst[:, 0:128:16], 65536.0, 8, ["rst"])
+    ts(T.mix[:], T.blk[:, 0:128:16], 15.0, A.add, 8, ["blk"], ["mix"])
+    ts(T.jl[:], T.row[:, 0:16], 16.0, A.mult, 16, ["row", "c01"], ["jl"], col(0), A.add)
+    act(T.dt[:], T.jl[:], F.Identity, 16, ["jl"], ["dt"], bias=1024.0)
+    act(T.j8r[:, 0:8], T.jl[:, 0:8], F.Identity, 8, ["jl"], ["j8r0"], scale=8.0)
+    act(T.j8r[:, 8:16], T.jl[:, 0:8], F.Identity, 8, ["jl"], ["j8r1"], scale=8.0)
+    ts(T.jc[:], T.jl[:], 16.0, A.mult, 16, ["jl"], ["jc"])
+    iota(T.j8c[:], [[8, 256]], 0, 0, 256, ["j8c"])
+    ms(T.m128[:], -128.0, 64, ["m128"])
+    ms(T.abias[:, 0:1], 0.5, 1, ["abias"])
+
+    cp(T.pl0[:], T.vpi[:], 32, ["vpi0", "vpi1"], ["pl0", "pl0p"])
+    W2I, W3I = ["w2a", "w2b", "w2c"], ["w3a", "w3b"]
+    ident = T.w2[:, 0:1024]
+    IDK = ["w2a", "w2b"]
+    rot = dict(wd=0, wf=0, bank=0, diff=0)
+
+    def repeats(src, skey, c0, vfk, dst, dkey):
+        off, first = 0, True
+        for grp in ((0, 1), (2, 3, 4), (5, 6, 7), (8, 9, 10, 11), (12, 13, 14, 15)):
+            fns, mms, n = [], [], 0
+            if first:
+                mms.append((ps[7][:, 0:256], T.wb[:], T.th2[:], True, False, 256))
+                first = False
+            for jh in grp:
+                wd = 256 - 16 * jh
+                m = T.mt[:, off:off + wd]
+                fns.append(lambda jh=jh, m=m: V.tensor_scalar(m, src[:, 16 * jh:256], T.vpf[:, c0 + jh:c0 + jh + 1], scale[jh], A.is_equal, A.mult))
+                mms.append((ps[7][:, 16 * jh:256], T.wb[:], m, False, jh == 15, max(64, wd)))
+                n += max(64, wd // 2)
+                off += wd
+            many("dve", fns, n, [skey, vfk], ["mt%d" % grp[0]])
+            pe(mms, ["mt%d" % grp[0], "wb", "th2"], ["B7"])
+        act(T.fl[:], ps[7][:, 0:256], F.Sign, 256, [], ["B7", "fl"])
+        pe([(ps[7][:, 256:272], T.bn[:, 15 - jl:143 - jl], T.fl[:, jl:256:16], jl == 0, jl == 15, 64) for jl in range(16)], ["bn", "fl"], ["B7"])
+        act(dst, ps[7][:, 256:272], F.Identity, 16, [], ["B7", dkey], scale=1.0 / 16)
+
+    def prepare(t):
+        pl, plk, f0, vfk = T["pl%d" % t], "pl%d" % t, 32 * (t % 2), "vpf%d" % (t % 2)
+        cp(T.vpf[:, f0:f0 + 32], pl[:], 32, [plk, plk + "p"], [vfk])
+        cp(T["vb%d" % t][:], ident.indirect(pl[:, 0:16]), 256, IDK + [plk], ["vb%d" % t], cost="g")
+        repeats(T["vb%d" % t], "vb%d" % t, f0, vfk, T["zo%d" % t][:, 256:272], "zos%d" % t)
+
+    for t in range(NV):
+        z, zo, pl, po, vb, pb = (T["%s%d" % (n, t)] for n in ("z", "zo", "pl", "po", "vb", "pb"))
+        zk, plk, pbk, vbk = "z%d" % t, "pl%d" % t, "pb%d" % t, "vb%d" % t
+        ndma[1] = t
+        last = t == NV - 1
+
+        if t == 0:
+            cp(T.e1[:], T.svd[:, 0:1024].indirect(pl[:, 0:16]), 256, ["svd", plk], ["e1"], cost="g")
+            for a in range(2):
+                cp(T.w2[:, 2048 + 512 * a:2560 + 512 * a], T.spd[:, 512 * a:512 * a + 512], 512, ["spd%d" % a], ["pd%d" % a])
+            for a in range(2):
+                cp(T.w3[:, 2048 + 512 * a:2560 + 512 * a], T.svd[:, 512 * a:512 * a + 512], 512, ["svd"], ["vd%d" % a])
+        else:
+            cp(T.e1[:], T.w3[:, 2048:3072].indirect(pl[:, 0:16]), 256, ["vd0", "vd1", plk], ["e1"], cost="g")
+        for lk, q in LOOKS:
+            win, wk = (T.w2, W2I + ["pd0", "pd1"]) if lk == 2 else (T.w3, W3I + ["vd0", "vd1"])
+            src, sk = (T.e1, "e1") if lk == 2 else (T.e2, "e2%d" % q)
+            dst, dk = (T.e2, "e2%d" % q) if lk == 2 else (T.e3, "e3%d" % q)
+            gath = win[:, 0:3072].indirect(src[:, 64 * q:64 * q + 64])
+            if q // 2 in ACT_H[lk]:
+                act(T.wf[:, 1024 * (q % 2):1024 * (q % 2) + 1024], gath, F.Identity, 1024, wk + [sk], ["wf%d" % (q % 2)], cost="g")
+                if q % 2:
+                    for a in range(8):
+                        pe([(ps[5][:, k:128:16], T.wf[:, k:2048:16], T.idf[:, k:128:16], k == 0, k == 15, 256) for k in range(2 * a, 2 * a + 2)], ["idf", "wf0", "wf1"], ["B5"])
+                    ts(T.et[:, 0:128], ps[5][:, 0:128], -1024.0, A.add, 128, [], ["B5", "et0"])
+                    pe([(ps[5][:, 128:256], T.et[:, 0:128], T.idh[:], True, True, 128)], ["et0", "idh"], ["B5"])
+                    ts(dst[:, 64 * q - 64:64 * q + 64], ps[5][:, 128:256], 1024.0, A.add, 128, [], ["B5", dk, dk[:2] + str(q - 1)])
+                continue
+            if q in ACT_Q[lk]:
+                s = rot["wf"] % 2; rot["wf"] += 1
+                o0, b, et = 1024 * s, 5 + s, T.et[:, 128 * s:128 * s + 128]
+                act(T.wf[:, o0:o0 + 1024], gath, F.Identity, 1024, wk + [sk], ["wf%d" % s], cost="g")
+                pe([(ps[b][:, 0:128], T.oneh[:], T.n8[:], True, False, 128)], ["oneh", "n8"], ["B%d" % b])
+                for a in range(4):
+                    pe([(ps[b][:, k:128:8], T.wf[:, o0 + k:o0 + 1024:8], T.idf[:, k:128:8], False, k == 7, 256) for k in range(2 * a, 2 * a + 2)],
+                       ["idf", "wf%d" % s], ["B%d" % b])
+                tt(et, ps[b][:, 0:128], T.par[:], A.mult, 128, ["par"], ["B%d" % b, "et%d" % s])
+                pe([(ps[b][:, 128:192], et, T.pair[:], True, True, 64)], ["et%d" % s, "pair"], ["B%d" % b])
+                ts(dst[:, 64 * q:64 * q + 64], ps[b][:, 128:192], 1024.0, A.add, 64, [], ["B%d" % b, dk])
+                continue
+            name = "wd%d" % (rot["wd"] % 3); rot["wd"] += 1
+            ts(T[name][:], gath, -1024.0, A.add, 1024, wk + [sk], [name], cost="g")
+            b = rot["bank"] % 2; rot["bank"] += 1
+            pe([(ps[b][:, 0:64], T.dh[:, 128 * k:128 * k + 128], T[name][:, k:1024:16], k == 0, k == 15, 64) for k in range(16)],
+               DH + [name], ["B%d" % b])
+            ts(dst[:, 64 * q:64 * q + 64], ps[b][:, 0:64], 1024.0, A.add, 64, [], ["B%d" % b, dk])
+
+        f0, vfk = 32 * (t % 2), "vpf%d" % (t % 2)
+        if t == 0 or not AHEAD:
+            prepare(t)
+        if t == 0:
+            cp(pb[:], ident.indirect(pl[:, 16:32]), 256, IDK + ["pl0p"], [pbk], cost="g")
+            repeats(pb, pbk, 16, vfk, z[:, 256:272], "z0s")
+        tt(T.dm[:], zo[:, 256:272], z[:, 256:272], A.max, 32, ["zos%d" % t, "z0s" if t == 0 else zk], ["dm"])
+        tt(T.dd[:], T.dm[:], T.dt[:], A.mult, 32, ["dm", "dt"], ["dd"])
+        tt(T.of[:, 0:16], T.vpf[:, f0:f0 + 16], T.dd[:], A.max, 32, [vfk, "dd"], ["of0"])
+        tt(T.of[:, 16:32], T.vpf[:, f0 + 16:f0 + 32], T.dd[:], A.max, 32, [vfk, "dd"], ["of1"])
+        cp(T.ou[:], T.of[:], 32, ["of0", "of1"], ["ou"])
+
+        pe([(ps[4][:, 0:16], T.bw[:, 15 - jl:143 - jl], z[:, jl:256:16], jl == 0, jl == 15, 64) for jl in range(16)], ["bw", zk], ["B4"])
+        cp(T.ui[:], ps[4][:, 0:16], 16, [], ["B4", "ui"])
+        ts(T.ri[:], T.ui[:], 7, A.bitwise_and, 16, ["ui"], ["ri"])
+        ts(T.um[:], T.ui[:], 4095, A.bitwise_and, 16, ["ui"], ["um"])
+        tt(T.sq[:], T.um[:], T.um[:], A.mult, 32, ["um"], ["sq"])
+        act(T.v37[:], T.vpf[:, f0:f0 + 16], F.Identity, 16, [vfk], ["v37"], scale=37.0)
+        ts(T.sh[:], T.sq[:], 5, A.logical_shift_right, 16, ["sq"], ["sh"], 1023, A.bitwise_and)
+        tt(T.nf[:], T.ri[:], T.j8r[:], A.add, 32, ["ri", "j8r0", "j8r1"], ["nf"])
+        tt(T.sm[:], T.sh[:], T.v37[:], A.add, 32, ["sh", "v37"], ["sm"])
+        cp(T.nu[:], T.nf[:], 16, ["nf"], ["nu"])
+        act(T.rb[:], T.t8[:, 0:1024].indirect(T.nu[:]), F.Identity, 256, ["t8", "nu"], ["rb"], cost="g")
+        ts(T.vi[:], T.sm[:], 1023, A.bitwise_and, 16, ["sm"], ["vi"])
+        cp(po[:, 0:16], T.vi[:], 16, ["vi"], ["po%d" % t])
+        if not last:
+            send(T["pl%d" % (t + 1)][:, 16:32], pl[:, 0:16], "rq%d" % (t + 1), 4096, [plk], ["pl%dp" % (t + 1)])
+            send(T["pl%d" % (t + 1)][:, 0:16], po[:, 0:16], "rp%d" % (t + 1), 4096, ["po%d" % t], ["pl%d" % (t + 1)])
+            send(T["pb%d" % (t + 1)][:], vb[:], "rb%d" % (t + 1), 65536, [vbk], ["pb%d" % (t + 1)])
+        else:
+            ts(T.yt[:], vb[:], 1024.0, A.mult, 256, [vbk], ["yt"])
+            tt(T.yv[:], ident.indirect(po[:, 0:16]), T.yt[:], A.add, 256, IDK + ["po%d" % t, "yt"], ["yv"], cost="g")
+            dma("sp", T.yvp[:], T.yv[0:128:16, :], 8192, ["yv"], [])
+
+        def winners(hs):
+            c0, c1, j0, j1 = 8 * hs[0], 8 * hs[-1] + 8, 128 * hs[0], 128 * hs[-1] + 128
+            n, hk = j1 - j0, "".join(str(h) for h in hs)
+            pe([(ps[7][:, 0:c1 - c0], T.idh[:], T.jc[:, c0:c1], True, False, 64)] +
+               [(ps[7][:, 0:c1 - c0], T.bk[:, 15 - jl:143 - jl], T.sl[:, j0 + jl:j1:16], False, jl == 15, 64) for jl in range(16)],
+               ["idh", "jc", "bk"] + ["sl%d" % h for h in hs], ["B7"])
+            KU, XS, NL = ["ku%d" % h for h in hs], ["xs%d" % h for h in hs], ["nl%d" % h for h in hs]
+            cp(T.ku[:, c0:c1], ps[7][:, 0:c1 - c0], 16, [], ["B7"] + KU)
+            act(T.xs[:, j0:j1], T.xg[:, 0:4096].indirect(T.ku[:, c0:c1]), F.Identity, n, KU + ["xg%d%d" % (q, a) for q in range(4) for a in range(2)], XS, cost="g")
+            pe([(ps[7][:, 256:256 + n], T.idb[:], T.xs[:, j0:j1], True, False, n), (ps[7][:, 256:256 + n], T.idn[:], z[:, j0:j1], False, True, n),
+                (ps[7][:, 0:n], T.idq[:], T.xs[:, j0:j1], True, False, n), (ps[7][:, 0:n], T.idq[:], z[:, j0:j1], False, True, n)],
+               XS + [zk, "idb", "idn", "idq"], ["B7"])
+            steps = [lambda: act(zo[:, j0:j1], ps[7][:, 256:256 + n], F.Abs, n, [], ["B7", "zo%d_%s" % (t, hk)]),
+                     lambda: act(T.nl[:, j0:j1], ps[7][:, 0:n], F.Identity, n, [], ["B7"] + NL, bias=127.75)]
+            for s in (steps[::-1] if last else steps):
+                s()
+            for h in hs:
+                tt(T.xw[:, 1024 * h:1024 * h + 1024].indirect(T.nu[:, 8 * h:8 * h + 8]), T.nl[:, 128 * h:128 * h + 128], T.m128[:], A.add,
+                   128, ["nu", "nl%d" % h, "m128"], ["x%d" % h], cost="s")
+
+        for q in range(4):
+            for a in range(2):
+                o, gath = T.xg[:, 1024 * q + 512 * a:1024 * q + 512 * a + 512], T.xw[:, 0:3072].indirect(T.e3[:, 64 * q + 32 * a:64 * q + 32 * a + 32])
+                if 2 * q + a in DVE_X:
+                    cp(o, gath, 512, ["x0", "x1", "xd", "e3%d" % q], ["xg%d%d" % (q, a)], cost="g")
+                else:
+                    act(o, gath, F.Identity, 512, ["x0", "x1", "xd", "e3%d" % q], ["xg%d%d" % (q, a)], cost="g")
+        if AHEAD and not last:
+            prepare(t + 1)
+        for h in range(2):
+            j0, j1 = 128 * h, 128 * h + 128
+            kb = KEY_BANKS[h]
+            pk, KB = ps[kb], "B%d" % kb
+            E3 = ["e3%d" % (2 * h), "e3%d" % (2 * h + 1)]
+            ts(T.ef[:, j0:j1], T.e3[:, j0:j1], -2048.0, A.add, 64, E3, ["ef%d" % h])
+            ts(T.hi[:, j0:j1], T.e3[:, j0:j1], 2048.0, A.is_lt, 64, E3, ["hi%d" % h], 2048.0, A.mult)
+            pe([(ps[5][:, 0:128], T.idh[:], T.ef[:, j0:j1], True, False, 128), (ps[5][:, 0:128], T.idh[:], T.hi[:, j0:j1], False, False, 128)],
+               ["idh", "ef%d" % h, "hi%d" % h], ["B5"])
+            pe([(ps[6][:, 0:128], T.idb[:], T.rb[:, j0:j1], True, False, 128), (ps[6][:, 0:128], T.idb[:], T.j8c[:, j0:j1], False, False, 128),
+                (ps[6][:, 128:256], T.idh[:], pb[:, j0:j1], False, False, 128), (ps[6][:, 256:384], T.idh[:], vb[:, j0:j1], False, False, 128)],
+               ["idb", "idh", "rb", "j8c", pbk, vbk], ["B6"])
+            for kt in range(4):
+                b = (DIFF_LAST if last else DIFF_BANKS)[h][kt]
+                XG = ["xg%d%d" % (q, a) for q in (2 * h, 2 * h + 1) for a in range(2)]
+                mms = []
+                for kk in range(4):
+                    k, o = 4 * kt + kk, ps[b][:, 128 * kk:128 * kk + 128]
+                    mms += [(o, T.idb[:], T.xg[:, 2048 * h + k:2048 * h + 2048:16], True, False, 128), (o, T.idn[:], z[:, j0:j1], False, True, 128)]
+                pe(mms, ["idb", "idn", zk] + XG, ["B%d" % b])
+                a0, ak = 2048 * h + 512 * kt, "ab%d%d" % (h, kt)
+                if kt == 0:
+                    pe([(pk[:, 0:256], T.oneh[:], T.kc[:], True, False, 256)], ["oneh", "kc0", "kc1"], [KB])
+                sel = T.sel[:, 0:16]
+                if (h, kt) in DVE_ABS:
+                    ts(T.ab[:, a0:a0 + 512], ps[b][:], 0.0, A.max, 512, [], ["B%d" % b, ak])
+                    mms = []
+                    for k in range(4 * kt, 4 * kt + 4):
+                        mms += [(pk[:, k:256:16], T.xg[:, 2048 * h + k:2048 * h + 2048:16], T.sel[:, 32:48], False, False, 64),
+                                (pk[:, k:256:16], z[:, j0:j1], sel, False, False, 64)]
+                    pe(mms, ["sel0", "sel1", "sel3", zk] + XG, [KB])
+                    sel = T.sel[:, 16:32]
+                else:
+                    act(T.ab[:, a0:a0 + 512], ps[b][:], F.Abs, 512, [], ["B%d" % b, ak])
+                mms = [(pk[:, 4 * kt + kk:256:16], T.ab[:, a0 + 128 * kk:a0 + 128 * kk + 128], sel, False, kt == 3 and kk == 3, 64) for kk in range(4)]
+                pe(mms, ["sel0", "sel1", "sel2", ak], [KB])
+            pm, ky, sT = T.pm[:, j0:j1], T.ky[:, j0:j1], T.st[:, j0:j1]
+            if h in DVE_KEY:
+                cp(ky, pk[:, 0:128], 128, [], [KB, "ky%d" % h])
+            else:
+                act(ky, pk[:, 0:128], F.Identity, 128, [], [KB, "ky%d" % h])
+            act(T.sg[:, j0:j1], pk[:, 128:256], F.Sign, 150, ["abias"], [KB, "sg%d" % h, "acc%d" % h], bias=T.abias[:, 0:1], accum_out=T.acc[:, h:h + 1])
+            op("dve", lambda pm=pm, ky=ky: V.tensor_tensor_scan(pm, T.rst[:], ky, 0.0, A.add, A.min), ("v", 128), ["rst", "ky%d" % h], ["pm%d" % h])
+            tt(sT, pm.indirect(T.mix[:]), ky, A.is_equal, 128, ["pm%d" % h, "ky%d" % h, "mix"], ["st%d" % h], cost="g")
+            pe([(ps[6][:, 128:256], T.sg[:, j0:j1], T.ip2[:], False, False, 128), (ps[6][:, 256:384], T.sg[:, j0:j1], T.in2[:], False, False, 128)],
+               ["sg%d" % h, "ip2", "in2"], ["B6"])
+            pe([(ps[6][:, 0:128], sT, T.ip2[:], False, False, 128), (ps[6][:, 384:512], sT, T.idb[:], False, True, 128)], ["st%d" % h, "ip2", "idb"], ["B6"])
+            pe([(ps[5][:, 0:128], sT, T.in2[:], False, True, 128)], ["st%d" % h, "in2"], ["B5"])
+            a0 = 384 * h
+            act(T.a2[:, a0:a0 + 128], ps[6][:, 0:128], F.Identity, 128, [], ["B6", "a2%d" % h], bias=-2048.0)
+            act(T.a2[:, a0 + 128:a0 + 384], ps[6][:, 128:384], F.Identity, 256, [], ["B6", "fn%d" % h])
+            act(T.sl[:, j0:j1], ps[6][:, 384:512], F.Identity, 128, [], ["B6", "sl%d" % h])
+            tt(T.ep[:, j0:j1], ps[5][:, 0:128], T.a2[:, a0:a0 + 128], A.max, 128, ["a2%d" % h], ["B5", "ep%d" % h])
+            tt(T.w3[:, 2048:3328].indirect(T.ou[:, 8 * h:8 * h + 8]), T.ep[:, j0:j1], T.a2[:, a0 + 128:a0 + 256], A.max, 128,
+               ["ou", "ep%d" % h, "fn%d" % h], ["vd0", "vd1"], cost="s")
+            tt(T.w2[:, 2048:3328].indirect(T.ou[:, 16 + 8 * h:24 + 8 * h]), T.ep[:, j0:j1], T.a2[:, a0 + 256:a0 + 384], A.max, 128,
+               ["ou", "ep%d" % h, "fn%d" % h], ["pd0", "pd1"], cost="s")
+            if last:
+                if h == 1:
+                    dma("sp", T.yvd[:], T.w3[:, 2048:3072], 524288, ["vd0", "vd1"], [])
+                    dma("sp", T.ypd[:], T.w2[:, 2048:3072], 524288, ["pd0", "pd1"], [])
+                winners([h])
+                pe([(ps[YB][:], T[n][:], T.xw[:, 512 * q:512 * q + 512], q == 0, q == 3, 512)
+                    for q, n in enumerate(("idb", "i64", "i4k", "i18")) if q // 2 == h], ["idb", "i64", "i4k", "i18", "x%d" % h], ["B%d" % YB])
+        if not last:
+            winners([0, 1])
+            send(T["z%d" % (t + 1)][:], zo[:], "rz%d" % (t + 1), 69632, ["zo%d_01" % t, "zos%d" % t], ["z%d" % (t + 1)])
+            dma("sp", T.xw[:, 2048:3072], T.xw[:, 0:1024], 262144, ["x0"], ["xd"])
+            pe([(ps[4][:, 0:1], T.onef[:], T.acc[:, h:h + 1], h == 0, h == 1, 256) for h in range(2)], ["onef", "acc0", "acc1"], ["B4"])
+            ts(T.ai[:, 0:1], ps[4][:, 0:1], 0.5, A.mult, 1, [], ["B4", "ai"], 16384.0, A.add)
+            ts(T.aj[:, 0:1], T.ai[:, 0:1], 255, A.bitwise_and, 1, ["ai"], ["aj"])
+            ts(T.abias[:, 0:1], T.aj[:, 0:1], -1.0, A.mult, 1, ["aj"], ["abias"], 0.5, A.add)
+        else:
+            act(T.yxs[:], ps[YB][:], F.Identity, 512, [], ["B%d" % YB, "yxs"])
+            dma("act", T.yx[:], T.yxs[:], 262144, ["yxs"], [])
+            dma("sp", T.yz[:], zo[:, 0:256], 65536, ["zo%d_0" % t, "zo%d_1" % t], [])
+    return ops
+
+
+def depends(ops):
+    writer, readers, pred = {}, {}, []
+    for i, o in enumerate(ops):
+        d = set()
+        for k in o["r"]:
+            if k in writer:
+                d.add(writer[k])
+        for k in o["w"]:
+            if k in writer:
+                d.add(writer[k])
+            d.update(readers.get(k, ()))
+        d.discard(i)
+        for k in o["r"]:
+            readers.setdefault(k, []).append(i)
+        for k in o["w"]:
+            writer[k] = i
+            readers[k] = []
+        pred.append(sorted(d))
+    return pred
+
+
+def timing(o, m):
+    c, n = o["cost"]
+    if c == "v":
+        x = max(64, n) * m["cy"]
+    elif c == "g":
+        x = 60 + n * m["g"] * m["cy"]
+    elif c == "s":
+        x = 60 + n * m["s"] * m["cy"]
+    elif c == "p":
+        x = n * m["pe"]
+    elif c == "i":
+        x = 150 + 2 * n * m["cy"]
+    elif c == "d":
+        return 60.0, 1800.0
+    else:
+        return 1000.0, 3000.0 + n / 60.0
+    return x, x
+
+
+def replay(ops, pred, order, m, prio=None):
+    n = len(ops)
+    tm = [timing(o, m) for o in ops]
+    succ = [[] for _ in range(n)]
+    left = [len(p) for p in pred]
+    for i, p in enumerate(pred):
+        for j in p:
+            succ[j].append(i)
+    ready, done, start = [0.0] * n, [0.0] * n, [0.0] * n
+    free = {e: 0.0 for e in ENG}
+    pos = {e: 0 for e in ENG}
+    cand = {e: [] for e in ENG}
+    for i in range(n):
+        if not left[i]:
+            cand[ops[i]["eng"]].append(i)
+    wire = 0.0
+    for _ in range(n):
+        best = None
+        for e in ENG:
+            if not cand[e]:
+                continue
+            if prio is None:
+                i = order[e][pos[e]]
+                if left[i]:
+                    continue
+            else:
+                t0 = max(free[e], min(ready[j] for j in cand[e]))
+                i = max((j for j in cand[e] if ready[j] <= t0), key=lambda j: prio[j])
+                soon = [j for j in cand[e] if t0 < ready[j] < t0 + min(0.5 * tm[i][0], 400.0) and prio[j] > prio[i] + 500.0]
+                if soon:
+                    i = max(soon, key=lambda j: prio[j])
+            s = max(free[e], ready[i])
+            if best is None or s < best[0]:
+                best = (s, e, i)
+        s, e, i = best
+        cand[e].remove(i)
+        if prio is None:
+            pos[e] += 1
+        else:
+            order[e].append(i)
+        start[i] = s
+        free[e] = s + tm[i][0]
+        done[i] = s + tm[i][1]
+        if ops[i]["kind"] == "dma":
+            wire = max(wire, done[i]) + ops[i]["cost"][1] / 300.0
+            done[i] = wire
+        for j in succ[i]:
+            same = e == "pe" and ops[j]["eng"] == "pe"
+            ready[j] = max(ready[j], done[i] + (0.0 if same else HOP))
+            left[j] -= 1
+            if not left[j]:
+                cand[ops[j]["eng"]].append(j)
+    return max(done), start, done
+
+
+def arrange(ops, pred):
+    n = len(ops)
+    m = MODELS[0]
+    level = [0.0] * n
+    for i in range(n - 1, -1, -1):
+        level[i] += timing(ops[i], m)[1] + (ops[i]["cost"][1] / 300.0 if ops[i]["kind"] == "dma" else 0.0)
+        for j in pred[i]:
+            level[j] = max(level[j], level[i] + HOP)
+    names, count, like = {}, {}, []
+    for o in ops:
+        key = (o["eng"], o["cost"], o["w"][-1][:2] if o["w"] else "")
+        count[key, o["visit"]] = count.get((key, o["visit"]), 0) + 1
+        like.append(names.setdefault((key, count[key, o["visit"]]), len(names)))
+    kinds, like = len(names), np.array(like)
+    rng = np.random.default_rng(SEED)
+    best = None
+    for k in range(TRIES):
+        prio = np.array(level) if best is None else best[2].copy()
+        if best is not None:
+            size = float(rng.choice([200.0, 1000.0, 3000.0]))
+            if rng.random() < 0.6:
+                a = int(rng.integers(0, kinds))
+                shift = np.zeros(kinds)
+                b = min(kinds, a + int(rng.integers(1, 30)))
+                shift[a:b] = rng.normal(0, size, b - a) * (rng.random(b - a) < 0.4)
+                prio += shift[like]
+            else:
+                a = int(rng.integers(0, n))
+                pick = np.arange(a, min(n, a + int(rng.integers(1, 40))))
+                prio[pick] += rng.normal(0, size, len(pick)) * (rng.random(len(pick)) < 0.4)
+        order = {e: [] for e in ENG}
+        score = replay(ops, pred, order, m, [float(x) for x in prio])[0]
+        if best is not None and score > best[3] + 300.0:
+            continue
+        total = score + sum(replay(ops, pred, order, mm)[0] for mm in MODELS[1:])
+        if best is None or total <= best[0]:
+            best = (total, order, prio, score)
+    return best[1]
+
+
+PLAN = {}
+
+
+def rank_program(g, core, T, topo):
+    if T.rank_of(core) is None:
+        return
+    ops = build_ops(g, T, topo, core)
+    if "order" not in PLAN:
+        PLAN["pred"] = depends(ops)
+        PLAN["order"] = arrange(ops, PLAN["pred"])
+    pred, order = PLAN["pred"], PLAN["order"]
+    queue = dict(pe=g.tensor, dve=g.vector, act=g.scalar, pool=g, sp=g.sync)
+    place = {i: k for e in ENG for k, i in enumerate(order[e])}
+    need = []
+    for i, o in enumerate(ops):
+        lastof, rest = {}, []
+        for j in pred[i]:
+            e = ops[j]["eng"]
+            if ops[j]["kind"] != "c":
+                rest.append(j)
+            elif not (e == "pe" and o["eng"] == "pe") and (e not in lastof or place[j] > place[lastof[e]]):
+                lastof[e] = j
+        need.append(rest + list(lastof.values()))
+    seen = {e: {} for e in ENG}
+    waits, marked = {}, set()
+    for e in ENG:
+        for i in order[e]:
+            waits[i] = []
+            for j in need[i]:
+                key, val = (ops[j]["eng"], place[j]) if ops[j]["kind"] == "c" else (ops[j]["sem"], 0)
+                if seen[e].get(key, -1) < val:
+                    seen[e][key] = val
+                    waits[i].append(j)
+                    marked.add(j)
+    signal, total = {}, {}
+    for e in ENG:
+        for i in order[e]:
+            o = ops[i]
+            if o["kind"] == "dma":
+                signal[i] = (o["sem"], 16)
+            elif o["kind"] == "send":
+                signal[i] = (o["sem"], REMOTE_ENGINES)
+                total["sent"] = total.get("sent", 0) + REMOTE_ENGINES
+            elif i in marked:
+                signal[i] = ("q_" + e, total.get("q_" + e, 0) + 1)
+            else:
+                continue
+            total[signal[i][0]] = signal[i][1]
+    for e in ENG:
+        for i in order[e]:
+            for j in waits[i]:
+                queue[e].wait_ge(T.sem[signal[j][0]], signal[j][1])
+            ins = ops[i]["fn"]()
+            if ops[i]["kind"] == "dma":
+                ins.then_inc(T.sem[signal[i][0]], 16)
+            elif ops[i]["kind"] == "c" and i in marked:
+                ins.then_inc(T.sem[signal[i][0]], 1)
+    for name, val in total.items():
+        g.wait_ge(T.sem[name], val)

@@ -1,51 +1,51 @@
+import math
 import numpy as np
 from concourse.mybir import AluOpType as A, AxisListType, ActivationFunctionType as F
 
 NV = 4
-ACT_Q = {2: (0, 2), 3: (0, 2)}
-ACT_H = {2: (), 3: ()}
-LOOKS = [(2, 0), (2, 1), (2, 2), (2, 3), (3, 0), (3, 1), (3, 2), (3, 3)]
-DVE_X = (3, 6, 7)
-DVE_ABS = ((1, 1),)
-DVE_KEY = ()
-AHEAD = True
-DIFF_BANKS = ((2, 3, 2, 3), (0, 2, 3, 0))
-DIFF_LAST = DIFF_BANKS
-KEY_BANKS = (4, 1)
-YB = 4
+LOOK2 = ("1D", "0A", "2A", "3D")
+LOOK3 = ("1A", "0D", "3A", "2A")
+LINES = ("2D", "3D", "0D", "1A", "6A", "7A", "4A", "5A")
+DIST = (("00A", "10A", "01M", "11M"), ("30A", "20A", "31M", "21M"))
+BANKS = ((0, 1, 0, 0), (1, 0, 1, 0))
+SPLIT_WIN = (False, False, False, True)
+OVER = {}
 BETA = 1.7
-TRIES = 3500
 SEED = 1
 REMOTE_ENGINES = 4
+MODELS = [dict(cy=1.04, g=1.56, s=3.8, pe=0.52, hop=90.0, far=3000.0, dma=1800.0, rate=300.0),
+          dict(cy=1.04, g=1.15, s=5.0, pe=0.58, hop=120.0, far=4000.0, dma=2200.0, rate=220.0),
+          dict(cy=1.04, g=1.95, s=2.5, pe=0.46, hop=70.0, far=2500.0, dma=1500.0, rate=350.0)]
+ROUNDS = ((1, 90000, 300.0, 40.0), (3, 40000, 80.0, 10.0))
 
 f32, bf, f16, i32, u16 = "float32", "bfloat16", "float16", "int32", "uint16"
 SCRATCH = {}
 for _n, _c, _d in [
     ("svd", 1024, i32), ("spd", 1024, i32), ("w2", 3328, f32), ("w3", 3328, f32), ("xw", 3072, bf),
     ("vpi", 32, i32), ("wti", 16, i32), ("z0", 272, bf), ("pb0", 256, f16),
-    ("e1", 256, u16), ("e2", 256, u16), ("e3", 256, u16), ("ef", 256, f16), ("hi", 256, f16),
+    ("e1", 256, u16), ("e2", 256, u16), ("e3", 256, u16), ("ef", 256, f16), ("hi", 256, bf),
     ("wd0", 1024, f16), ("wd1", 1024, f16), ("wd2", 1024, f16), ("wf", 2048, f32),
-    ("xg", 4096, bf), ("ab", 4096, bf), ("pm", 256, f32), ("st", 288, bf), ("sg", 256, bf), ("acc", 8, f32),
-    ("a2", 768, f32), ("ep", 256, f32), ("sl", 256, bf), ("ku", 16, u16), ("xs", 256, bf), ("nl", 256, bf),
-    ("rb", 256, bf), ("mt", 2176, bf), ("fl", 256, bf), ("vpf", 64, f32),
-    ("ui", 16, i32), ("um", 16, i32), ("ri", 16, i32), ("ru", 16, u16), ("nf", 16, f32), ("nu", 16, u16),
-    ("sq", 16, i32), ("sh", 16, i32), ("v37", 16, f32), ("sm", 16, i32), ("vi", 16, i32),
-    ("dm", 16, f32), ("dd", 16, f32), ("of", 32, f32), ("ou", 32, u16), ("ai", 8, i32), ("aj", 8, i32), ("abias", 8, f32),
+    ("xg", 4096, bf), ("ab", 4096, bf), ("ky", 256, f32), ("pm", 256, f32), ("st", 256, bf), ("sg", 256, bf), ("acc", 8, f32),
+    ("a2", 768, f32), ("ep", 256, f32), ("sl", 512, bf), ("ku", 16, u16), ("xs", 256, bf), ("nl", 256, bf),
+    ("rb", 256, bf), ("mt", 2176, bf), ("vpf", 64, f32),
+    ("ui", 16, i32), ("um", 16, i32), ("ri", 16, i32), ("nf", 16, f32), ("nu", 16, u16),
+    ("sq", 16, i32), ("vm", 16, f32), ("sm", 16, i32), ("vi", 16, i32),
+    ("of", 32, f32), ("ou", 32, u16), ("ai", 8, i32), ("abias", 8, f32),
     ("yv", 256, f32), ("yt", 256, f32), ("yxs", 512, f32),
     ("pi", 8, i32), ("pj", 8, i32), ("col", 16, f32), ("row", 256, f32), ("m16", 16, f32), ("idb", 128, bf), ("idn", 128, bf),
     ("idh", 128, f16), ("idq", 128, bf), ("ip2", 128, bf), ("in2", 128, bf), ("i64", 128, bf), ("i4k", 128, bf), ("i18", 128, bf),
-    ("bk", 144, bf), ("ky", 256, f32), ("dh", 2048, f16), ("bn", 144, bf), ("bw", 144, bf), ("blk", 128, f32), ("wb", 128, bf),
+    ("dh", 2048, f16), ("bn", 144, bf), ("bw", 144, bf), ("blk", 128, f32), ("wb", 128, bf),
     ("sel", 48, bf), ("idf", 128, f32), ("et", 256, f16),
-    ("b8", 128, f32), ("par", 128, f32), ("pair", 64, f16), ("n8", 128, f16), ("t8", 1024, bf), ("th2", 256, bf), ("oneh", 128, f16), ("onef", 128, f32), ("kc", 256, f16), ("rst", 128, f32),
-    ("mix", 8, u16), ("jl", 16, f32), ("dt", 16, f32), ("j8r", 16, f32), ("jc", 16, f16), ("j8c", 256, bf),
+    ("b8", 128, f32), ("par", 128, f32), ("pair", 64, f16), ("t8", 1024, bf), ("th2", 256, bf), ("oneh", 128, f16),
+    ("half", 128, f32), ("kc", 256, f16), ("rst", 128, f32),
+    ("mix", 8, u16), ("jl", 16, f32), ("dt", 32, f32), ("j8r", 16, f32), ("jc", 32, f16), ("j8c", 256, bf),
     ("m128", 128, bf), ("pw", 64, f32),
 ]:
     SCRATCH[_n] = ("sbuf", [128, _c], _d)
 for _t in range(NV):
     SCRATCH["zo%d" % _t] = ("sbuf", [128, 272], bf)
-    SCRATCH["po%d" % _t] = ("sbuf", [128, 32], u16)
     SCRATCH["vb%d" % _t] = ("sbuf", [128, 256], f16)
-    SCRATCH["pl%d" % _t] = ("sbuf", [128, 32], u16)
+    SCRATCH["pl%d" % _t] = ("sbuf", [128, 48], u16)
     if _t:
         SCRATCH["z%d" % _t] = ("sbuf", [128, 272], bf)
         SCRATCH["pb%d" % _t] = ("sbuf", [128, 256], f16)
@@ -54,10 +54,7 @@ for _b in range(8):
 
 ENG = ("pe", "dve", "act", "pool", "sp")
 SEMAPHORES = ["q_" + e for e in ENG[:4]] + ["d%d" % i for i in range(24)] + ["sent"] + \
-             ["r%s%d" % (k, t) for k in "pqbz" for t in range(1, NV)]
-
-MODELS = [dict(cy=1.04, g=1.56, s=3.8, pe=0.52), dict(cy=1.04, g=1.1, s=2.0, pe=0.52), dict(cy=1.04, g=2.0, s=5.5, pe=0.52)]
-HOP = 90.0
+             ["r%s%d" % (k, t) for k in "pbz" for t in range(1, NV)]
 
 
 def build_ops(g, T, topo, core):
@@ -67,10 +64,10 @@ def build_ops(g, T, topo, core):
     nxt = T.cores[(T.rank_of(core) + 1) % len(T.cores)]
     rid, pid, _ = topo.addr(nxt)
     mask = sum(1 << e for e in topo.engines(core, nxt)[:REMOTE_ENGINES])
-    ndma = [0, -1]
+    ndma = [0]
 
     def op(eng, fn, cost, r, w, kind="c", sem=None):
-        ops.append(dict(eng=eng, fn=fn, cost=cost, r=list(r), w=list(w), kind=kind, sem=sem, visit=ndma[1]))
+        ops.append(dict(eng=eng, fn=fn, cost=cost, r=list(r), w=list(w), kind=kind, sem=sem))
 
     def ts(out, in0, s1, o0, n, r, w, s2=None, o1=None, cost="v"):
         if o1 is None:
@@ -121,13 +118,13 @@ def build_ops(g, T, topo, core):
         op("pool", lambda: g.remote_dma(dst, src, T.sem[sem], T.sem.sent, pid, rid, mask), ("r", nbytes), r, w, kind="send", sem=sem)
 
     dma("sp", T.vpi[:, 0:16], T.vn[:], 8192, [], ["vpi0"])
-    dma("sp", T.svd[:], T.vdir[:], 524288, [], ["svd"])
-    dma("sp", T.spd[:, 0:512], T.pdir[:, 0:512], 262144, [], ["spd0"])
-    dma("sp", T.spd[:, 512:1024], T.pdir[:, 512:1024], 262144, [], ["spd1"])
     dma("act", T.vpi[:, 16:32], T.pn[:], 8192, [], ["vpi1"])
+    dma("sp", T.svd[:], T.vdir[:], 524288, [], ["svd"])
+    dma("sp", T.spd[:, 0:768], T.pdir[:, 0:768], 393216, [], ["spd0"])
+    dma("sp", T.spd[:, 768:1024], T.pdir[:, 768:1024], 131072, [], ["spd1"])
     dma("act", T.wti[:, 0:1], T.wt[:], 512, [], ["wti0"])
     dma("act", T.wti[:, 8:9], T.th[:], 512, [], ["wti1"])
-    dma("act", T.z0[:, 0:256], T.z[:], 65536, [], ["z0"])
+    dma("sp", T.z0[:, 0:256], T.z[:], 65536, [], ["z0"])
     dma("sp", T.xw[:, 0:2048], T.xl[:], 524288, [], ["x0", "x1"])
     dma("sp", T.xw[:, 2048:3072], T.xl[:, 0:1024], 262144, [], ["xd"])
 
@@ -136,75 +133,100 @@ def build_ops(g, T, topo, core):
     iota(T.row[:], [[1, 256]], 0, 0, 256, ["row"])
     iota(T.w2[:, 0:512], [[1, 512]], 0, 0, 512, ["w2a"])
     iota(T.blk[:], [[16, 8], [0, 16]], 0, 0, 128, ["blk"])
+    iota(T.b8[:], [[0, 8], [1, 2], [0, 8]], 0, 0, 128, ["b8"])
     iota(T.w3[:, 0:1024], [[1, 1024]], 0, 0, 1024, ["w3a"])
     iota(T.w3[:, 1024:2048], [[1, 1024]], 1024, 0, 1024, ["w3b"])
     act(T.w2[:, 512:1024], T.w2[:, 0:512], F.Identity, 512, ["w2a"], ["w2b"], bias=512.0)
     act(T.w2[:, 1024:2048], T.w2[:, 0:1024], F.Identity, 1024, ["w2a", "w2b"], ["w2c"], bias=1024.0)
-    ts(T.pj[:, 0:1], T.pi[:, 0:1], 15, A.bitwise_and, 1, ["pi"], ["pj0"])
-    ts(T.pj[:, 1:2], T.pi[:, 0:1], 112, A.bitwise_and, 1, ["pi"], ["pj1"])
-    cp(T.col[:, 0:2], T.pj[:, 0:2], 2, ["pj0", "pj1"], ["c01"])
-    cp(col(2), T.pi[:, 0:1], 1, ["pi"], ["c2"])
-    ts(T.m16[:], T.row[:, 0:16], col(0), A.is_equal, 16, ["row", "c01"], ["m16"])
-    ts(T.idb[:], T.row[:, 0:128], col(2), A.is_equal, 128, ["row", "c2"], ["idb"])
-    cp(T.idh[:], T.idb[:], 64, ["idb"], ["idh"])
+    for c, bits in enumerate((15, 112, 1, 126, 127)):
+        ts(T.pj[:, c:c + 1], T.pi[:, 0:1], bits, A.bitwise_and, 1, ["pi"], ["pj%d" % c])
+    cp(T.col[:, 0:5], T.pj[:, 0:5], 5, ["pj%d" % c for c in range(5)], ["c0"])
+    ts(T.m16[:], T.row[:, 0:16], col(0), A.is_equal, 16, ["row", "c0"], ["m16"])
+    ts(T.idb[:], T.row[:, 0:128], col(4), A.is_equal, 128, ["row", "c0"], ["idb"])
+    cp(T.pl0[:, 16:48], T.vpi[:], 32, ["vpi0", "vpi1"], ["pl0"])
+    cp(T.e1[:], T.svd[:, 0:1024].indirect(T.pl0[:, 16:32]), 256, ["svd", "pl0"], ["e1"], cost="g")
+    cp(T.w2[:, 2048:2816], T.spd[:, 0:768], 768, ["spd0"], ["pd0"])
+    cp(T.w2[:, 2816:3072], T.spd[:, 768:1024], 256, ["spd1"], ["pd1"])
+    for a in range(2):
+        cp(T.w3[:, 2048 + 512 * a:2560 + 512 * a], T.svd[:, 512 * a:512 * a + 512], 512, ["svd"], ["vd%d" % a])
     for a in range(4):
         many("dve", [(lambda k=k: V.tensor_scalar(T.dh[:, 128 * k:128 * k + 128], T.idb[:], T.m16[:, k:k + 1], None, A.mult))
                      for k in range(4 * a, 4 * a + 4)], 256, ["idb", "m16"], ["dh%d" % a])
     DH = ["dh%d" % a for a in range(4)]
     act(T.idf[:], T.idb[:], F.Identity, 128, ["idb"], ["idf"])
-    if ACT_Q[2] or ACT_Q[3]:
-        ts(T.pj[:, 2:3], T.pi[:, 0:1], 1, A.bitwise_and, 1, ["pi"], ["pj2"])
-        ts(T.pj[:, 3:4], T.pi[:, 0:1], 126, A.bitwise_and, 1, ["pi"], ["pj3"])
-        cp(T.col[:, 5:7], T.pj[:, 2:4], 2, ["pj2", "pj3"], ["c56"])
-        iota(T.b8[:], [[0, 8], [1, 2], [0, 8]], 0, 0, 128, ["b8"])
-        ts(T.par[:], T.b8[:], col(5), A.is_equal, 128, ["b8", "c56"], ["par"])
-        ts(T.pair[:], T.row[:, 0:128:2], col(6), A.is_equal, 64, ["row", "c56"], ["pair"])
-        ts(T.n8[:], T.row[:, 0:128], 0.0, A.mult, 128, ["row"], ["n8"], -8.0, A.add)
-    iota(T.t8[:], [[0, 128], [1, 8]], 0, 0, 1024, ["t8"])
-    for name, val in (("idn", -1.0), ("idq", 0.5), ("ip2", 2048.0), ("in2", -2048.0), ("i64", 64.0), ("i4k", 4096.0), ("i18", 262144.0)):
-        act(T[name][:], T.idb[:], F.Identity, 128, ["idb"], [name], scale=val)
-    ts(col(3), col(1), 15.0, A.add, 1, ["c01"], ["c3"])
-    cp(T.col[:, 7:9], T.wti[:, 0:9:8], 2, ["wti0", "wti1"], ["c7", "c8"])
-    ts(T.bn[:], T.row[:, 0:144], col(3), A.is_equal, 144, ["row", "c3"], ["bn"])
-    act(T.bw[:], T.bn[:], F.Identity, 144, ["bn", "c7"], ["bw"], scale=col(7))
-    act(T.bk[:], T.bn[:], F.Identity, 144, ["bn", "c01"], ["bk"], scale=col(0))
+    ts(T.par[:], T.b8[:], col(2), A.is_equal, 128, ["b8", "c0"], ["par"])
+    ts(T.pair[:], T.row[:, 0:128:2], col(3), A.is_equal, 64, ["row", "c0"], ["pair"])
+    ts(col(5), col(1), 15.0, A.add, 1, ["c0"], ["c5"])
+    ts(T.bn[:], T.row[:, 0:144], col(5), A.is_equal, 144, ["row", "c5"], ["bn"])
     ms(T.pw[:, 0:16], 1.0 / BETA, 16, ["pw0"])
     ms(T.pw[:, 16:32], 0.0, 16, ["pw1"])
     op("dve", lambda: V.tensor_tensor_scan(T.pw[:, 32:48], T.pw[:, 0:16], T.pw[:, 16:32], BETA ** 9, A.mult, A.add), ("v", 16), ["pw0", "pw1"], ["pw2"])
     tt(T.pw[:, 48:64], T.pw[:, 32:48], T.m16[:], A.mult, 32, ["pw2", "m16"], ["pw3"])
-    op("dve", lambda: V.tensor_reduce(col(4), T.pw[:, 48:64], AxisListType.X, A.add), ("v", 16), ["pw3"], ["c4"])
-    ts(T.wb[:], T.blk[:], col(1), A.is_equal, 128, ["blk", "c01", "c4"], ["wb"], col(4), A.mult)
-    ts(T.sel[:, 8:16], T.blk[:, 0:128:16], col(1), A.is_equal, 8, ["blk", "c01"], ["sel1"])
-    act(T.sel[:, 0:8], T.sel[:, 8:16], F.Identity, 8, ["sel1"], ["sel0"], scale=16.0)
-    if DVE_ABS:
-        act(T.sel[:, 16:32], T.sel[:, 0:16], F.Identity, 16, ["sel0", "sel1"], ["sel2"], scale=2.0)
-        act(T.sel[:, 32:48], T.sel[:, 0:16], F.Identity, 16, ["sel0", "sel1"], ["sel3"], scale=-1.0)
+    op("dve", lambda: V.tensor_reduce(col(6), T.pw[:, 48:64], AxisListType.X, A.add), ("v", 16), ["pw3"], ["c6"])
+    ts(T.wb[:], T.blk[:], col(1), A.is_equal, 128, ["blk", "c0", "c6"], ["wb"], col(6), A.mult)
     scale = [2.0 ** (97 - 13 * jh) for jh in range(16)]
     many("act", [(lambda jh=jh: S.activation(T.th2[:, 16 * jh:16 * jh + 16], T.m16[:], F.Identity, scale=-2.56 * scale[jh]))
                  for jh in range(16)], 1024, ["m16"], ["th2"])
-    ms(T.onef[:], 1.0, 128, ["onef"])
-    cp(T.oneh[:], T.onef[:], 128, ["onef"], ["oneh"])
-    ts(T.kc[:, 0:128], T.idb[:], col(0), A.mult, 64, ["idb", "c01"], ["kc0"])
-    ts(T.kc[:, 128:256], T.idb[:], col(8), A.mult, 64, ["idb", "c8"], ["kc1"], -1.0, A.mult)
+    cp(T.idh[:], T.idb[:], 64, ["idb"], ["idh"])
+    cp(T.col[:, 7:9], T.wti[:, 0:9:8], 2, ["wti0", "wti1"], ["c7"])
+    act(T.bw[:], T.bn[:], F.Identity, 144, ["bn", "c7"], ["bw"], scale=col(7))
+    iota(T.t8[:], [[0, 128], [1, 8]], 0, 0, 1024, ["t8"])
+    iota(T.j8c[:], [[8, 256]], 0, 0, 256, ["j8c"])
+    for name, val in (("idn", -1.0), ("idq", 0.5), ("ip2", 2048.0), ("in2", -2048.0), ("i64", 64.0), ("i4k", 4096.0), ("i18", 262144.0)):
+        act(T[name][:], T.idb[:], F.Identity, 128, ["idb"], [name], scale=val)
+    ts(T.sel[:, 8:16], T.blk[:, 0:128:16], col(1), A.is_equal, 8, ["blk", "c0"], ["sel1"])
+    act(T.sel[:, 0:8], T.sel[:, 8:16], F.Identity, 8, ["sel1"], ["sel0"], scale=16.0)
+    act(T.sel[:, 16:32], T.sel[:, 0:16], F.Identity, 16, ["sel0", "sel1"], ["sel2"], scale=2.0)
+    act(T.sel[:, 32:48], T.sel[:, 0:16], F.Identity, 16, ["sel0", "sel1"], ["sel3"], scale=-1.0)
+    SEL = ["sel0", "sel1", "sel2", "sel3"]
+    ms(T.half[:], 0.5, 128, ["half"])
+    ts(T.oneh[:], T.half[:], 2.0, A.mult, 128, ["half"], ["oneh"])
+    act(col(9), col(8), F.Identity, 1, ["c7"], ["c9"], scale=-1.0, bias=0.5)
+    ts(T.kc[:, 0:128], T.idb[:], col(0), A.mult, 64, ["idb", "c0"], ["kc0"])
+    ts(T.kc[:, 128:256], T.idb[:], col(9), A.mult, 64, ["idb", "c9"], ["kc"])
     ms(T.rst[:], 0.0, 128, ["rst"])
     ms(T.rst[:, 0:128:16], 65536.0, 8, ["rst"])
     ts(T.mix[:], T.blk[:, 0:128:16], 15.0, A.add, 8, ["blk"], ["mix"])
-    ts(T.jl[:], T.row[:, 0:16], 16.0, A.mult, 16, ["row", "c01"], ["jl"], col(0), A.add)
-    act(T.dt[:], T.jl[:], F.Identity, 16, ["jl"], ["dt"], bias=1024.0)
-    act(T.j8r[:, 0:8], T.jl[:, 0:8], F.Identity, 8, ["jl"], ["j8r0"], scale=8.0)
-    act(T.j8r[:, 8:16], T.jl[:, 0:8], F.Identity, 8, ["jl"], ["j8r1"], scale=8.0)
-    ts(T.jc[:], T.jl[:], 16.0, A.mult, 16, ["jl"], ["jc"])
-    iota(T.j8c[:], [[8, 256]], 0, 0, 256, ["j8c"])
+    ts(T.jl[:], T.row[:, 0:16], 16.0, A.mult, 16, ["row", "c0"], ["jl"], col(0), A.add)
+    for a in range(2):
+        act(T.dt[:, 16 * a:16 * a + 16], T.jl[:], F.Identity, 16, ["jl"], ["dt%d" % a], bias=1024.0)
+        act(T.j8r[:, 8 * a:8 * a + 8], T.jl[:, 0:8], F.Identity, 8, ["jl"], ["j8r%d" % a], scale=8.0)
+    ts(T.jc[:, 0:16], T.jl[:], 16.0, A.mult, 16, ["jl"], ["jc"])
+    ts(T.jc[:, 16:32], T.jl[:], 0.0, A.mult, 16, ["jl"], ["jc0"])
     ms(T.m128[:], -128.0, 64, ["m128"])
-    ms(T.abias[:, 0:1], 0.5, 1, ["abias"])
+    ms(T.abias[:, 0:1], 0.0, 1, ["abias"])
 
-    cp(T.pl0[:], T.vpi[:], 32, ["vpi0", "vpi1"], ["pl0", "pl0p"])
     W2I, W3I = ["w2a", "w2b", "w2c"], ["w3a", "w3b"]
     ident = T.w2[:, 0:1024]
     IDK = ["w2a", "w2b"]
-    rot = dict(wd=0, wf=0, bank=0, diff=0)
+    XG = ["xg%d" % c for c in range(8)]
+    rot = dict(wd=0, wf=0, bank=0)
 
-    def repeats(src, skey, c0, vfk, dst, dkey):
+    def look(lk, q, eng):
+        win, wk = (T.w2, W2I + ["pd0", "pd1"]) if lk == 2 else (T.w3, W3I + ["vd0", "vd1"])
+        src, sk = (T.e1, "e1") if lk == 2 else (T.e2, "e2%d" % q)
+        dst, dk = (T.e2, "e2%d" % q) if lk == 2 else (T.e3, "e3%d" % q)
+        if eng == "A":
+            s = rot["wf"] % 2; rot["wf"] += 1
+            o0, b, et = 1024 * s, 2 + s, T.et[:, 128 * s:128 * s + 128]
+            act(T.wf[:, o0:o0 + 1024], win[:, 0:3072].indirect(src[:, 64 * q:64 * q + 64]), F.Identity, 1024, wk + [sk], ["wf%d" % s], cost="g", bias=-1024.0)
+            for a in range(4):
+                pe([(ps[b][:, k:128:8], T.wf[:, o0 + k:o0 + 1024:8], T.idf[:, k:128:8], k == 0, k == 7, 256) for k in range(2 * a, 2 * a + 2)],
+                   ["idf", "wf%d" % s], ["B%d" % b])
+            tt(et, ps[b][:, 0:128], T.par[:], A.mult, 128, ["par"], ["B%d" % b, "et%d" % s])
+            pe([(ps[b][:, 128:192], et, T.pair[:], True, True, 64)], ["et%d" % s, "pair"], ["B%d" % b])
+            ts(dst[:, 64 * q:64 * q + 64], ps[b][:, 128:192], 1024.0, A.add, 64, [], ["B%d" % b, dk])
+            return
+        name = "wd%d" % (rot["wd"] % 3); rot["wd"] += 1
+        for a in range(2):
+            ts(T[name][:, 512 * a:512 * a + 512], win[:, 0:3072].indirect(src[:, 64 * q + 32 * a:64 * q + 32 * a + 32]), -1024.0, A.add, 512,
+               wk + [sk], [name + "ab"[a]], cost="g")
+        b = rot["bank"] % 2; rot["bank"] += 1
+        pe([(ps[b][:, 0:64], T.dh[:, 128 * k:128 * k + 128], T[name][:, k:1024:16], k == 0, k == 15, 64) for k in range(16)],
+           DH + [name + "a", name + "b"], ["B%d" % b])
+        ts(dst[:, 64 * q:64 * q + 64], ps[b][:, 0:64], 1024.0, A.add, 64, [], ["B%d" % b, dk])
+
+    def repeats(src, skey, c0, vfk, half):
         off, first = 0, True
         for grp in ((0, 1), (2, 3, 4), (5, 6, 7), (8, 9, 10, 11), (12, 13, 14, 15)):
             fns, mms, n = [], [], 0
@@ -220,338 +242,381 @@ def build_ops(g, T, topo, core):
                 off += wd
             many("dve", fns, n, [skey, vfk], ["mt%d" % grp[0]])
             pe(mms, ["mt%d" % grp[0], "wb", "th2"], ["B7"])
-        act(T.fl[:], ps[7][:, 0:256], F.Sign, 256, [], ["B7", "fl"])
-        pe([(ps[7][:, 256:272], T.bn[:, 15 - jl:143 - jl], T.fl[:, jl:256:16], jl == 0, jl == 15, 64) for jl in range(16)], ["bn", "fl"], ["B7"])
-        act(dst, ps[7][:, 256:272], F.Identity, 16, [], ["B7", dkey], scale=1.0 / 16)
+        act(T.sl[:, 256 * half:256 * half + 256], ps[7][:, 0:256], F.Sign, 256, [], ["B7"] + (["fl"] if half else ["sl0", "sl1"]))
+
+    def to_list(j0, j1, keys, start):
+        pe(start + [(ps[7][:, 0:(j1 - j0) // 16], T.bn[:, 15 - jl:143 - jl], T.sl[:, j0 + jl:j1:16], jl == 0 and not start, jl == 15, 64) for jl in range(16)],
+           ["idh", "jc", "jc0", "bn"] + keys, ["B7"])
+
+    def marks(dst, c0, key):
+        act(dst[:, 256:272], ps[7][:, c0:c0 + 16], F.Identity, 16, [], ["B7", key], scale=128.0, bias=2048.0)
 
     def prepare(t):
         pl, plk, f0, vfk = T["pl%d" % t], "pl%d" % t, 32 * (t % 2), "vpf%d" % (t % 2)
-        cp(T.vpf[:, f0:f0 + 32], pl[:], 32, [plk, plk + "p"], [vfk])
-        cp(T["vb%d" % t][:], ident.indirect(pl[:, 0:16]), 256, IDK + [plk], ["vb%d" % t], cost="g")
-        repeats(T["vb%d" % t], "vb%d" % t, f0, vfk, T["zo%d" % t][:, 256:272], "zos%d" % t)
+        cp(T.vpf[:, f0:f0 + 32], pl[:, 16:48], 32, [plk], [vfk])
+        cp(T["vb%d" % t][:], ident.indirect(pl[:, 16:32]), 256, IDK + [plk], ["vb%d" % t], cost="g")
+        if t < NV - 1:
+            send(T["pb%d" % (t + 1)][:], T["vb%d" % t][:], "rb%d" % (t + 1), 65536, ["vb%d" % t], ["pb%d" % (t + 1)])
+        repeats(T["vb%d" % t], "vb%d" % t, f0, vfk, 1)
+
+    def winners(t, hs):
+        z, zo, zk = T["z%d" % t], T["zo%d" % t], "z%d" % t
+        c0, c1, j0, j1 = 8 * hs[0], 8 * hs[-1] + 8, 128 * hs[0], 128 * hs[-1] + 128
+        n, more = j1 - j0, t < NV - 1 and hs[-1] == 1
+        c2 = 32 if more else c1
+        to_list(j0, 16 * c2, ["sl%d" % h for h in hs] + ["fl"] * more, [(ps[7][:, 0:c2 - c0], T.idh[:], T.jc[:, c0:c2], True, False, 64)])
+        KU, XS, NL, ZO = ([k + str(h) for h in hs] for k in ("ku", "xs", "nl", "zo%d_" % t))
+        cp(T.ku[:, c0:c1], ps[7][:, 0:c1 - c0], 16, [], ["B7"] + KU)
+        if more:
+            marks(T["zo%d" % (t + 1)], c1 - c0, "zos%d" % (t + 1))
+        act(T.xs[:, j0:j1], T.xg[:, 0:4096].indirect(T.ku[:, c0:c1]), F.Identity, n, KU + XG, XS, cost="g")
+        pe([(ps[7][:, 0:n], T.idb[:], T.xs[:, j0:j1], True, False, n), (ps[7][:, 0:n], T.idn[:], z[:, j0:j1], False, True, n)],
+           XS + [zk, "idb", "idn"], ["B7"])
+        act(zo[:, j0:j1], ps[7][:, 0:n], F.Abs, n, [], ["B7"] + ZO)
+        pe([(ps[4][:, 256:256 + n], T.idq[:], T.xs[:, j0:j1], True, False, n), (ps[4][:, 256:256 + n], T.idq[:], z[:, j0:j1], False, True, n)],
+           XS + [zk, "idq"], ["B4"])
+        act(T.nl[:, j0:j1], ps[4][:, 256:256 + n], F.Identity, n, [], ["B4"] + NL, bias=127.75)
+
+    def lines_out(h):
+        tt(T.xw[:, 1024 * h:1024 * h + 1024].indirect(T.nu[:, 8 * h:8 * h + 8]), T.nl[:, 128 * h:128 * h + 128], T.m128[:], A.add,
+           128, ["nu", "nl%d" % h, "m128"], ["x%d" % h], cost="s")
 
     for t in range(NV):
-        z, zo, pl, po, vb, pb = (T["%s%d" % (n, t)] for n in ("z", "zo", "pl", "po", "vb", "pb"))
-        zk, plk, pbk, vbk = "z%d" % t, "pl%d" % t, "pb%d" % t, "vb%d" % t
-        ndma[1] = t
+        z, zo, pl, vb, pb = (T["%s%d" % (n, t)] for n in ("z", "zo", "pl", "vb", "pb"))
+        zk, plk, pbk, vbk, pok = "z%d" % t, "pl%d" % t, "pb%d" % t, "vb%d" % t, "po%d" % t
         last = t == NV - 1
-
-        if t == 0:
-            cp(T.e1[:], T.svd[:, 0:1024].indirect(pl[:, 0:16]), 256, ["svd", plk], ["e1"], cost="g")
-            for a in range(2):
-                cp(T.w2[:, 2048 + 512 * a:2560 + 512 * a], T.spd[:, 512 * a:512 * a + 512], 512, ["spd%d" % a], ["pd%d" % a])
-            for a in range(2):
-                cp(T.w3[:, 2048 + 512 * a:2560 + 512 * a], T.svd[:, 512 * a:512 * a + 512], 512, ["svd"], ["vd%d" % a])
-        else:
-            cp(T.e1[:], T.w3[:, 2048:3072].indirect(pl[:, 0:16]), 256, ["vd0", "vd1", plk], ["e1"], cost="g")
-        for lk, q in LOOKS:
-            win, wk = (T.w2, W2I + ["pd0", "pd1"]) if lk == 2 else (T.w3, W3I + ["vd0", "vd1"])
-            src, sk = (T.e1, "e1") if lk == 2 else (T.e2, "e2%d" % q)
-            dst, dk = (T.e2, "e2%d" % q) if lk == 2 else (T.e3, "e3%d" % q)
-            gath = win[:, 0:3072].indirect(src[:, 64 * q:64 * q + 64])
-            if q // 2 in ACT_H[lk]:
-                act(T.wf[:, 1024 * (q % 2):1024 * (q % 2) + 1024], gath, F.Identity, 1024, wk + [sk], ["wf%d" % (q % 2)], cost="g")
-                if q % 2:
-                    for a in range(8):
-                        pe([(ps[5][:, k:128:16], T.wf[:, k:2048:16], T.idf[:, k:128:16], k == 0, k == 15, 256) for k in range(2 * a, 2 * a + 2)], ["idf", "wf0", "wf1"], ["B5"])
-                    ts(T.et[:, 0:128], ps[5][:, 0:128], -1024.0, A.add, 128, [], ["B5", "et0"])
-                    pe([(ps[5][:, 128:256], T.et[:, 0:128], T.idh[:], True, True, 128)], ["et0", "idh"], ["B5"])
-                    ts(dst[:, 64 * q - 64:64 * q + 64], ps[5][:, 128:256], 1024.0, A.add, 128, [], ["B5", dk, dk[:2] + str(q - 1)])
-                continue
-            if q in ACT_Q[lk]:
-                s = rot["wf"] % 2; rot["wf"] += 1
-                o0, b, et = 1024 * s, 5 + s, T.et[:, 128 * s:128 * s + 128]
-                act(T.wf[:, o0:o0 + 1024], gath, F.Identity, 1024, wk + [sk], ["wf%d" % s], cost="g")
-                pe([(ps[b][:, 0:128], T.oneh[:], T.n8[:], True, False, 128)], ["oneh", "n8"], ["B%d" % b])
-                for a in range(4):
-                    pe([(ps[b][:, k:128:8], T.wf[:, o0 + k:o0 + 1024:8], T.idf[:, k:128:8], False, k == 7, 256) for k in range(2 * a, 2 * a + 2)],
-                       ["idf", "wf%d" % s], ["B%d" % b])
-                tt(et, ps[b][:, 0:128], T.par[:], A.mult, 128, ["par"], ["B%d" % b, "et%d" % s])
-                pe([(ps[b][:, 128:192], et, T.pair[:], True, True, 64)], ["et%d" % s, "pair"], ["B%d" % b])
-                ts(dst[:, 64 * q:64 * q + 64], ps[b][:, 128:192], 1024.0, A.add, 64, [], ["B%d" % b, dk])
-                continue
-            name = "wd%d" % (rot["wd"] % 3); rot["wd"] += 1
-            ts(T[name][:], gath, -1024.0, A.add, 1024, wk + [sk], [name], cost="g")
-            b = rot["bank"] % 2; rot["bank"] += 1
-            pe([(ps[b][:, 0:64], T.dh[:, 128 * k:128 * k + 128], T[name][:, k:1024:16], k == 0, k == 15, 64) for k in range(16)],
-               DH + [name], ["B%d" % b])
-            ts(dst[:, 64 * q:64 * q + 64], ps[b][:, 0:64], 1024.0, A.add, 64, [], ["B%d" % b, dk])
-
+        look2, look3, lines, dist = OVER.get(t, (LOOK2, LOOK3, LINES, DIST))
         f0, vfk = 32 * (t % 2), "vpf%d" % (t % 2)
-        if t == 0 or not AHEAD:
-            prepare(t)
-        if t == 0:
-            cp(pb[:], ident.indirect(pl[:, 16:32]), 256, IDK + ["pl0p"], [pbk], cost="g")
-            repeats(pb, pbk, 16, vfk, z[:, 256:272], "z0s")
-        tt(T.dm[:], zo[:, 256:272], z[:, 256:272], A.max, 32, ["zos%d" % t, "z0s" if t == 0 else zk], ["dm"])
-        tt(T.dd[:], T.dm[:], T.dt[:], A.mult, 32, ["dm", "dt"], ["dd"])
-        tt(T.of[:, 0:16], T.vpf[:, f0:f0 + 16], T.dd[:], A.max, 32, [vfk, "dd"], ["of0"])
-        tt(T.of[:, 16:32], T.vpf[:, f0 + 16:f0 + 32], T.dd[:], A.max, 32, [vfk, "dd"], ["of1"])
-        cp(T.ou[:], T.of[:], 32, ["of0", "of1"], ["ou"])
 
+        if t:
+            cp(T.e1[:], T.w3[:, 2048:3072].indirect(pl[:, 16:32]), 256, ["vd0", "vd1", plk], ["e1"], cost="g")
+        for a, (q, eng) in enumerate(look2):
+            look(2, int(q), eng)
+            if t and a == 0:
+                lines_out(0)
+                dma("sp", T.xw[:, 2048:3072], T.xw[:, 0:1024], 262144, ["x0"], ["xd"])
+        for q, eng in look3:
+            look(3, int(q), eng)
+        if t:
+            lines_out(1)
+            pe([(ps[4][:, 0:1], T.half[:], T.acc[:, h:h + 1], h == 0, h == 1, 256) for h in range(2)], ["half", "acc0", "acc1"], ["B4"])
+            ts(T.ai[:, 0:1], ps[4][:, 0:1], 1.0 / 256, A.mult, 1, [], ["B4", "ai"], -127.5 / 256, A.add)
+            ts(T.abias[:, 0:1], T.ai[:, 0:1], 256.0, A.mult, 1, ["ai"], ["B4", "abias"], ps[4][:, 0:1], A.subtract)
+
+        if t == 0:
+            prepare(0)
+            cp(pb[:], ident.indirect(pl[:, 32:48]), 256, IDK + [plk], [pbk], cost="g")
+            repeats(pb, pbk, 16, vfk, 0)
+            to_list(0, 512, ["sl0", "sl1", "fl"], [])
+            marks(z, 0, "z0s")
+            marks(zo, 16, "zos0")
         pe([(ps[4][:, 0:16], T.bw[:, 15 - jl:143 - jl], z[:, jl:256:16], jl == 0, jl == 15, 64) for jl in range(16)], ["bw", zk], ["B4"])
         cp(T.ui[:], ps[4][:, 0:16], 16, [], ["B4", "ui"])
-        ts(T.ri[:], T.ui[:], 7, A.bitwise_and, 16, ["ui"], ["ri"])
         ts(T.um[:], T.ui[:], 4095, A.bitwise_and, 16, ["ui"], ["um"])
         tt(T.sq[:], T.um[:], T.um[:], A.mult, 32, ["um"], ["sq"])
-        act(T.v37[:], T.vpf[:, f0:f0 + 16], F.Identity, 16, [vfk], ["v37"], scale=37.0)
-        ts(T.sh[:], T.sq[:], 5, A.logical_shift_right, 16, ["sq"], ["sh"], 1023, A.bitwise_and)
+        act(T.vm[:], T.vpf[:, f0:f0 + 16], F.Identity, 16, [vfk], ["vm"], scale=37.0 * 32)
+        tt(T.sm[:], T.sq[:], T.vm[:], A.add, 32, ["sq", "vm"], ["sm"])
+        ts(T.vi[:], T.sm[:], 5, A.logical_shift_right, 16, ["sm"], ["vi"], 1023, A.bitwise_and)
+        cp(pl[:, 0:16], T.vi[:], 16, ["vi"], [pok])
+        if not last:
+            send(T["pl%d" % (t + 1)][:, 16:48], pl[:, 0:32], "rp%d" % (t + 1), 8192, [pok, plk], ["pl%d" % (t + 1)])
+        ts(T.ri[:], T.ui[:], 7, A.bitwise_and, 16, ["ui"], ["ri"])
         tt(T.nf[:], T.ri[:], T.j8r[:], A.add, 32, ["ri", "j8r0", "j8r1"], ["nf"])
-        tt(T.sm[:], T.sh[:], T.v37[:], A.add, 32, ["sh", "v37"], ["sm"])
+
+        for c, eng in lines:
+            c = int(c)
+            o, gath = T.xg[:, 512 * c:512 * c + 512], T.xw[:, 0:3072].indirect(T.e3[:, 32 * c:32 * c + 32])
+            if eng == "D":
+                cp(o, gath, 512, ["x0", "x1", "xd", "e3%d" % (c // 2)], ["xg%d" % c], cost="g")
+            else:
+                act(o, gath, F.Identity, 512, ["x0", "x1", "xd", "e3%d" % (c // 2)], ["xg%d" % c], cost="g")
         cp(T.nu[:], T.nf[:], 16, ["nf"], ["nu"])
         act(T.rb[:], T.t8[:, 0:1024].indirect(T.nu[:]), F.Identity, 256, ["t8", "nu"], ["rb"], cost="g")
-        ts(T.vi[:], T.sm[:], 1023, A.bitwise_and, 16, ["sm"], ["vi"])
-        cp(po[:, 0:16], T.vi[:], 16, ["vi"], ["po%d" % t])
+
+        pe([(ps[7][:, 0:32], T.idf[:], T.vpf[:, f0:f0 + 32], True, False, 256)] +
+           [(ps[7][:, 16 * a:16 * a + 16], T.idb[:], m[:, 256:272], False, a == 1 and m is z, 64) for m in (zo, z) for a in range(2)],
+           ["idf", "idb", vfk, "zos%d" % t, "z0s" if t == 0 else zk], ["B7"])
+        tt(T.of[:], ps[7][:, 0:32], T.dt[:], A.min, 32, ["dt0", "dt1"], ["B7", "of"])
+        cp(T.ou[:], T.of[:], 32, ["of"], ["ou"])
         if not last:
-            send(T["pl%d" % (t + 1)][:, 16:32], pl[:, 0:16], "rq%d" % (t + 1), 4096, [plk], ["pl%dp" % (t + 1)])
-            send(T["pl%d" % (t + 1)][:, 0:16], po[:, 0:16], "rp%d" % (t + 1), 4096, ["po%d" % t], ["pl%d" % (t + 1)])
-            send(T["pb%d" % (t + 1)][:], vb[:], "rb%d" % (t + 1), 65536, [vbk], ["pb%d" % (t + 1)])
+            prepare(t + 1)
         else:
             ts(T.yt[:], vb[:], 1024.0, A.mult, 256, [vbk], ["yt"])
-            tt(T.yv[:], ident.indirect(po[:, 0:16]), T.yt[:], A.add, 256, IDK + ["po%d" % t, "yt"], ["yv"], cost="g")
+            tt(T.yv[:], ident.indirect(pl[:, 0:16]), T.yt[:], A.add, 256, IDK + [pok, "yt"], ["yv"], cost="g")
             dma("sp", T.yvp[:], T.yv[0:128:16, :], 8192, ["yv"], [])
 
-        def winners(hs):
-            c0, c1, j0, j1 = 8 * hs[0], 8 * hs[-1] + 8, 128 * hs[0], 128 * hs[-1] + 128
-            n, hk = j1 - j0, "".join(str(h) for h in hs)
-            pe([(ps[7][:, 0:c1 - c0], T.idh[:], T.jc[:, c0:c1], True, False, 64)] +
-               [(ps[7][:, 0:c1 - c0], T.bk[:, 15 - jl:143 - jl], T.sl[:, j0 + jl:j1:16], False, jl == 15, 64) for jl in range(16)],
-               ["idh", "jc", "bk"] + ["sl%d" % h for h in hs], ["B7"])
-            KU, XS, NL = ["ku%d" % h for h in hs], ["xs%d" % h for h in hs], ["nl%d" % h for h in hs]
-            cp(T.ku[:, c0:c1], ps[7][:, 0:c1 - c0], 16, [], ["B7"] + KU)
-            act(T.xs[:, j0:j1], T.xg[:, 0:4096].indirect(T.ku[:, c0:c1]), F.Identity, n, KU + ["xg%d%d" % (q, a) for q in range(4) for a in range(2)], XS, cost="g")
-            pe([(ps[7][:, 256:256 + n], T.idb[:], T.xs[:, j0:j1], True, False, n), (ps[7][:, 256:256 + n], T.idn[:], z[:, j0:j1], False, True, n),
-                (ps[7][:, 0:n], T.idq[:], T.xs[:, j0:j1], True, False, n), (ps[7][:, 0:n], T.idq[:], z[:, j0:j1], False, True, n)],
-               XS + [zk, "idb", "idn", "idq"], ["B7"])
-            steps = [lambda: act(zo[:, j0:j1], ps[7][:, 256:256 + n], F.Abs, n, [], ["B7", "zo%d_%s" % (t, hk)]),
-                     lambda: act(T.nl[:, j0:j1], ps[7][:, 0:n], F.Identity, n, [], ["B7"] + NL, bias=127.75)]
-            for s in (steps[::-1] if last else steps):
-                s()
-            for h in hs:
-                tt(T.xw[:, 1024 * h:1024 * h + 1024].indirect(T.nu[:, 8 * h:8 * h + 8]), T.nl[:, 128 * h:128 * h + 128], T.m128[:], A.add,
-                   128, ["nu", "nl%d" % h, "m128"], ["x%d" % h], cost="s")
-
-        for q in range(4):
-            for a in range(2):
-                o, gath = T.xg[:, 1024 * q + 512 * a:1024 * q + 512 * a + 512], T.xw[:, 0:3072].indirect(T.e3[:, 64 * q + 32 * a:64 * q + 32 * a + 32])
-                if 2 * q + a in DVE_X:
-                    cp(o, gath, 512, ["x0", "x1", "xd", "e3%d" % q], ["xg%d%d" % (q, a)], cost="g")
-                else:
-                    act(o, gath, F.Identity, 512, ["x0", "x1", "xd", "e3%d" % q], ["xg%d%d" % (q, a)], cost="g")
-        if AHEAD and not last:
-            prepare(t + 1)
         for h in range(2):
             j0, j1 = 128 * h, 128 * h + 128
-            kb = KEY_BANKS[h]
+            kb = (4, 3)[h]
             pk, KB = ps[kb], "B%d" % kb
             E3 = ["e3%d" % (2 * h), "e3%d" % (2 * h + 1)]
-            ts(T.ef[:, j0:j1], T.e3[:, j0:j1], -2048.0, A.add, 64, E3, ["ef%d" % h])
-            ts(T.hi[:, j0:j1], T.e3[:, j0:j1], 2048.0, A.is_lt, 64, E3, ["hi%d" % h], 2048.0, A.mult)
-            pe([(ps[5][:, 0:128], T.idh[:], T.ef[:, j0:j1], True, False, 128), (ps[5][:, 0:128], T.idh[:], T.hi[:, j0:j1], False, False, 128)],
-               ["idh", "ef%d" % h, "hi%d" % h], ["B5"])
-            pe([(ps[6][:, 0:128], T.idb[:], T.rb[:, j0:j1], True, False, 128), (ps[6][:, 0:128], T.idb[:], T.j8c[:, j0:j1], False, False, 128),
-                (ps[6][:, 128:256], T.idh[:], pb[:, j0:j1], False, False, 128), (ps[6][:, 256:384], T.idh[:], vb[:, j0:j1], False, False, 128)],
-               ["idb", "idh", "rb", "j8c", pbk, vbk], ["B6"])
-            for kt in range(4):
-                b = (DIFF_LAST if last else DIFF_BANKS)[h][kt]
-                XG = ["xg%d%d" % (q, a) for q in (2 * h, 2 * h + 1) for a in range(2)]
+            XH = XG[4 * h:4 * h + 4]
+            pe([(pk[:, 0:256], T.oneh[:], T.kc[:], True, False, 256)], ["oneh", "kc0", "kc"], [KB])
+            xk = lambda k: T.xg[:, 2048 * h + k:2048 * h + 2048:16]
+            how = {int(kh): eng for q, kh, eng in dist[h]}
+            for kh in range(2):
+                if how[kh] != "A":
+                    zs = T.sel[:, 0:16] if how[kh] == "D" else T.sel[:, 32:48]
+                    pe([(pk[:, k:256:16], z[:, j0:j1], zs, False, False, 64) for k in range(8 * kh, 8 * kh + 8)], SEL + [zk], [KB])
+                    pe([(pk[:, k:256:16], xk(k), T.sel[:, 32:48], False, False, 64) for k in range(8 * kh, 8 * kh + 8)], SEL + XH, [KB])
+            seen, todo = set(), 4
+            for (q, kh, eng), b in zip(dist[h], BANKS[h]):
+                q, kh = int(q), int(kh)
+                a0 = 2048 * h + 1024 * kh
+                AB = ["ab%d%d" % (2 * h + a, kh) for a in range(2)]
+                abk = lambda k: T.ab[:, a0 + 128 * (k % 8):a0 + 128 * (k % 8) + 128] if eng == "M" else T.ab[:, a0 + k % 8:a0 + 1024:8]
+                sel = T.sel[:, 0:16] if eng == "A" else T.sel[:, 16:32]
+                sums = lambda a, keys: pe([(pk[:, k:256:16], abk(k), sel, False, todo == 1 and k % 4 == 3, 64) for k in range(8 * kh + 4 * a, 8 * kh + 4 * a + 4)],
+                                          SEL + keys, [KB])
+                if eng == "M":
+                    if kh not in seen:
+                        seen.add(kh)
+                        pe([(ps[b][:, 0:128], T.idb[:], z[:, j0:j1], True, True, 128)], ["idb", zk], ["B%d" % b])
+                        for a in range(2):
+                            many("dve", [(lambda k=k, o=abk(k), x=xk(k), b=b: V.tensor_tensor(o, x, ps[b][:, 0:128], A.max)) for k in range(8 * kh + 4 * a, 8 * kh + 4 * a + 4)],
+                                 512, XH, ["B%d" % b, AB[a]])
+                            sums(a, [AB[a]])
+                            todo -= 1
+                    continue
                 mms = []
-                for kk in range(4):
-                    k, o = 4 * kt + kk, ps[b][:, 128 * kk:128 * kk + 128]
-                    mms += [(o, T.idb[:], T.xg[:, 2048 * h + k:2048 * h + 2048:16], True, False, 128), (o, T.idn[:], z[:, j0:j1], False, True, 128)]
-                pe(mms, ["idb", "idn", zk] + XG, ["B%d" % b])
-                a0, ak = 2048 * h + 512 * kt, "ab%d%d" % (h, kt)
-                if kt == 0:
-                    pe([(pk[:, 0:256], T.oneh[:], T.kc[:], True, False, 256)], ["oneh", "kc0", "kc1"], [KB])
-                sel = T.sel[:, 0:16]
-                if (h, kt) in DVE_ABS:
-                    ts(T.ab[:, a0:a0 + 512], ps[b][:], 0.0, A.max, 512, [], ["B%d" % b, ak])
-                    mms = []
-                    for k in range(4 * kt, 4 * kt + 4):
-                        mms += [(pk[:, k:256:16], T.xg[:, 2048 * h + k:2048 * h + 2048:16], T.sel[:, 32:48], False, False, 64),
-                                (pk[:, k:256:16], z[:, j0:j1], sel, False, False, 64)]
-                    pe(mms, ["sel0", "sel1", "sel3", zk] + XG, [KB])
-                    sel = T.sel[:, 16:32]
+                for kk in range(8):
+                    o = ps[b][:, kk:512:8]
+                    mms += [(o, T.idb[:], T.xg[:, 1024 * q + 8 * kh + kk:1024 * q + 1024:16], True, False, 64),
+                            (o, T.idn[:], z[:, 64 * q:64 * q + 64], False, True, 64)]
+                pe(mms, ["idb", "idn", zk, XG[2 * q], XG[2 * q + 1]], ["B%d" % b])
+                o = T.ab[:, a0 + 512 * (q % 2):a0 + 512 * (q % 2) + 512]
+                if eng == "D":
+                    ts(o, ps[b][:], 0.0, A.max, 512, [], ["B%d" % b, "ab%d%d" % (q, kh)])
                 else:
-                    act(T.ab[:, a0:a0 + 512], ps[b][:], F.Abs, 512, [], ["B%d" % b, ak])
-                mms = [(pk[:, 4 * kt + kk:256:16], T.ab[:, a0 + 128 * kk:a0 + 128 * kk + 128], sel, False, kt == 3 and kk == 3, 64) for kk in range(4)]
-                pe(mms, ["sel0", "sel1", "sel2", ak], [KB])
+                    act(o, ps[b][:], F.Abs, 512, [], ["B%d" % b, "ab%d%d" % (q, kh)])
+                if kh in seen:
+                    for a in range(2):
+                        sums(a, AB)
+                        todo -= 1
+                seen.add(kh)
+            ts(T.ef[:, j0:j1], T.e3[:, j0:j1], -2048.0, A.add, 64, E3, ["ef%d" % h])
+            ts(T.hi[:, j0:j1], T.e3[:, j0:j1], 2048.0, A.is_lt, 64, E3, ["hi%d" % h])
+            pe([(ps[5][:, 0:128], T.idh[:], T.ef[:, j0:j1], True, False, 128), (ps[5][:, 0:128], T.ip2[:], T.hi[:, j0:j1], False, False, 128)],
+               ["idh", "ip2", "ef%d" % h, "hi%d" % h], ["B5"])
+            pe([(ps[2][:, 0:128], T.idb[:], T.rb[:, j0:j1], True, False, 128), (ps[2][:, 0:128], T.idb[:], T.j8c[:, j0:j1], False, False, 128)],
+               ["idb", "rb", "j8c"], ["B2"])
+            pe([(ps[6][:, 128:256], T.idh[:], pb[:, j0:j1], True, False, 128), (ps[6][:, 256:384], T.idh[:], vb[:, j0:j1], False, False, 128)],
+               ["idh", pbk, vbk], ["B6"])
             pm, ky, sT = T.pm[:, j0:j1], T.ky[:, j0:j1], T.st[:, j0:j1]
-            if h in DVE_KEY:
-                cp(ky, pk[:, 0:128], 128, [], [KB, "ky%d" % h])
-            else:
-                act(ky, pk[:, 0:128], F.Identity, 128, [], [KB, "ky%d" % h])
+            act(ky, pk[:, 0:128], F.Identity, 128, [], [KB, "ky%d" % h])
             act(T.sg[:, j0:j1], pk[:, 128:256], F.Sign, 150, ["abias"], [KB, "sg%d" % h, "acc%d" % h], bias=T.abias[:, 0:1], accum_out=T.acc[:, h:h + 1])
             op("dve", lambda pm=pm, ky=ky: V.tensor_tensor_scan(pm, T.rst[:], ky, 0.0, A.add, A.min), ("v", 128), ["rst", "ky%d" % h], ["pm%d" % h])
             tt(sT, pm.indirect(T.mix[:]), ky, A.is_equal, 128, ["pm%d" % h, "ky%d" % h, "mix"], ["st%d" % h], cost="g")
-            pe([(ps[6][:, 128:256], T.sg[:, j0:j1], T.ip2[:], False, False, 128), (ps[6][:, 256:384], T.sg[:, j0:j1], T.in2[:], False, False, 128)],
+            pe([(ps[6][:, 128:256], T.sg[:, j0:j1], T.ip2[:], False, False, 128), (ps[6][:, 256:384], T.sg[:, j0:j1], T.in2[:], False, True, 128)],
                ["sg%d" % h, "ip2", "in2"], ["B6"])
-            pe([(ps[6][:, 0:128], sT, T.ip2[:], False, False, 128), (ps[6][:, 384:512], sT, T.idb[:], False, True, 128)], ["st%d" % h, "ip2", "idb"], ["B6"])
-            pe([(ps[5][:, 0:128], sT, T.in2[:], False, True, 128)], ["st%d" % h, "in2"], ["B5"])
             a0 = 384 * h
-            act(T.a2[:, a0:a0 + 128], ps[6][:, 0:128], F.Identity, 128, [], ["B6", "a2%d" % h], bias=-2048.0)
-            act(T.a2[:, a0 + 128:a0 + 384], ps[6][:, 128:384], F.Identity, 256, [], ["B6", "fn%d" % h])
-            act(T.sl[:, j0:j1], ps[6][:, 384:512], F.Identity, 128, [], ["B6", "sl%d" % h])
+            act(T.a2[:, a0 + 128:a0 + 384], ps[6][:, 128:384], F.Identity, 256, [], ["B6", "fv%d" % h, "fp%d" % h])
+            pe([(ps[2][:, 0:128], sT, T.ip2[:], False, True, 128)], ["st%d" % h, "ip2"], ["B2"])
+            pe([(ps[5][:, 0:128], sT, T.in2[:], False, True, 128)], ["st%d" % h, "in2"], ["B5"])
+            pe([(ps[6][:, 0:128], sT, T.idb[:], True, True, 128)], ["st%d" % h, "idb"], ["B6"])
+            act(T.a2[:, a0:a0 + 128], ps[2][:, 0:128], F.Identity, 128, [], ["B2", "a2%d" % h], bias=-2048.0)
+            act(T.sl[:, j0:j1], ps[6][:, 0:128], F.Identity, 128, ["c0"], ["B6", "sl%d" % h], scale=col(0))
             tt(T.ep[:, j0:j1], ps[5][:, 0:128], T.a2[:, a0:a0 + 128], A.max, 128, ["a2%d" % h], ["B5", "ep%d" % h])
             tt(T.w3[:, 2048:3328].indirect(T.ou[:, 8 * h:8 * h + 8]), T.ep[:, j0:j1], T.a2[:, a0 + 128:a0 + 256], A.max, 128,
-               ["ou", "ep%d" % h, "fn%d" % h], ["vd0", "vd1"], cost="s")
+               ["ou", "ep%d" % h, "fv%d" % h], ["vd0", "vd1"], cost="s")
             tt(T.w2[:, 2048:3328].indirect(T.ou[:, 16 + 8 * h:24 + 8 * h]), T.ep[:, j0:j1], T.a2[:, a0 + 256:a0 + 384], A.max, 128,
-               ["ou", "ep%d" % h, "fn%d" % h], ["pd0", "pd1"], cost="s")
-            if last:
-                if h == 1:
-                    dma("sp", T.yvd[:], T.w3[:, 2048:3072], 524288, ["vd0", "vd1"], [])
-                    dma("sp", T.ypd[:], T.w2[:, 2048:3072], 524288, ["pd0", "pd1"], [])
-                winners([h])
-                pe([(ps[YB][:], T[n][:], T.xw[:, 512 * q:512 * q + 512], q == 0, q == 3, 512)
-                    for q, n in enumerate(("idb", "i64", "i4k", "i18")) if q // 2 == h], ["idb", "i64", "i4k", "i18", "x%d" % h], ["B%d" % YB])
+               ["ou", "ep%d" % h, "fp%d" % h], ["pd0", "pd1"], cost="s")
+            if last and h == 1:
+                dma("sp", T.yvd[:], T.w3[:, 2048:3072], 524288, ["vd0", "vd1"], [])
+                dma("sp", T.ypd[:], T.w2[:, 2048:3072], 524288, ["pd0", "pd1"], [])
+            if SPLIT_WIN[t]:
+                winners(t, [h])
+        if not SPLIT_WIN[t]:
+            winners(t, [0, 1])
+        ZO = ["zo%d_0" % t, "zo%d_1" % t]
         if not last:
-            winners([0, 1])
-            send(T["z%d" % (t + 1)][:], zo[:], "rz%d" % (t + 1), 69632, ["zo%d_01" % t, "zos%d" % t], ["z%d" % (t + 1)])
-            dma("sp", T.xw[:, 2048:3072], T.xw[:, 0:1024], 262144, ["x0"], ["xd"])
-            pe([(ps[4][:, 0:1], T.onef[:], T.acc[:, h:h + 1], h == 0, h == 1, 256) for h in range(2)], ["onef", "acc0", "acc1"], ["B4"])
-            ts(T.ai[:, 0:1], ps[4][:, 0:1], 0.5, A.mult, 1, [], ["B4", "ai"], 16384.0, A.add)
-            ts(T.aj[:, 0:1], T.ai[:, 0:1], 255, A.bitwise_and, 1, ["ai"], ["aj"])
-            ts(T.abias[:, 0:1], T.aj[:, 0:1], -1.0, A.mult, 1, ["aj"], ["abias"], 0.5, A.add)
+            send(T["z%d" % (t + 1)][:], zo[:], "rz%d" % (t + 1), 69632, ZO + ["zos%d" % t], ["z%d" % (t + 1)])
         else:
-            act(T.yxs[:], ps[YB][:], F.Identity, 512, [], ["B%d" % YB, "yxs"])
-            dma("act", T.yx[:], T.yxs[:], 262144, ["yxs"], [])
-            dma("sp", T.yz[:], zo[:, 0:256], 65536, ["zo%d_0" % t, "zo%d_1" % t], [])
+            dma("act", T.yz[:], zo[:, 0:256], 65536, ZO, [])
+            for h in range(2):
+                lines_out(h)
+                for b in range(2):
+                    pe([(ps[b][:, 0:256], T[n][:], T.xw[:, 512 * q + 256 * b:512 * q + 256 * b + 256], q == 0, q == 3, 256)
+                        for q, n in enumerate(("idb", "i64", "i4k", "i18")) if q // 2 == h], ["idb", "i64", "i4k", "i18", "x%d" % h], ["B%d" % b])
+            act(T.yxs[:, 0:256], ps[0][:, 0:256], F.Identity, 256, [], ["B0", "yx0"])
+            cp(T.yxs[:, 256:512], ps[1][:, 0:256], 256, [], ["B1", "yx1"])
+            dma("sp", T.yx[:], T.yxs[:], 262144, ["yx0", "yx1"], [])
     return ops
 
 
 def depends(ops):
     writer, readers, pred = {}, {}, []
     for i, o in enumerate(ops):
-        d = set()
-        for k in o["r"]:
+        d = {}
+        for k in o["r"] + o["w"]:
             if k in writer:
-                d.add(writer[k])
+                j = writer[k]
+                d[j] = d.get(j, False) or ops[j]["eng"] != o["eng"] or (o["eng"] != "pe" and k[0] != "B")
         for k in o["w"]:
-            if k in writer:
-                d.add(writer[k])
-            d.update(readers.get(k, ()))
-        d.discard(i)
+            for j in readers.get(k, ()):
+                d[j] = d.get(j, False) or ops[j]["eng"] != "pe" or o["eng"] != "pe"
+        d.pop(i, None)
         for k in o["r"]:
             readers.setdefault(k, []).append(i)
         for k in o["w"]:
             writer[k] = i
             readers[k] = []
-        pred.append(sorted(d))
+        pred.append(d)
     return pred
 
 
-def timing(o, m):
-    c, n = o["cost"]
-    if c == "v":
-        x = max(64, n) * m["cy"]
-    elif c == "g":
-        x = 60 + n * m["g"] * m["cy"]
-    elif c == "s":
-        x = 60 + n * m["s"] * m["cy"]
-    elif c == "p":
-        x = n * m["pe"]
-    elif c == "i":
-        x = 150 + 2 * n * m["cy"]
-    elif c == "d":
-        return 60.0, 1800.0
+def tables(ops, pred, m):
+    eng, hold, lat, wire = [], [], [], []
+    for o in ops:
+        c, n = o["cost"]
+        x = dict(v=max(64, n) * m["cy"], g=60 + n * m["g"] * m["cy"], s=60 + n * m["s"] * m["cy"], p=n * m["pe"],
+                 i=150 + 2 * n * m["cy"], d=60.0, r=1000.0)[c]
+        eng.append(ENG.index(o["eng"]))
+        hold.append(x)
+        lat.append(m["dma"] if c == "d" else m["far"] + n / 60.0 if c == "r" else x)
+        wire.append(n / m["rate"] if c == "d" else 0.0)
+    return eng, hold, lat, wire, [[(j, m["hop"] if sem else 0.0) for j, sem in p.items()] for p in pred]
+
+
+def play(seq, tab, a=0, base=None):
+    eng, hold, lat, wire, inn = tab
+    free, last, w = [0.0] * 5, [-1] * 5, 0.0
+    if base is None:
+        done, why = [0.0] * len(seq), [None] * len(seq)
     else:
-        return 1000.0, 3000.0 + n / 60.0
-    return x, x
+        done, why = base[1][:], base[2][:]
+        for i in seq[:a]:
+            last[eng[i]] = i
+            if wire[i]:
+                w = done[i]
+        for e, i in enumerate(last):
+            if i >= 0:
+                free[e] = why[i][2]
+    for i in seq[a:]:
+        e = eng[i]
+        s, y, q = free[e], last[e], True
+        for j, h in inn[i]:
+            x = done[j] + h
+            if x > s:
+                s, y, q = x, j, False
+        free[e] = x = s + hold[i]
+        last[e] = i
+        d = s + lat[i]
+        if wire[i]:
+            d = w = (w if w > d else d) + wire[i]
+        done[i] = d
+        why[i] = (y, q, x)
+    return max(done), done, why
 
 
-def replay(ops, pred, order, m, prio=None):
+def first_order(ops, pred, tab):
+    eng, hold, lat, wire, inn = tab
     n = len(ops)
-    tm = [timing(o, m) for o in ops]
     succ = [[] for _ in range(n)]
+    for i in range(n):
+        for j, h in inn[i]:
+            succ[j].append((i, h))
     left = [len(p) for p in pred]
+    ready, free, w = [0.0] * n, [0.0] * 5, 0.0
+    cand = [[i for i in range(n) if not left[i] and eng[i] == e] for e in range(5)]
+    seq = []
+    for _ in range(n):
+        best = None
+        for e in range(5):
+            if cand[e]:
+                t0 = max(free[e], min(ready[j] for j in cand[e]))
+                i = min(j for j in cand[e] if ready[j] <= t0 + 120.0)
+                t0 = max(t0, ready[i])
+                if best is None or t0 < best[0]:
+                    best = (t0, e, i)
+        s, e, i = best
+        cand[e].remove(i)
+        seq.append(i)
+        free[e] = s + hold[i]
+        d = s + lat[i]
+        if wire[i]:
+            d = w = max(w, d) + wire[i]
+        for j, h in succ[i]:
+            ready[j] = max(ready[j], d + h)
+            left[j] -= 1
+            if not left[j]:
+                cand[eng[j]].append(j)
+    return seq
+
+
+def improve(seq, pred, tabs, tries, hot, cold, rng):
+    eng, n = tabs[0][0], len(seq)
+    succ = [[] for _ in range(n)]
     for i, p in enumerate(pred):
         for j in p:
             succ[j].append(i)
-    ready, done, start = [0.0] * n, [0.0] * n, [0.0] * n
-    free = {e: 0.0 for e in ENG}
-    pos = {e: 0 for e in ENG}
-    cand = {e: [] for e in ENG}
-    for i in range(n):
-        if not left[i]:
-            cand[ops[i]["eng"]].append(i)
-    wire = 0.0
-    for _ in range(n):
-        best = None
-        for e in ENG:
-            if not cand[e]:
-                continue
-            if prio is None:
-                i = order[e][pos[e]]
-                if left[i]:
-                    continue
-            else:
-                t0 = max(free[e], min(ready[j] for j in cand[e]))
-                i = max((j for j in cand[e] if ready[j] <= t0), key=lambda j: prio[j])
-                soon = [j for j in cand[e] if t0 < ready[j] < t0 + min(0.5 * tm[i][0], 400.0) and prio[j] > prio[i] + 500.0]
-                if soon:
-                    i = max(soon, key=lambda j: prio[j])
-            s = max(free[e], ready[i])
-            if best is None or s < best[0]:
-                best = (s, e, i)
-        s, e, i = best
-        cand[e].remove(i)
-        if prio is None:
-            pos[e] += 1
+    res = [play(seq, t) for t in tabs]
+    cur = sum(r[0] for r in res)
+    best, paths = (cur, seq), None
+    for k, r in enumerate(rng.random((tries, 5)).tolist()):
+        if paths is None:
+            pos = [0] * n
+            for a, i in enumerate(seq):
+                pos[i] = a
+            paths = []
+            for tot, done, why in res:
+                i, p = done.index(tot), []
+                while i >= 0:
+                    y = why[i][0]
+                    if why[i][1] and y >= 0:
+                        p.append((i, y))
+                    i = y
+                paths.append(p)
+        p = paths[int(r[0] * len(paths))]
+        i, y = p[int(r[1] * len(p))]
+        a, b = pos[y], pos[i]
+        more = int(-1.5 * math.log(1.0 - r[2]))
+        if r[3] < 0.5:
+            while more and a > 0:
+                a -= 1
+                more -= eng[seq[a]] == eng[i]
+            want, front, back = {i}, [], []
+            for j in seq[b:a - 1 if a else None:-1]:
+                if j in want:
+                    want.update(pred[j])
+                    front.append(j)
+                else:
+                    back.append(j)
+            new = seq[:a] + front[::-1] + back[::-1] + seq[b + 1:]
         else:
-            order[e].append(i)
-        start[i] = s
-        free[e] = s + tm[i][0]
-        done[i] = s + tm[i][1]
-        if ops[i]["kind"] == "dma":
-            wire = max(wire, done[i]) + ops[i]["cost"][1] / 300.0
-            done[i] = wire
-        for j in succ[i]:
-            same = e == "pe" and ops[j]["eng"] == "pe"
-            ready[j] = max(ready[j], done[i] + (0.0 if same else HOP))
-            left[j] -= 1
-            if not left[j]:
-                cand[ops[j]["eng"]].append(j)
-    return max(done), start, done
+            while more and b < n - 1:
+                b += 1
+                more -= eng[seq[b]] == eng[i]
+            want, front, back = {y}, [], []
+            for j in seq[a:b + 1]:
+                if j in want:
+                    want.update(succ[j])
+                    back.append(j)
+                else:
+                    front.append(j)
+            new = seq[:a] + front + back + seq[b + 1:]
+        limit = cur - len(tabs) * hot * (cold / hot) ** (k / tries) * math.log(1.0 - r[4])
+        out, tot = [], 0.0
+        for t, old in zip(tabs, res):
+            out.append(play(new, t, a, old))
+            tot += out[-1][0]
+            if out[-1][0] > old[0] + 2500.0:
+                break
+        else:
+            if tot <= limit:
+                seq, res, cur, paths = new, out, tot, None
+                if cur < best[0]:
+                    best = (cur, seq)
+    return best[1]
 
 
 def arrange(ops, pred):
-    n = len(ops)
-    m = MODELS[0]
-    level = [0.0] * n
-    for i in range(n - 1, -1, -1):
-        level[i] += timing(ops[i], m)[1] + (ops[i]["cost"][1] / 300.0 if ops[i]["kind"] == "dma" else 0.0)
-        for j in pred[i]:
-            level[j] = max(level[j], level[i] + HOP)
-    names, count, like = {}, {}, []
-    for o in ops:
-        key = (o["eng"], o["cost"], o["w"][-1][:2] if o["w"] else "")
-        count[key, o["visit"]] = count.get((key, o["visit"]), 0) + 1
-        like.append(names.setdefault((key, count[key, o["visit"]]), len(names)))
-    kinds, like = len(names), np.array(like)
+    tabs = [tables(ops, pred, m) for m in MODELS]
     rng = np.random.default_rng(SEED)
-    best = None
-    for k in range(TRIES):
-        prio = np.array(level) if best is None else best[2].copy()
-        if best is not None:
-            size = float(rng.choice([200.0, 1000.0, 3000.0]))
-            if rng.random() < 0.6:
-                a = int(rng.integers(0, kinds))
-                shift = np.zeros(kinds)
-                b = min(kinds, a + int(rng.integers(1, 30)))
-                shift[a:b] = rng.normal(0, size, b - a) * (rng.random(b - a) < 0.4)
-                prio += shift[like]
-            else:
-                a = int(rng.integers(0, n))
-                pick = np.arange(a, min(n, a + int(rng.integers(1, 40))))
-                prio[pick] += rng.normal(0, size, len(pick)) * (rng.random(len(pick)) < 0.4)
-        order = {e: [] for e in ENG}
-        score = replay(ops, pred, order, m, [float(x) for x in prio])[0]
-        if best is not None and score > best[3] + 300.0:
-            continue
-        total = score + sum(replay(ops, pred, order, mm)[0] for mm in MODELS[1:])
-        if best is None or total <= best[0]:
-            best = (total, order, prio, score)
-    return best[1]
+    seq = first_order(ops, pred, tabs[0])
+    for count, tries, hot, cold in ROUNDS:
+        seq = improve(seq, pred, tabs[:count], tries, hot, cold, rng)
+    return seq
 
 
 PLAN = {}
@@ -561,49 +626,44 @@ def rank_program(g, core, T, topo):
     if T.rank_of(core) is None:
         return
     ops = build_ops(g, T, topo, core)
-    if "order" not in PLAN:
+    if "seq" not in PLAN:
         PLAN["pred"] = depends(ops)
-        PLAN["order"] = arrange(ops, PLAN["pred"])
-    pred, order = PLAN["pred"], PLAN["order"]
+        PLAN["seq"] = arrange(ops, PLAN["pred"])
+    pred, seq = PLAN["pred"], PLAN["seq"]
     queue = dict(pe=g.tensor, dve=g.vector, act=g.scalar, pool=g, sp=g.sync)
-    place = {i: k for e in ENG for k, i in enumerate(order[e])}
-    need = []
-    for i, o in enumerate(ops):
-        lastof, rest = {}, []
-        for j in pred[i]:
-            e = ops[j]["eng"]
-            if ops[j]["kind"] != "c":
-                rest.append(j)
-            elif not (e == "pe" and o["eng"] == "pe") and (e not in lastof or place[j] > place[lastof[e]]):
-                lastof[e] = j
-        need.append(rest + list(lastof.values()))
-    seen = {e: {} for e in ENG}
-    waits, marked = {}, set()
-    for e in ENG:
-        for i in order[e]:
-            waits[i] = []
-            for j in need[i]:
-                key, val = (ops[j]["eng"], place[j]) if ops[j]["kind"] == "c" else (ops[j]["sem"], 0)
-                if seen[e].get(key, -1) < val:
-                    seen[e][key] = val
-                    waits[i].append(j)
-                    marked.add(j)
+    place = {i: k for k, i in enumerate(seq)}
+    name = lambda j: ops[j]["eng"] if ops[j]["kind"] == "c" else ops[j]["sem"]
+    known = {e: {} for e in ENG}
+    knew, waits, marked = {}, {}, set()
+    for i in seq:
+        mine = known[ops[i]["eng"]]
+        waits[i] = []
+        for j in sorted((j for j, sem in pred[i].items() if sem), key=lambda j: -place[j]):
+            if mine.get(name(j), -1) < place[j]:
+                waits[i].append(j)
+                marked.add(j)
+                mine[name(j)] = place[j]
+                if ops[j]["kind"] != "send":
+                    for key, val in knew[j].items():
+                        mine[key] = max(mine.get(key, -1), val)
+        knew[i] = dict(mine)
     signal, total = {}, {}
+    for i in seq:
+        o = ops[i]
+        if o["kind"] == "dma":
+            signal[i] = (o["sem"], 16)
+        elif o["kind"] == "send":
+            signal[i] = (o["sem"], REMOTE_ENGINES)
+            total["sent"] = total.get("sent", 0) + REMOTE_ENGINES
+        elif i in marked:
+            signal[i] = ("q_" + o["eng"], total.get("q_" + o["eng"], 0) + 1)
+        else:
+            continue
+        total[signal[i][0]] = signal[i][1]
     for e in ENG:
-        for i in order[e]:
-            o = ops[i]
-            if o["kind"] == "dma":
-                signal[i] = (o["sem"], 16)
-            elif o["kind"] == "send":
-                signal[i] = (o["sem"], REMOTE_ENGINES)
-                total["sent"] = total.get("sent", 0) + REMOTE_ENGINES
-            elif i in marked:
-                signal[i] = ("q_" + e, total.get("q_" + e, 0) + 1)
-            else:
+        for i in seq:
+            if ops[i]["eng"] != e:
                 continue
-            total[signal[i][0]] = signal[i][1]
-    for e in ENG:
-        for i in order[e]:
             for j in waits[i]:
                 queue[e].wait_ge(T.sem[signal[j][0]], signal[j][1])
             ins = ops[i]["fn"]()
@@ -611,5 +671,5 @@ def rank_program(g, core, T, topo):
                 ins.then_inc(T.sem[signal[i][0]], 16)
             elif ops[i]["kind"] == "c" and i in marked:
                 ins.then_inc(T.sem[signal[i][0]], 1)
-    for name, val in total.items():
-        g.wait_ge(T.sem[name], val)
+    for key, val in total.items():
+        g.wait_ge(T.sem[key], val)

@@ -3,20 +3,23 @@ import numpy as np
 from concourse.mybir import AluOpType as A, AxisListType, ActivationFunctionType as F
 
 NV = 4
-LOOK2 = ("1D", "0A", "2A", "3D")
+LOOK2 = ("1W", "0A", "2A", "3D")
 LOOK3 = ("1A", "0D", "3A", "2A")
-LINES = ("2D", "3D", "0D", "1A", "6A", "7A", "4A", "5A")
-DIST = (("00A", "10A", "01M", "11M"), ("30A", "20A", "31M", "21M"))
-BANKS = ((0, 1, 0, 0), (1, 0, 1, 0))
+LINES = ("2D", "3D", "0A", "1A", "6A", "7A", "4A", "5A")
+ORDER = ((1, 0), (3, 2))
+WHOLE = 1
+ZT = "D"
+RB = 2
+FIRST = 1
 SPLIT_WIN = (False, False, False, True)
-OVER = {}
+OVER = {3: (LOOK2, LOOK3, LINES[:7] + ("5D",))}
 BETA = 1.7
 SEED = 1
 REMOTE_ENGINES = 4
-MODELS = [dict(cy=1.04, g=1.56, s=3.8, pe=0.52, hop=90.0, far=3000.0, dma=1800.0, rate=300.0),
-          dict(cy=1.04, g=1.15, s=5.0, pe=0.58, hop=120.0, far=4000.0, dma=2200.0, rate=220.0),
-          dict(cy=1.04, g=1.95, s=2.5, pe=0.46, hop=70.0, far=2500.0, dma=1500.0, rate=350.0)]
-ROUNDS = ((1, 90000, 300.0, 40.0), (3, 40000, 80.0, 10.0))
+MODELS = [dict(cy=0.95, fix=45, g=1.56, s=3.8, pe=0.48, hop=90.0, far=3000.0, dma=1800.0, rate=300.0),
+          dict(cy=0.95, fix=45, g=1.15, s=5.0, pe=0.53, hop=120.0, far=4000.0, dma=2200.0, rate=220.0),
+          dict(cy=0.95, fix=45, g=1.95, s=2.5, pe=0.43, hop=70.0, far=2500.0, dma=1500.0, rate=350.0)]
+ROUNDS = ((1, 100000, 300.0, 40.0), (3, 40000, 80.0, 10.0))
 
 f32, bf, f16, i32, u16 = "float32", "bfloat16", "float16", "int32", "uint16"
 SCRATCH = {}
@@ -24,7 +27,7 @@ for _n, _c, _d in [
     ("svd", 1024, i32), ("spd", 1024, i32), ("w2", 3328, f32), ("w3", 3328, f32), ("xw", 3072, bf),
     ("vpi", 32, i32), ("wti", 16, i32), ("z0", 272, bf), ("pb0", 256, f16),
     ("e1", 256, u16), ("e2", 256, u16), ("e3", 256, u16), ("ef", 256, f16), ("hi", 256, bf),
-    ("wd0", 1024, f16), ("wd1", 1024, f16), ("wd2", 1024, f16), ("wf", 2048, f32),
+    ("wd0", 1024, f16), ("wd1", 1024, f16), ("wd2", 1024, f16), ("wf", 4096, f32),
     ("xg", 4096, bf), ("ab", 4096, bf), ("ky", 256, f32), ("pm", 256, f32), ("st", 256, bf), ("sg", 256, bf), ("acc", 8, f32),
     ("a2", 768, f32), ("ep", 256, f32), ("sl", 512, bf), ("ku", 16, u16), ("xs", 256, bf), ("nl", 256, bf),
     ("rb", 256, bf), ("mt", 2176, bf), ("vpf", 64, f32),
@@ -35,11 +38,11 @@ for _n, _c, _d in [
     ("pi", 8, i32), ("pj", 8, i32), ("col", 16, f32), ("row", 256, f32), ("m16", 16, f32), ("idb", 128, bf), ("idn", 128, bf),
     ("idh", 128, f16), ("idq", 128, bf), ("ip2", 128, bf), ("in2", 128, bf), ("i64", 128, bf), ("i4k", 128, bf), ("i18", 128, bf),
     ("dh", 2048, f16), ("bn", 144, bf), ("bw", 144, bf), ("blk", 128, f32), ("wb", 128, bf),
-    ("sel", 48, bf), ("idf", 128, f32), ("et", 256, f16),
+    ("sel", 32, bf), ("selz", 256, bf), ("zt", 512, bf), ("zz", 512, bf), ("idf", 128, f32), ("et", 256, f16),
     ("b8", 128, f32), ("par", 128, f32), ("pair", 64, f16), ("t8", 1024, bf), ("th2", 256, bf), ("oneh", 128, f16),
     ("half", 128, f32), ("kc", 256, f16), ("rst", 128, f32),
     ("mix", 8, u16), ("jl", 16, f32), ("dt", 32, f32), ("j8r", 16, f32), ("jc", 32, f16), ("j8c", 256, bf),
-    ("m128", 128, bf), ("pw", 64, f32),
+    ("m128", 128, bf), ("i1k", 8, f16), ("big", 128, f32), ("pw", 64, f32),
 ]:
     SCRATCH[_n] = ("sbuf", [128, _c], _d)
 for _t in range(NV):
@@ -49,8 +52,10 @@ for _t in range(NV):
     if _t:
         SCRATCH["z%d" % _t] = ("sbuf", [128, 272], bf)
         SCRATCH["pb%d" % _t] = ("sbuf", [128, 256], f16)
-for _b in range(8):
+for _b in range(2, 8):
     SCRATCH["ps%d" % _b] = ("psum", [128, 512], f32)
+for _b in range(2):
+    SCRATCH["pz%d" % _b] = ("psum", [128, 128, 4, 2], bf)
 
 ENG = ("pe", "dve", "act", "pool", "sp")
 SEMAPHORES = ["q_" + e for e in ENG[:4]] + ["d%d" % i for i in range(24)] + ["sent"] + \
@@ -60,7 +65,7 @@ SEMAPHORES = ["q_" + e for e in ENG[:4]] + ["d%d" % i for i in range(24)] + ["se
 def build_ops(g, T, topo, core):
     ops = []
     V, S, P = g.vector, g.scalar, g.tensor
-    ps = [T["ps%d" % b] for b in range(8)]
+    ps = {b: T["ps%d" % b] for b in range(2, 8)}
     nxt = T.cores[(T.rank_of(core) + 1) % len(T.cores)]
     rid, pid, _ = topo.addr(nxt)
     mask = sum(1 << e for e in topo.engines(core, nxt)[:REMOTE_ENGINES])
@@ -93,7 +98,7 @@ def build_ops(g, T, topo, core):
             for f in fns:
                 last = f()
             return last
-        op(eng, fn, ("v", n), r, w)
+        op(eng, fn, ("m", n), r, w)
 
     def pe(mms, r, w):
         def fn():
@@ -102,6 +107,14 @@ def build_ops(g, T, topo, core):
                 last = P.matmul(o, l, x, s0, s1)
             return last
         op("pe", fn, ("p", sum(m[5] for m in mms)), r, w)
+
+    def turn(pairs, r, bank):
+        def fn():
+            last = None
+            for o, x in pairs:
+                last = P.transpose(o, x, T.idb[:])
+            return last
+        op("pe", fn, ("p", 128 * len(pairs)), r + ["idb"], [bank])
 
     def iota(out, pattern, base, cm, n, w, flag=True):
         if flag:
@@ -144,14 +157,14 @@ def build_ops(g, T, topo, core):
     ts(T.m16[:], T.row[:, 0:16], col(0), A.is_equal, 16, ["row", "c0"], ["m16"])
     ts(T.idb[:], T.row[:, 0:128], col(4), A.is_equal, 128, ["row", "c0"], ["idb"])
     cp(T.pl0[:, 16:48], T.vpi[:], 32, ["vpi0", "vpi1"], ["pl0"])
-    cp(T.e1[:], T.svd[:, 0:1024].indirect(T.pl0[:, 16:32]), 256, ["svd", "pl0"], ["e1"], cost="g")
+    cp(T.e1[:], T.svd[:, 0:1024].indirect(T.pl0[:, 16:32]), 256, ["svd", "pl0"], ["e10", "e1"], cost="g")
     cp(T.w2[:, 2048:2816], T.spd[:, 0:768], 768, ["spd0"], ["pd0"])
     cp(T.w2[:, 2816:3072], T.spd[:, 768:1024], 256, ["spd1"], ["pd1"])
     for a in range(2):
         cp(T.w3[:, 2048 + 512 * a:2560 + 512 * a], T.svd[:, 512 * a:512 * a + 512], 512, ["svd"], ["vd%d" % a])
     for a in range(4):
         many("dve", [(lambda k=k: V.tensor_scalar(T.dh[:, 128 * k:128 * k + 128], T.idb[:], T.m16[:, k:k + 1], None, A.mult))
-                     for k in range(4 * a, 4 * a + 4)], 256, ["idb", "m16"], ["dh%d" % a])
+                     for k in range(4 * a, 4 * a + 4)], [64] * 4, ["idb", "m16"], ["dh%d" % a])
     DH = ["dh%d" % a for a in range(4)]
     act(T.idf[:], T.idb[:], F.Identity, 128, ["idb"], ["idf"])
     ts(T.par[:], T.b8[:], col(2), A.is_equal, 128, ["b8", "c0"], ["par"])
@@ -166,7 +179,7 @@ def build_ops(g, T, topo, core):
     ts(T.wb[:], T.blk[:], col(1), A.is_equal, 128, ["blk", "c0", "c6"], ["wb"], col(6), A.mult)
     scale = [2.0 ** (97 - 13 * jh) for jh in range(16)]
     many("act", [(lambda jh=jh: S.activation(T.th2[:, 16 * jh:16 * jh + 16], T.m16[:], F.Identity, scale=-2.56 * scale[jh]))
-                 for jh in range(16)], 1024, ["m16"], ["th2"])
+                 for jh in range(16)], [16] * 16, ["m16"], ["th2"])
     cp(T.idh[:], T.idb[:], 64, ["idb"], ["idh"])
     cp(T.col[:, 7:9], T.wti[:, 0:9:8], 2, ["wti0", "wti1"], ["c7"])
     act(T.bw[:], T.bn[:], F.Identity, 144, ["bn", "c7"], ["bw"], scale=col(7))
@@ -174,18 +187,18 @@ def build_ops(g, T, topo, core):
     iota(T.j8c[:], [[8, 256]], 0, 0, 256, ["j8c"])
     for name, val in (("idn", -1.0), ("idq", 0.5), ("ip2", 2048.0), ("in2", -2048.0), ("i64", 64.0), ("i4k", 4096.0), ("i18", 262144.0)):
         act(T[name][:], T.idb[:], F.Identity, 128, ["idb"], [name], scale=val)
-    ts(T.sel[:, 8:16], T.blk[:, 0:128:16], col(1), A.is_equal, 8, ["blk", "c0"], ["sel1"])
-    act(T.sel[:, 0:8], T.sel[:, 8:16], F.Identity, 8, ["sel1"], ["sel0"], scale=16.0)
-    act(T.sel[:, 16:32], T.sel[:, 0:16], F.Identity, 16, ["sel0", "sel1"], ["sel2"], scale=2.0)
-    act(T.sel[:, 32:48], T.sel[:, 0:16], F.Identity, 16, ["sel0", "sel1"], ["sel3"], scale=-1.0)
-    SEL = ["sel0", "sel1", "sel2", "sel3"]
-    ms(T.half[:], 0.5, 128, ["half"])
-    ts(T.oneh[:], T.half[:], 2.0, A.mult, 128, ["half"], ["oneh"])
+    ts(T.selz[:, 128:256], T.blk[:], col(1), A.is_equal, 128, ["blk", "c0"], ["selz1"], -1.0, A.mult)
+    act(T.selz[:, 0:128], T.selz[:, 128:256], F.Identity, 128, ["selz1"], ["selz0"], scale=16.0)
+    act(T.sel[:, 0:16], T.selz[:, 0:256:16], F.Identity, 16, ["selz0", "selz1"], ["sel0"], scale=-2.0)
+    act(T.sel[:, 16:32], T.selz[:, 0:256:16], F.Identity, 16, ["selz0", "selz1"], ["sel1"])
+    SEL = ["sel0", "sel1"]
+    iota(T.big[:], [[0, 128]], 65536, 0, 128, ["big"])
+    act(T.half[:], T.big[:], F.Identity, 128, ["big"], ["half"], scale=0.5 / 65536)
+    ts(T.oneh[:], T.idb[:], -1.0, A.is_gt, 64, ["idb"], ["oneh"])
     act(col(9), col(8), F.Identity, 1, ["c7"], ["c9"], scale=-1.0, bias=0.5)
     ts(T.kc[:, 0:128], T.idb[:], col(0), A.mult, 64, ["idb", "c0"], ["kc0"])
     ts(T.kc[:, 128:256], T.idb[:], col(9), A.mult, 64, ["idb", "c9"], ["kc"])
-    ms(T.rst[:], 0.0, 128, ["rst"])
-    ms(T.rst[:, 0:128:16], 65536.0, 8, ["rst"])
+    op("pool", lambda: g.affine_select(T.rst[:], T.big[:], [[0, 8], [1, 16]], A.is_equal, 0.0, 0, 0), ("i", 128), ["big"], ["rst"])
     ts(T.mix[:], T.blk[:, 0:128:16], 15.0, A.add, 8, ["blk"], ["mix"])
     ts(T.jl[:], T.row[:, 0:16], 16.0, A.mult, 16, ["row", "c0"], ["jl"], col(0), A.add)
     for a in range(2):
@@ -193,7 +206,8 @@ def build_ops(g, T, topo, core):
         act(T.j8r[:, 8 * a:8 * a + 8], T.jl[:, 0:8], F.Identity, 8, ["jl"], ["j8r%d" % a], scale=8.0)
     ts(T.jc[:, 0:16], T.jl[:], 16.0, A.mult, 16, ["jl"], ["jc"])
     ts(T.jc[:, 16:32], T.jl[:], 0.0, A.mult, 16, ["jl"], ["jc0"])
-    ms(T.m128[:], -128.0, 64, ["m128"])
+    iota(T.m128[:], [[0, 128]], -128, 0, 128, ["m128"])
+    ts(T.i1k[:], T.idb[:, 0:128:16], 1024.0, A.mult, 8, ["idb"], ["i1k"])
     ms(T.abias[:, 0:1], 0.0, 1, ["abias"])
 
     W2I, W3I = ["w2a", "w2b", "w2c"], ["w3a", "w3b"]
@@ -204,8 +218,21 @@ def build_ops(g, T, topo, core):
 
     def look(lk, q, eng):
         win, wk = (T.w2, W2I + ["pd0", "pd1"]) if lk == 2 else (T.w3, W3I + ["vd0", "vd1"])
-        src, sk = (T.e1, "e1") if lk == 2 else (T.e2, "e2%d" % q)
+        src, sk = (T.e1, "e1" if q else "e10") if lk == 2 else (T.e2, "e2%d" % q)
         dst, dk = (T.e2, "e2%d" % q) if lk == 2 else (T.e3, "e3%d" % q)
+        if eng in "HJ":
+            o0 = 2048 + 1024 * (q % 2)
+            act(T.wf[:, o0:o0 + 1024], win[:, 0:3072].indirect(src[:, 64 * q:64 * q + 64]), F.Identity, 1024, wk + [sk], ["wh%d" % (q % 2)], cost="g", bias=-1024.0)
+            if eng == "J":
+                s = rot["wf"] % 2; rot["wf"] += 1
+                b, et, j0 = 2 + s, T.et[:, 128 * s:128 * s + 128], 128 * (q // 2)
+                for a in range(8):
+                    pe([(ps[b][:, k:128:16], T.wf[:, 2048 + k:4096:16], T.idf[:, k:128:16], k == 0, k == 15, 256) for k in range(2 * a, 2 * a + 2)],
+                       ["idf", "wh0", "wh1"], ["B%d" % b])
+                cp(et, ps[b][:, 0:128], 128, [], ["B%d" % b, "et%d" % s])
+                pe([(ps[b][:, 128:256], et, T.idh[:], True, True, 128)], ["et%d" % s, "idh"], ["B%d" % b])
+                ts(dst[:, j0:j0 + 128], ps[b][:, 128:256], 1024.0, A.add, 128, [], ["B%d" % b, dk[:2] + str(q ^ 1), dk])
+            return
         if eng == "A":
             s = rot["wf"] % 2; rot["wf"] += 1
             o0, b, et = 1024 * s, 2 + s, T.et[:, 128 * s:128 * s + 128]
@@ -218,10 +245,12 @@ def build_ops(g, T, topo, core):
             ts(dst[:, 64 * q:64 * q + 64], ps[b][:, 128:192], 1024.0, A.add, 64, [], ["B%d" % b, dk])
             return
         name = "wd%d" % (rot["wd"] % 3); rot["wd"] += 1
-        for a in range(2):
+        if eng == "W":
+            ts(T[name][:], win[:, 0:3072].indirect(src[:, 64 * q:64 * q + 64]), -1024.0, A.add, 1024, wk + [sk], [name + "a", name + "b"], cost="g")
+        for a in range(2 * (eng == "D")):
             ts(T[name][:, 512 * a:512 * a + 512], win[:, 0:3072].indirect(src[:, 64 * q + 32 * a:64 * q + 32 * a + 32]), -1024.0, A.add, 512,
                wk + [sk], [name + "ab"[a]], cost="g")
-        b = rot["bank"] % 2; rot["bank"] += 1
+        b = (5, 6)[rot["bank"] % 2]; rot["bank"] += 1
         pe([(ps[b][:, 0:64], T.dh[:, 128 * k:128 * k + 128], T[name][:, k:1024:16], k == 0, k == 15, 64) for k in range(16)],
            DH + [name + "a", name + "b"], ["B%d" % b])
         ts(dst[:, 64 * q:64 * q + 64], ps[b][:, 0:64], 1024.0, A.add, 64, [], ["B%d" % b, dk])
@@ -229,7 +258,7 @@ def build_ops(g, T, topo, core):
     def repeats(src, skey, c0, vfk, half):
         off, first = 0, True
         for grp in ((0, 1), (2, 3, 4), (5, 6, 7), (8, 9, 10, 11), (12, 13, 14, 15)):
-            fns, mms, n = [], [], 0
+            fns, mms, n = [], [], []
             if first:
                 mms.append((ps[7][:, 0:256], T.wb[:], T.th2[:], True, False, 256))
                 first = False
@@ -238,7 +267,7 @@ def build_ops(g, T, topo, core):
                 m = T.mt[:, off:off + wd]
                 fns.append(lambda jh=jh, m=m: V.tensor_scalar(m, src[:, 16 * jh:256], T.vpf[:, c0 + jh:c0 + jh + 1], scale[jh], A.is_equal, A.mult))
                 mms.append((ps[7][:, 16 * jh:256], T.wb[:], m, False, jh == 15, max(64, wd)))
-                n += max(64, wd // 2)
+                n.append(wd // 2)
                 off += wd
             many("dve", fns, n, [skey, vfk], ["mt%d" % grp[0]])
             pe(mms, ["mt%d" % grp[0], "wb", "th2"], ["B7"])
@@ -277,6 +306,12 @@ def build_ops(g, T, topo, core):
            XS + [zk, "idq"], ["B4"])
         act(T.nl[:, j0:j1], ps[4][:, 256:256 + n], F.Identity, n, [], ["B4"] + NL, bias=127.75)
 
+    def rests(h):
+        if RB == 2:
+            act(T.rb[:, 128 * h:128 * h + 128], T.t8[:, 0:1024].indirect(T.nu[:, 8 * h:8 * h + 8]), F.Identity, 128, ["t8", "nu"], ["rb%d" % h], cost="g")
+        elif h == RB:
+            act(T.rb[:], T.t8[:, 0:1024].indirect(T.nu[:]), F.Identity, 256, ["t8", "nu"], ["rb0", "rb1"], cost="g")
+
     def lines_out(h):
         tt(T.xw[:, 1024 * h:1024 * h + 1024].indirect(T.nu[:, 8 * h:8 * h + 8]), T.nl[:, 128 * h:128 * h + 128], T.m128[:], A.add,
            128, ["nu", "nl%d" % h, "m128"], ["x%d" % h], cost="s")
@@ -285,11 +320,14 @@ def build_ops(g, T, topo, core):
         z, zo, pl, vb, pb = (T["%s%d" % (n, t)] for n in ("z", "zo", "pl", "vb", "pb"))
         zk, plk, pbk, vbk, pok = "z%d" % t, "pl%d" % t, "pb%d" % t, "vb%d" % t, "po%d" % t
         last = t == NV - 1
-        look2, look3, lines, dist = OVER.get(t, (LOOK2, LOOK3, LINES, DIST))
+        look2, look3, lines = OVER.get(t, (LOOK2, LOOK3, LINES))
         f0, vfk = 32 * (t % 2), "vpf%d" % (t % 2)
 
-        if t:
-            cp(T.e1[:], T.w3[:, 2048:3072].indirect(pl[:, 16:32]), 256, ["vd0", "vd1", plk], ["e1"], cost="g")
+        if t and FIRST:
+            cp(T.e1[:, 0:64], T.w3[:, 2048:3072].indirect(pl[:, 16:20]), 64, ["vd0", "vd1", plk], ["e10"], cost="g")
+            cp(T.e1[:, 64:256], T.w3[:, 2048:3072].indirect(pl[:, 20:32]), 192, ["vd0", "vd1", plk], ["e1"], cost="g")
+        elif t:
+            cp(T.e1[:], T.w3[:, 2048:3072].indirect(pl[:, 16:32]), 256, ["vd0", "vd1", plk], ["e10", "e1"], cost="g")
         for a, (q, eng) in enumerate(look2):
             look(2, int(q), eng)
             if t and a == 0:
@@ -323,27 +361,33 @@ def build_ops(g, T, topo, core):
         ts(T.ri[:], T.ui[:], 7, A.bitwise_and, 16, ["ui"], ["ri"])
         tt(T.nf[:], T.ri[:], T.j8r[:], A.add, 32, ["ri", "j8r0", "j8r1"], ["nf"])
 
-        for c, eng in lines:
+        for a in range(2):
+            op("pool", lambda a=a, z=z: g.affine_select(T.zz[:, a:512:2], z[:, 0:256], [[0, 256]], A.is_ge, 0.0, 0, 0), ("i", 256), [zk], ["zz%d" % a])
+        turn([(T.pz1[:, 16 * q:16 * q + 16, :, :], T.zz[:, 128 * q:128 * q + 128]) for q in range(4)], ["zz0", "zz1"], "Bz1")
+        if ZT == "D":
+            cp(T.zt[:], T.pz1[:, 0:64, :, :], 256, [], ["Bz1", "zt"])
+        else:
+            act(T.zt[:], T.pz1[:, 0:64, :, :], F.Identity, 512, [], ["Bz1", "zt"])
+        for q in ORDER[0] + ORDER[1]:
+            turn([(T["pz%d" % (q // 2)][:, 64 * (q % 2):64 * (q % 2) + 64, r, :], T.zt[:, 128 * q:128 * q + 128]) for r in range(4)], ["zt"], "Bz%d" % (q // 2))
+
+        cp(T.nu[:], T.nf[:], 16, ["nf"], ["nu"])
+        for a, (c, eng) in enumerate(lines):
             c = int(c)
+            if a == 4:
+                rests(0)
             o, gath = T.xg[:, 512 * c:512 * c + 512], T.xw[:, 0:3072].indirect(T.e3[:, 32 * c:32 * c + 32])
             if eng == "D":
                 cp(o, gath, 512, ["x0", "x1", "xd", "e3%d" % (c // 2)], ["xg%d" % c], cost="g")
             else:
                 act(o, gath, F.Identity, 512, ["x0", "x1", "xd", "e3%d" % (c // 2)], ["xg%d" % c], cost="g")
-        cp(T.nu[:], T.nf[:], 16, ["nf"], ["nu"])
-        act(T.rb[:], T.t8[:, 0:1024].indirect(T.nu[:]), F.Identity, 256, ["t8", "nu"], ["rb"], cost="g")
+        rests(1)
 
         pe([(ps[7][:, 0:32], T.idf[:], T.vpf[:, f0:f0 + 32], True, False, 256)] +
            [(ps[7][:, 16 * a:16 * a + 16], T.idb[:], m[:, 256:272], False, a == 1 and m is z, 64) for m in (zo, z) for a in range(2)],
            ["idf", "idb", vfk, "zos%d" % t, "z0s" if t == 0 else zk], ["B7"])
         tt(T.of[:], ps[7][:, 0:32], T.dt[:], A.min, 32, ["dt0", "dt1"], ["B7", "of"])
         cp(T.ou[:], T.of[:], 32, ["of"], ["ou"])
-        if not last:
-            prepare(t + 1)
-        else:
-            ts(T.yt[:], vb[:], 1024.0, A.mult, 256, [vbk], ["yt"])
-            tt(T.yv[:], ident.indirect(pl[:, 0:16]), T.yt[:], A.add, 256, IDK + [pok, "yt"], ["yv"], cost="g")
-            dma("sp", T.yvp[:], T.yv[0:128:16, :], 8192, ["yv"], [])
 
         for h in range(2):
             j0, j1 = 128 * h, 128 * h + 128
@@ -353,53 +397,28 @@ def build_ops(g, T, topo, core):
             XH = XG[4 * h:4 * h + 4]
             pe([(pk[:, 0:256], T.oneh[:], T.kc[:], True, False, 256)], ["oneh", "kc0", "kc"], [KB])
             xk = lambda k: T.xg[:, 2048 * h + k:2048 * h + 2048:16]
-            how = {int(kh): eng for q, kh, eng in dist[h]}
-            for kh in range(2):
-                if how[kh] != "A":
-                    zs = T.sel[:, 0:16] if how[kh] == "D" else T.sel[:, 32:48]
-                    pe([(pk[:, k:256:16], z[:, j0:j1], zs, False, False, 64) for k in range(8 * kh, 8 * kh + 8)], SEL + [zk], [KB])
-                    pe([(pk[:, k:256:16], xk(k), T.sel[:, 32:48], False, False, 64) for k in range(8 * kh, 8 * kh + 8)], SEL + XH, [KB])
-            seen, todo = set(), 4
-            for (q, kh, eng), b in zip(dist[h], BANKS[h]):
-                q, kh = int(q), int(kh)
-                a0 = 2048 * h + 1024 * kh
-                AB = ["ab%d%d" % (2 * h + a, kh) for a in range(2)]
-                abk = lambda k: T.ab[:, a0 + 128 * (k % 8):a0 + 128 * (k % 8) + 128] if eng == "M" else T.ab[:, a0 + k % 8:a0 + 1024:8]
-                sel = T.sel[:, 0:16] if eng == "A" else T.sel[:, 16:32]
-                sums = lambda a, keys: pe([(pk[:, k:256:16], abk(k), sel, False, todo == 1 and k % 4 == 3, 64) for k in range(8 * kh + 4 * a, 8 * kh + 4 * a + 4)],
-                                          SEL + keys, [KB])
-                if eng == "M":
-                    if kh not in seen:
-                        seen.add(kh)
-                        pe([(ps[b][:, 0:128], T.idb[:], z[:, j0:j1], True, True, 128)], ["idb", zk], ["B%d" % b])
-                        for a in range(2):
-                            many("dve", [(lambda k=k, o=abk(k), x=xk(k), b=b: V.tensor_tensor(o, x, ps[b][:, 0:128], A.max)) for k in range(8 * kh + 4 * a, 8 * kh + 4 * a + 4)],
-                                 512, XH, ["B%d" % b, AB[a]])
-                            sums(a, [AB[a]])
-                            todo -= 1
-                    continue
-                mms = []
-                for kk in range(8):
-                    o = ps[b][:, kk:512:8]
-                    mms += [(o, T.idb[:], T.xg[:, 1024 * q + 8 * kh + kk:1024 * q + 1024:16], True, False, 64),
-                            (o, T.idn[:], z[:, 64 * q:64 * q + 64], False, True, 64)]
-                pe(mms, ["idb", "idn", zk, XG[2 * q], XG[2 * q + 1]], ["B%d" % b])
-                o = T.ab[:, a0 + 512 * (q % 2):a0 + 512 * (q % 2) + 512]
-                if eng == "D":
-                    ts(o, ps[b][:], 0.0, A.max, 512, [], ["B%d" % b, "ab%d%d" % (q, kh)])
-                else:
-                    act(o, ps[b][:], F.Abs, 512, [], ["B%d" % b, "ab%d%d" % (q, kh)])
-                if kh in seen:
-                    for a in range(2):
-                        sums(a, AB)
-                        todo -= 1
-                seen.add(kh)
-            ts(T.ef[:, j0:j1], T.e3[:, j0:j1], -2048.0, A.add, 64, E3, ["ef%d" % h])
-            ts(T.hi[:, j0:j1], T.e3[:, j0:j1], 2048.0, A.is_lt, 64, E3, ["hi%d" % h])
+            abk = lambda k: T.ab[:, 2048 * h + 1024 * (k % 2) + k // 2:2048 * h + 1024 * (k % 2) + 1024:8]
+            pe([(pk[:, 0:256], z[:, j0:j1], T.selz[:], False, False, 256)], ["selz0", "selz1", zk], [KB])
+            for q in ORDER[h]:
+                for par in range(2):
+                    a0 = 2048 * h + 1024 * par + 512 * (q % 2)
+                    tt(T.ab[:, a0:a0 + 512], T.xg[:, 1024 * q + par:1024 * q + 1024:2], T["pz%d" % h][:, 64 * (q % 2):64 * (q % 2) + 64, :, :], A.max, 256,
+                       XG[2 * q:2 * q + 2], ["Bz%d" % h, "ab%d%d" % (q, par)])
+            for a in range(2):
+                pe([(pk[:, k:256:16], xk(k), T.sel[:, 16:32], False, False, 64) for k in range(8 * a, 8 * a + 8)], SEL + XH, [KB])
+            for par in range(2):
+                pe([(pk[:, k:256:16], abk(k), T.sel[:, 0:16], False, k == 15, 64) for k in range(par, 16, 2)],
+                   SEL + ["ab%d%d" % (2 * h + a, par) for a in range(2)], [KB])
+            if not WHOLE:
+                ts(T.ef[:, j0:j1], T.e3[:, j0:j1], -2048.0, A.add, 64, E3, ["ef%d" % h])
+                ts(T.hi[:, j0:j1], T.e3[:, j0:j1], 2048.0, A.is_lt, 64, E3, ["hi%d" % h])
+            elif h == 0:
+                ts(T.ef[:], T.e3[:], -2048.0, A.add, 128, ["e30", "e31", "e32", "e33"], ["ef0", "ef1"])
+                ts(T.hi[:], T.e3[:], 2048.0, A.is_lt, 128, ["e30", "e31", "e32", "e33"], ["hi0", "hi1"])
             pe([(ps[5][:, 0:128], T.idh[:], T.ef[:, j0:j1], True, False, 128), (ps[5][:, 0:128], T.ip2[:], T.hi[:, j0:j1], False, False, 128)],
                ["idh", "ip2", "ef%d" % h, "hi%d" % h], ["B5"])
             pe([(ps[2][:, 0:128], T.idb[:], T.rb[:, j0:j1], True, False, 128), (ps[2][:, 0:128], T.idb[:], T.j8c[:, j0:j1], False, False, 128)],
-               ["idb", "rb", "j8c"], ["B2"])
+               ["idb", "rb%d" % h, "j8c"], ["B2"])
             pe([(ps[6][:, 128:256], T.idh[:], pb[:, j0:j1], True, False, 128), (ps[6][:, 256:384], T.idh[:], vb[:, j0:j1], False, False, 128)],
                ["idh", pbk, vbk], ["B6"])
             pm, ky, sT = T.pm[:, j0:j1], T.ky[:, j0:j1], T.st[:, j0:j1]
@@ -426,6 +445,14 @@ def build_ops(g, T, topo, core):
                 dma("sp", T.ypd[:], T.w2[:, 2048:3072], 524288, ["pd0", "pd1"], [])
             if SPLIT_WIN[t]:
                 winners(t, [h])
+            if h == 0 and not last:
+                prepare(t + 1)
+            elif h == 0:
+                act(T.yt[:], ident.indirect(pl[:, 0:16]), F.Identity, 256, IDK + [pok], ["yt"], cost="g")
+                pe([(ps[7][0:8, 0:256], T.i1k[:], vb[:], True, False, 256), (ps[7][0:8, 0:256], T.idf[:, 0:128:16], T.yt[:], False, True, 1024)],
+                   ["i1k", "idf", vbk, "yt"], ["B7"])
+                act(T.yv[0:8, :], ps[7][0:8, 0:256], F.Identity, 256, [], ["B7", "yv"])
+                dma("sp", T.yvp[:], T.yv[0:8, :], 8192, ["yv"], [])
         if not SPLIT_WIN[t]:
             winners(t, [0, 1])
         ZO = ["zo%d_0" % t, "zo%d_1" % t]
@@ -435,11 +462,11 @@ def build_ops(g, T, topo, core):
             dma("act", T.yz[:], zo[:, 0:256], 65536, ZO, [])
             for h in range(2):
                 lines_out(h)
-                for b in range(2):
-                    pe([(ps[b][:, 0:256], T[n][:], T.xw[:, 512 * q + 256 * b:512 * q + 256 * b + 256], q == 0, q == 3, 256)
+                for a, b in enumerate((3, 5)):
+                    pe([(ps[b][:, 0:256], T[n][:], T.xw[:, 512 * q + 256 * a:512 * q + 256 * a + 256], q == 0, q == 3, 256)
                         for q, n in enumerate(("idb", "i64", "i4k", "i18")) if q // 2 == h], ["idb", "i64", "i4k", "i18", "x%d" % h], ["B%d" % b])
-            act(T.yxs[:, 0:256], ps[0][:, 0:256], F.Identity, 256, [], ["B0", "yx0"])
-            cp(T.yxs[:, 256:512], ps[1][:, 0:256], 256, [], ["B1", "yx1"])
+            act(T.yxs[:, 0:256], ps[3][:, 0:256], F.Identity, 256, [], ["B3", "yx0"])
+            cp(T.yxs[:, 256:512], ps[5][:, 0:256], 256, [], ["B5", "yx1"])
             dma("sp", T.yx[:], T.yxs[:], 262144, ["yx0", "yx1"], [])
     return ops
 
@@ -469,12 +496,16 @@ def tables(ops, pred, m):
     eng, hold, lat, wire = [], [], [], []
     for o in ops:
         c, n = o["cost"]
-        x = dict(v=max(64, n) * m["cy"], g=60 + n * m["g"] * m["cy"], s=60 + n * m["s"] * m["cy"], p=n * m["pe"],
-                 i=150 + 2 * n * m["cy"], d=60.0, r=1000.0)[c]
+        fix = m["fix"] * (1.3 if o["eng"] == "act" else 1.0)
+        if c == "m":
+            x = sum(max(64, fix + a) for a in n) * m["cy"]
+        else:
+            x = dict(v=max(64, fix + n) * m["cy"], g=(1.3 * fix + n * m["g"]) * m["cy"], s=(1.3 * fix + n * m["s"]) * m["cy"], p=n * m["pe"],
+                     i=150 + 2 * n * m["cy"], d=60.0, r=1000.0)[c]
         eng.append(ENG.index(o["eng"]))
         hold.append(x)
         lat.append(m["dma"] if c == "d" else m["far"] + n / 60.0 if c == "r" else x)
-        wire.append(n / m["rate"] if c == "d" else 0.0)
+        wire.append(0.0 if c != "d" else n / m["rate"])
     return eng, hold, lat, wire, [[(j, m["hop"] if sem else 0.0) for j, sem in p.items()] for p in pred]
 
 

@@ -1,74 +1,100 @@
 import math
 import numpy as np
+from concourse.bass import DstId, RemoteDMATransfer
 from concourse.mybir import AluOpType as A, AxisListType, ActivationFunctionType as F
 
 NV = 4
-LOOK2 = ("1W", "0A", "2A", "3D")
-LOOK3 = ("1A", "0D", "3A", "2A")
-LINES = ("2D", "3D", "0A", "1A", "6A", "7A", "4A", "5A")
-ORDER = ((1, 0), (3, 2))
-WHOLE = 1
+LOOK2 = ("0W", "1A", "2W", "3A")
+LOOK3 = ("0A", "1W", "2A", "3W")
+LINES = ("02A", "22A", "42A", "62A")
+ORDER = ((0, 1), (2, 3))
 ZT = "D"
-RB = 2
-FIRST = 1
-SPLIT_WIN = (False, False, False, True)
-OVER = {3: (LOOK2, LOOK3, LINES[:7] + ("5D",))}
+HJ = "D"
+FIRST = (1, 0, 0, 0)
+BOTH, EACH = ([0, 1],), ([0], [1])
+TAILS = (BOTH, BOTH, BOTH, EACH)
+WINS = (BOTH, BOTH, BOTH, EACH)
+TOKENS = (0, 1)
+PN = "D"
+TOKEN_ENG = "AA"
+PICK = (2, 3)
+ZSEND = 1
+ZPARTS = (BOTH, BOTH, BOTH, BOTH)
+AFTER = 9
+HSPLIT = 2
+MAXH = ((0, 0),) * 4
+REPICK = (0, 0, 0, 0)
+TWICE = (0, 0, 0)
+NEAR = (6, 6, 6, 7)
+ZR = 8
+JOIN = 0
+VBP = 0
+PIECE = 1100
+A2, SL = "AAAA", "AAAA"
+TPARTS = BOTH
+XSPLIT = 0
+CONST = dict(dh="DDPP", ids="P", w3="P")
+SH = 1536.0
+TK = 3328
+OVER = {0: (("0A", "1W", "2A", "3A"), LOOK3, LINES), 3: (LOOK2, LOOK3, ("02A", "22A", "42A", "61A", "71D"))}
 BETA = 1.7
-SEED = 1
-REMOTE_ENGINES = 4
+SEED = 2
+FREE = 10 ** 9
+REMOTE_ENGINES = 8
 MODELS = [dict(cy=0.95, fix=45, g=1.56, s=3.8, pe=0.48, hop=90.0, far=3000.0, dma=1800.0, rate=300.0),
           dict(cy=0.95, fix=45, g=1.15, s=5.0, pe=0.53, hop=120.0, far=4000.0, dma=2200.0, rate=220.0),
-          dict(cy=0.95, fix=45, g=1.95, s=2.5, pe=0.43, hop=70.0, far=2500.0, dma=1500.0, rate=350.0)]
-ROUNDS = ((1, 100000, 300.0, 40.0), (3, 40000, 80.0, 10.0))
+          dict(cy=0.95, fix=45, g=1.95, s=2.5, pe=0.43, hop=70.0, far=2500.0, dma=1500.0, rate=350.0),
+          dict(cy=0.8, fix=45, g=2.0, s=5.5, pe=0.4, hop=65.0, far=2300.0, dma=1300.0, rate=420.0)]
+ROUNDS = ((1, 60000, 220.0, 30.0), (4, 65000, 60.0, 4.0), (4, 80000, 35.0, 3.0))
 
 f32, bf, f16, i32, u16 = "float32", "bfloat16", "float16", "int32", "uint16"
 SCRATCH = {}
 for _n, _c, _d in [
-    ("svd", 1024, i32), ("spd", 1024, i32), ("w2", 3328, f32), ("w3", 3328, f32), ("xw", 3072, bf),
-    ("vpi", 32, i32), ("wti", 16, i32), ("z0", 272, bf), ("pb0", 256, f16),
-    ("e1", 256, u16), ("e2", 256, u16), ("e3", 256, u16), ("ef", 256, f16), ("hi", 256, bf),
-    ("wd0", 1024, f16), ("wd1", 1024, f16), ("wd2", 1024, f16), ("wf", 4096, f32),
-    ("xg", 4096, bf), ("ab", 4096, bf), ("ky", 256, f32), ("pm", 256, f32), ("st", 256, bf), ("sg", 256, bf), ("acc", 8, f32),
-    ("a2", 768, f32), ("ep", 256, f32), ("sl", 512, bf), ("ku", 16, u16), ("xs", 256, bf), ("nl", 256, bf),
-    ("rb", 256, bf), ("mt", 2176, bf), ("vpf", 64, f32),
-    ("ui", 16, i32), ("um", 16, i32), ("ri", 16, i32), ("nf", 16, f32), ("nu", 16, u16),
-    ("sq", 16, i32), ("vm", 16, f32), ("sm", 16, i32), ("vi", 16, i32),
-    ("of", 32, f32), ("ou", 32, u16), ("ai", 8, i32), ("abias", 8, f32),
-    ("yv", 256, f32), ("yt", 256, f32), ("yxs", 512, f32),
+    ("svd", 1024, i32), ("spd", 1024, i32), ("w2", 3584, f32), ("w3", 3584, f32), ("xw", 3072, bf),
+    ("vpi", 32, i32), ("wti", 16, i32), ("z0", 256, bf), ("bw2", 144, bf),
+    ("e1", 256, u16), ("e2", 256, u16), ("e3", 256, u16), ("hi", 256, bf),
+    ("wd0", 1024, f16), ("wd1", 1024, f16), ("wd2", 1024, f16), ("wk0", 1024, f16), ("wk1", 1024, f16), ("wk2", 1024, f16), ("wk3", 1024, f16), ("wf", 6144, f32),
+    ("xg", 4096, bf), ("ab", 4096, bf), ("pm", 256, f32), ("pn8", 16, f32), ("st", 272, bf), ("sg", 256, bf), ("acc", 8, f32),
+    ("a2", 768, f32), ("sl", 512, bf), ("ku", 16, u16), ("xs", 256, bf), ("nl", 256, bf),
+    ("mt", 2176, bf), ("vpf", 64, f32),
+    ("ui", 24, i32), ("um", 24, i32), ("ri", 32, i32), ("i37", 128, bf),
+    ("sq", 16, i32), ("sm", 16, i32),
+    ("of", 32, f32), ("ou", 64, u16), ("abias", 8, f32),
+    ("yv", 256, f32), ("yxs", 512, f32),
     ("pi", 8, i32), ("pj", 8, i32), ("col", 16, f32), ("row", 256, f32), ("m16", 16, f32), ("idb", 128, bf), ("idn", 128, bf),
-    ("idh", 128, f16), ("idq", 128, bf), ("ip2", 128, bf), ("in2", 128, bf), ("i64", 128, bf), ("i4k", 128, bf), ("i18", 128, bf),
-    ("dh", 2048, f16), ("bn", 144, bf), ("bw", 144, bf), ("blk", 128, f32), ("wb", 128, bf),
-    ("sel", 32, bf), ("selz", 256, bf), ("zt", 512, bf), ("zz", 512, bf), ("idf", 128, f32), ("et", 256, f16),
-    ("b8", 128, f32), ("par", 128, f32), ("pair", 64, f16), ("t8", 1024, bf), ("th2", 256, bf), ("oneh", 128, f16),
-    ("half", 128, f32), ("kc", 256, f16), ("rst", 128, f32),
-    ("mix", 8, u16), ("jl", 16, f32), ("dt", 32, f32), ("j8r", 16, f32), ("jc", 32, f16), ("j8c", 256, bf),
-    ("m128", 128, bf), ("i1k", 8, f16), ("big", 128, f32), ("pw", 64, f32),
+    ("idq", 128, bf), ("ip2", 128, bf), ("in2", 128, bf), ("i64", 128, bf), ("i4k", 128, bf), ("i18", 128, bf),
+    ("dh", 2048, bf), ("lb", 2048, bf), ("zr", 512, bf), ("bn", 144, bf), ("bw", 144, bf), ("blk", 128, f32), ("wb", 128, bf),
+    ("sel", 80, bf), ("selz", 256, bf), ("zt", 512, bf), ("zz", 512, bf), ("idf", 128, f32), ("et", 768, f16),
+    ("b8", 128, f32), ("par", 128, f32), ("pair", 64, f16), ("th2", 256, bf), ("oneh", 128, bf),
+    ("half", 128, f32), ("kc", 256, f16), ("rst", 256, f32),
+    ("mix", 16, u16), ("jl", 16, f32), ("dt", 32, f32), ("j8r", 32, f32), ("jc", 32, f16),
+    ("m128", 256, bf), ("i1k", 8, bf), ("big", 256, f32), ("pw", 64, f32),
 ]:
     SCRATCH[_n] = ("sbuf", [128, _c], _d)
 for _t in range(NV):
-    SCRATCH["zo%d" % _t] = ("sbuf", [128, 272], bf)
-    SCRATCH["vb%d" % _t] = ("sbuf", [128, 256], f16)
-    SCRATCH["pl%d" % _t] = ("sbuf", [128, 48], u16)
+    SCRATCH["zo%d" % _t] = ("sbuf", [128, 256], bf)
+    SCRATCH["vb%d" % _t] = ("sbuf", [128, 288], f16)
+    SCRATCH["pb%d" % _t] = ("sbuf", [128, 288], f16)
+    SCRATCH["pl%d" % _t] = ("sbuf", [128, 64], u16)
+    SCRATCH["ph%d" % _t] = ("sbuf", [128, 32], f16)
     if _t:
-        SCRATCH["z%d" % _t] = ("sbuf", [128, 272], bf)
-        SCRATCH["pb%d" % _t] = ("sbuf", [128, 256], f16)
-for _b in range(2, 8):
+        SCRATCH["z%d" % _t] = ("sbuf", [128, 256], bf)
+        SCRATCH["so%d" % _t] = ("sbuf", [128, 32], u16)
+        SCRATCH["sh%d" % _t] = ("sbuf", [128, 32], f16)
+for _b in range(ZR // 4, 8):
     SCRATCH["ps%d" % _b] = ("psum", [128, 512], f32)
-for _b in range(2):
-    SCRATCH["pz%d" % _b] = ("psum", [128, 128, 4, 2], bf)
+for _b in range(ZR // 4):
+    SCRATCH["pz%d" % _b] = ("psum", [128, 1024 // ZR, ZR // 2, 2], bf)
 
 ENG = ("pe", "dve", "act", "pool", "sp")
-SEMAPHORES = ["q_" + e for e in ENG[:4]] + ["d%d" % i for i in range(24)] + ["sent"] + \
-             ["r%s%d" % (k, t) for k in "pbz" for t in range(1, NV)]
+SEMAPHORES = ["q_" + e for e in ENG[:4]] + ["d%d" % i for i in range(24)] + ["sent", "rw"] + \
+             ["r%s%d" % (k, t) for k in "apbyz" for t in range(1, NV)]
 
 
 def build_ops(g, T, topo, core):
     ops = []
     V, S, P = g.vector, g.scalar, g.tensor
-    ps = {b: T["ps%d" % b] for b in range(2, 8)}
-    nxt = T.cores[(T.rank_of(core) + 1) % len(T.cores)]
-    rid, pid, _ = topo.addr(nxt)
-    mask = sum(1 << e for e in topo.engines(core, nxt)[:REMOTE_ENGINES])
+    ps = {b: T["ps%d" % b] for b in range(ZR // 4, 8)}
     ndma = [0]
 
     def op(eng, fn, cost, r, w, kind="c", sem=None):
@@ -101,6 +127,11 @@ def build_ops(g, T, topo, core):
         op(eng, fn, ("m", n), r, w)
 
     def pe(mms, r, w):
+        if len(mms) > 1 and sum(m[5] for m in mms) > PIECE:
+            pe(mms[:len(mms) // 2], r, w)
+            pe(mms[len(mms) // 2:], r, w)
+            return
+
         def fn():
             last = None
             for o, l, x, s0, s1, c in mms:
@@ -122,13 +153,27 @@ def build_ops(g, T, topo, core):
         else:
             op("pool", lambda: g.iota(out, pattern, base, cm), ("i", n), [], w)
 
+    def mark(out, pattern, base, val, n, w):
+        op("pool", lambda: g.affine_select(out, T.zr[:, 0:n], pattern, A.not_equal, val, base, 1), ("i", n), ["zr"], w)
+
     def dma(eng, out, in_, nbytes, r, w):
         q = g.sync if eng == "sp" else g.scalar
         op(eng, lambda: q.dma_start(out, in_), ("d", nbytes), r, w, kind="dma", sem="d%d" % ndma[0])
         ndma[0] += 1
 
-    def send(dst, src, sem, nbytes, r, w):
+    def send(dst, src, sem, nbytes, r, w, ahead=1):
+        to = T.cores[(T.rank_of(core) + ahead) % len(T.cores)]
+        rid, pid, _ = topo.addr(to)
+        mask = sum(1 << e for e in topo.engines(core, to)[:REMOTE_ENGINES])
         op("pool", lambda: g.remote_dma(dst, src, T.sem[sem], T.sem.sent, pid, rid, mask), ("r", nbytes), r, w, kind="send", sem=sem)
+
+    def send2(pairs, sem, nbytes, r, w, ahead):
+        to = T.cores[(T.rank_of(core) + ahead) % len(T.cores)]
+        rid, pid, _ = topo.addr(to)
+        some = topo.engines(core, to)[:REMOTE_ENGINES]
+        moves = [RemoteDMATransfer(dst_ids=[DstId(rid=rid, pnc=pid)], dma_engine_mask=sum(1 << e for e in some[a::2]), remote_sem=T.sem[sem], src=x, dst=y)
+                 for a, (y, x) in enumerate(pairs)]
+        op("pool", lambda: g.remote_dma_fused(moves, local_sem=T.sem.sent), ("r", nbytes), r, w, kind="send", sem=sem)
 
     dma("sp", T.vpi[:, 0:16], T.vn[:], 8192, [], ["vpi0"])
     dma("act", T.vpi[:, 16:32], T.pn[:], 8192, [], ["vpi1"])
@@ -137,7 +182,7 @@ def build_ops(g, T, topo, core):
     dma("sp", T.spd[:, 768:1024], T.pdir[:, 768:1024], 131072, [], ["spd1"])
     dma("act", T.wti[:, 0:1], T.wt[:], 512, [], ["wti0"])
     dma("act", T.wti[:, 8:9], T.th[:], 512, [], ["wti1"])
-    dma("sp", T.z0[:, 0:256], T.z[:], 65536, [], ["z0"])
+    dma("sp", T.z0[:], T.z[:], 65536, [], ["z0_0", "z0_1"])
     dma("sp", T.xw[:, 0:2048], T.xl[:], 524288, [], ["x0", "x1"])
     dma("sp", T.xw[:, 2048:3072], T.xl[:, 0:1024], 262144, [], ["xd"])
 
@@ -147,24 +192,33 @@ def build_ops(g, T, topo, core):
     iota(T.w2[:, 0:512], [[1, 512]], 0, 0, 512, ["w2a"])
     iota(T.blk[:], [[16, 8], [0, 16]], 0, 0, 128, ["blk"])
     iota(T.b8[:], [[0, 8], [1, 2], [0, 8]], 0, 0, 128, ["b8"])
-    iota(T.w3[:, 0:1024], [[1, 1024]], 0, 0, 1024, ["w3a"])
-    iota(T.w3[:, 1024:2048], [[1, 1024]], 1024, 0, 1024, ["w3b"])
+    ms(T.zr[:], 0.0, 256, ["zr"])
+    mark(T.idb[:], [[-1, 128]], 0, 1.0, 128, ["idb"])
     act(T.w2[:, 512:1024], T.w2[:, 0:512], F.Identity, 512, ["w2a"], ["w2b"], bias=512.0)
     act(T.w2[:, 1024:2048], T.w2[:, 0:1024], F.Identity, 1024, ["w2a", "w2b"], ["w2c"], bias=1024.0)
-    for c, bits in enumerate((15, 112, 1, 126, 127)):
+    act(T.big[:], T.zr[:, 0:256], F.Silu, 256 + 1400, ["zr"], ["big"], bias=65536.0)
+    for a, k in enumerate("ab"):
+        if CONST["w3"][a % len(CONST["w3"])] == "P":
+            iota(T.w3[:, 1024 * a:1024 * a + 1024], [[1, 1024]], 1024 * a, 0, 1024, ["w3" + k])
+        else:
+            act(T.w3[:, 1024 * a:1024 * a + 1024], T.w2[:, 0:1024], F.Identity, 1024, ["w2a", "w2b"], ["w3" + k], bias=1024.0 * a)
+    for c, bits in enumerate((15, 112, 1, 126)):
         ts(T.pj[:, c:c + 1], T.pi[:, 0:1], bits, A.bitwise_and, 1, ["pi"], ["pj%d" % c])
-    cp(T.col[:, 0:5], T.pj[:, 0:5], 5, ["pj%d" % c for c in range(5)], ["c0"])
+    cp(T.col[:, 0:4], T.pj[:, 0:4], 4, ["pj%d" % c for c in range(4)], ["c0"])
     ts(T.m16[:], T.row[:, 0:16], col(0), A.is_equal, 16, ["row", "c0"], ["m16"])
-    ts(T.idb[:], T.row[:, 0:128], col(4), A.is_equal, 128, ["row", "c0"], ["idb"])
-    cp(T.pl0[:, 16:48], T.vpi[:], 32, ["vpi0", "vpi1"], ["pl0"])
-    cp(T.e1[:], T.svd[:, 0:1024].indirect(T.pl0[:, 16:32]), 256, ["svd", "pl0"], ["e10", "e1"], cost="g")
+    cp(T.pl0[:, 32:64], T.vpi[:], 32, ["vpi0", "vpi1"], ["pl0"])
+    cp(T.vb0[:, 272:288], T.vpi[:, 0:16], 16, ["vpi0"], ["vl0"])
+    cp(T.pb0[:, 272:288], T.vpi[:, 16:32], 16, ["vpi1"], ["pq0"])
     cp(T.w2[:, 2048:2816], T.spd[:, 0:768], 768, ["spd0"], ["pd0"])
     cp(T.w2[:, 2816:3072], T.spd[:, 768:1024], 256, ["spd1"], ["pd1"])
     for a in range(2):
         cp(T.w3[:, 2048 + 512 * a:2560 + 512 * a], T.svd[:, 512 * a:512 * a + 512], 512, ["svd"], ["vd%d" % a])
     for a in range(4):
-        many("dve", [(lambda k=k: V.tensor_scalar(T.dh[:, 128 * k:128 * k + 128], T.idb[:], T.m16[:, k:k + 1], None, A.mult))
-                     for k in range(4 * a, 4 * a + 4)], [64] * 4, ["idb", "m16"], ["dh%d" % a])
+        if CONST["dh"][a % len(CONST["dh"])] == "P":
+            mark(T.dh[:, 512 * a:512 * a + 512], [[128, 4], [-16, 8], [-129, 16]], 512 * a, 1.0, 512, ["dh%d" % a])
+        else:
+            many("dve", [(lambda k=k: V.tensor_scalar(T.dh[:, 128 * k:128 * k + 128], T.idb[:], T.m16[:, k:k + 1], None, A.mult))
+                         for k in range(4 * a, 4 * a + 4)], [64] * 4, ["idb", "m16"], ["dh%d" % a])
     DH = ["dh%d" % a for a in range(4)]
     act(T.idf[:], T.idb[:], F.Identity, 128, ["idb"], ["idf"])
     ts(T.par[:], T.b8[:], col(2), A.is_equal, 128, ["b8", "c0"], ["par"])
@@ -180,80 +234,176 @@ def build_ops(g, T, topo, core):
     scale = [2.0 ** (97 - 13 * jh) for jh in range(16)]
     many("act", [(lambda jh=jh: S.activation(T.th2[:, 16 * jh:16 * jh + 16], T.m16[:], F.Identity, scale=-2.56 * scale[jh]))
                  for jh in range(16)], [16] * 16, ["m16"], ["th2"])
-    cp(T.idh[:], T.idb[:], 64, ["idb"], ["idh"])
     cp(T.col[:, 7:9], T.wti[:, 0:9:8], 2, ["wti0", "wti1"], ["c7"])
     act(T.bw[:], T.bn[:], F.Identity, 144, ["bn", "c7"], ["bw"], scale=col(7))
-    iota(T.t8[:], [[0, 128], [1, 8]], 0, 0, 1024, ["t8"])
-    iota(T.j8c[:], [[8, 256]], 0, 0, 256, ["j8c"])
-    for name, val in (("idn", -1.0), ("idq", 0.5), ("ip2", 2048.0), ("in2", -2048.0), ("i64", 64.0), ("i4k", 4096.0), ("i18", 262144.0)):
-        act(T[name][:], T.idb[:], F.Identity, 128, ["idb"], [name], scale=val)
+    send(T.bw2[:], T.bw[:], "rw", 36864, ["bw"], ["bw2"], -1)
+    for name, val in (("i37", 37.0 * 32), ("ip2", 2048.0), ("in2", -2048.0), ("idn", -1.0), ("idq", 0.5), ("i64", 64.0), ("i4k", 4096.0), ("i18", 262144.0)):
+        if CONST["ids"] == "P":
+            mark(T[name][:], [[-1, 128]], 0, val, 128, [name])
+        else:
+            act(T[name][:], T.idb[:], F.Identity, 128, ["idb"], [name], scale=val)
+    for a in range(4):
+        mark(T.lb[:, 512 * a:512 * a + 512], [[-1, 4], [-16, 8], [0, 16]], -4 * a, 1.0, 512, ["lb%d" % a])
+    LB = ["lb%d" % a for a in range(4)]
+    iota(T.w2[:, 3072:3584], [[1, 512]], 3072, 0, 512, ["w2t"])
+    iota(T.w3[:, 3072:3584], [[1, 512]], 3072, 0, 512, ["w3t", "E0", "E1"])
     ts(T.selz[:, 128:256], T.blk[:], col(1), A.is_equal, 128, ["blk", "c0"], ["selz1"], -1.0, A.mult)
     act(T.selz[:, 0:128], T.selz[:, 128:256], F.Identity, 128, ["selz1"], ["selz0"], scale=16.0)
-    act(T.sel[:, 0:16], T.selz[:, 0:256:16], F.Identity, 16, ["selz0", "selz1"], ["sel0"], scale=-2.0)
-    act(T.sel[:, 16:32], T.selz[:, 0:256:16], F.Identity, 16, ["selz0", "selz1"], ["sel1"])
-    SEL = ["sel0", "sel1"]
-    iota(T.big[:], [[0, 128]], 65536, 0, 128, ["big"])
-    act(T.half[:], T.big[:], F.Identity, 128, ["big"], ["half"], scale=0.5 / 65536)
-    ts(T.oneh[:], T.idb[:], -1.0, A.is_gt, 64, ["idb"], ["oneh"])
+    ms(T.sel[:], 0.0, 40, ["sel"])
+    many("act", [(lambda w=w, a=a: S.activation(T.sel[:, 40 * w + 16 * a + 8:40 * w + 16 * a + 16], T.selz[:, 128 * a:128 * a + 128:16], F.Identity,
+                                                scale=(-2.0, 1.0)[w])) for w in range(2) for a in range(2)], [21] * 4, ["selz0", "selz1"], ["sel"])
+    act(T.half[:], T.big[:, 0:128], F.Identity, 128, ["big"], ["half"], scale=8.0 / 65536)
+    iota(T.oneh[:], [[0, 128]], 1, 0, 128, ["oneh"])
+    ms(T.st[:, 7:8], 1.0, 1, ["stp"])
+    act(col(11), T.m16[:, 0:1], F.Identity, 1, ["m16"], ["c11"], bias=1.0 - SH / 2048)
+    act(col(10), T.m16[:, 0:1], F.Identity, 1, ["m16"], ["c10"], scale=2048.0, bias=-2048.0)
     act(col(9), col(8), F.Identity, 1, ["c7"], ["c9"], scale=-1.0, bias=0.5)
     ts(T.kc[:, 0:128], T.idb[:], col(0), A.mult, 64, ["idb", "c0"], ["kc0"])
     ts(T.kc[:, 128:256], T.idb[:], col(9), A.mult, 64, ["idb", "c9"], ["kc"])
-    op("pool", lambda: g.affine_select(T.rst[:], T.big[:], [[0, 8], [1, 16]], A.is_equal, 0.0, 0, 0), ("i", 128), ["big"], ["rst"])
-    ts(T.mix[:], T.blk[:, 0:128:16], 15.0, A.add, 8, ["blk"], ["mix"])
+    op("pool", lambda: g.affine_select(T.rst[:], T.big[:], [[0, 16], [1, 16]], A.is_equal, 0.0, 0, 0), ("i", 256), ["big"], ["rst"])
+    cp(T.mix[:], T.row[:, 0:16], 16, ["row"], ["mix"])
     ts(T.jl[:], T.row[:, 0:16], 16.0, A.mult, 16, ["row", "c0"], ["jl"], col(0), A.add)
     for a in range(2):
         act(T.dt[:, 16 * a:16 * a + 16], T.jl[:], F.Identity, 16, ["jl"], ["dt%d" % a], bias=1024.0)
-        act(T.j8r[:, 8 * a:8 * a + 8], T.jl[:, 0:8], F.Identity, 8, ["jl"], ["j8r%d" % a], scale=8.0)
-    ts(T.jc[:, 0:16], T.jl[:], 16.0, A.mult, 16, ["jl"], ["jc"])
+    act(T.j8r[:, 0:16], T.jl[:], F.Identity, 16, ["jl"], ["j8r"], scale=8.0)
+    ms(T.j8r[:, 16:32], 0.0, 16, ["j8z"])
+    ts(T.jc[:, 0:16], T.jl[:], 16.0, A.mult, 16, ["jl"], ["jc"], 16.0, A.add)
     ts(T.jc[:, 16:32], T.jl[:], 0.0, A.mult, 16, ["jl"], ["jc0"])
-    iota(T.m128[:], [[0, 128]], -128, 0, 128, ["m128"])
-    ts(T.i1k[:], T.idb[:, 0:128:16], 1024.0, A.mult, 8, ["idb"], ["i1k"])
+    iota(T.m128[:], [[0, 256]], -128, 0, 256, ["m128"])
+    mark(T.i1k[:], [[-16, 8]], 0, 1024.0, 8, ["i1k"])
     ms(T.abias[:, 0:1], 0.0, 1, ["abias"])
 
     W2I, W3I = ["w2a", "w2b", "w2c"], ["w3a", "w3b"]
     ident = T.w2[:, 0:1024]
     IDK = ["w2a", "w2b"]
     XG = ["xg%d" % c for c in range(8)]
-    rot = dict(wd=0, wf=0, bank=0)
+    rot = dict(wd=0, wf=0, wh=0, wv=0, bank=0, held=0)
 
-    def look(lk, q, eng):
+    kept = {}
+
+    SETS = 16 // ZR
+    zbank = lambda h: "Bz%d" % (h * (ZR == 8))
+
+    def zin(q, m, r=slice(None)):
+        c = 64 * (q % 2 if ZR == 8 else q)
+        return T["pz%d" % (q // 2 * (ZR == 8))][:, c:c + 64 * m, r, :]
+
+    def bank():
+        rot["bank"] += 1
+        return PICK[rot["bank"] % len(PICK)]
+
+    def look(t, lk, q, eng):
         win, wk = (T.w2, W2I + ["pd0", "pd1"]) if lk == 2 else (T.w3, W3I + ["vd0", "vd1"])
+        if t and TOKENS:
+            win, wk = win[:, 0:3584], wk + (["w2t"] if lk == 2 else ["w3t", "E0", "E1"])
+        else:
+            win = win[:, 0:3072]
         src, sk = (T.e1, "e1" if q else "e10") if lk == 2 else (T.e2, "e2%d" % q)
         dst, dk = (T.e2, "e2%d" % q) if lk == 2 else (T.e3, "e3%d" % q)
-        if eng in "HJ":
-            o0 = 2048 + 1024 * (q % 2)
-            act(T.wf[:, o0:o0 + 1024], win[:, 0:3072].indirect(src[:, 64 * q:64 * q + 64]), F.Identity, 1024, wk + [sk], ["wh%d" % (q % 2)], cost="g", bias=-1024.0)
-            if eng == "J":
-                s = rot["wf"] % 2; rot["wf"] += 1
-                b, et, j0 = 2 + s, T.et[:, 128 * s:128 * s + 128], 128 * (q // 2)
+        defer, eng = eng.islower(), eng.upper()
+
+        def land(b, c, n):
+            if rot["held"]:
+                b = rot["held"]
+            return ps[b][:, 256 + 64 * (c % 2):256 + 64 * (c % 2 + n)], "B%d" % b, True
+
+        def offsets(b, n):
+            if defer:
+                rot["held"] = b
+                return
+            if rot["held"]:
+                b, n = rot["held"], 2
+            rot["held"] = 0
+            c = q - q % n
+            got, key = ps[b][:, 256 + 64 * (c % 2):256 + 64 * (c % 2 + n)], "B%d" % b
+            ts(dst[:, 64 * c:64 * (c + n)], got, SH, A.add, 64 * n, [], [key] + [dk[:2] + str(c + a) for a in range(n)])
+
+        both = [sk, sk if lk == 2 and q > 1 else sk[:2] + str(q ^ 1) if lk == 3 else "e1"]
+        if eng == "V":
+            s = rot["wv"] % 2; rot["wv"] += 1
+            o0 = 2048 * s
+            ts(T.wv[:, o0:o0 + 2048], win.indirect(src[:, 64 * q:64 * q + 128]), -SH, A.add, 2048, wk + both, ["wv%d" % s], cost="g")
+            b = bank()
+            got, key, start = land(b, q, 2)
+            for a in range(2):
+                pe([(got, T.dh[:, 128 * k:128 * k + 128], T.wv[:, o0 + k:o0 + 2048:16], k == 0, k == 15, 128) for k in range(8 * a, 8 * a + 8)],
+                   DH + ["wv%d" % s], [key])
+            offsets(b, 2)
+            return
+        if eng in "HJG":
+            s = rot["wh"] % 2
+            o0 = 2048 + 2048 * s
+            if eng == "G":
+                act(T.wf[:, o0:o0 + 2048], win.indirect(src[:, 64 * q:64 * q + 128]), F.Identity, 2048, wk + both, ["wh%d0" % s, "wh%d1" % s], cost="g", bias=-SH)
+            else:
+                for a in range(HSPLIT):
+                    n = 64 // HSPLIT
+                    c = 64 * (q % 2) + n * a
+                    act(T.wf[:, o0 + 16 * c:o0 + 16 * (c + n)], win.indirect(src[:, 64 * q + n * a:64 * q + n * a + n]), F.Identity, 16 * n, wk + [sk],
+                        ["wh%d%d" % (s, q % 2) + "x" * a], cost="g", bias=-SH)
+            if eng != "H":
+                rot["wh"] += 1
+                b = bank()
                 for a in range(8):
-                    pe([(ps[b][:, k:128:16], T.wf[:, 2048 + k:4096:16], T.idf[:, k:128:16], k == 0, k == 15, 256) for k in range(2 * a, 2 * a + 2)],
-                       ["idf", "wh0", "wh1"], ["B%d" % b])
-                cp(et, ps[b][:, 0:128], 128, [], ["B%d" % b, "et%d" % s])
-                pe([(ps[b][:, 128:256], et, T.idh[:], True, True, 128)], ["et%d" % s, "idh"], ["B%d" % b])
-                ts(dst[:, j0:j0 + 128], ps[b][:, 128:256], 1024.0, A.add, 128, [], ["B%d" % b, dk[:2] + str(q ^ 1), dk])
+                    pe([(ps[b][:, k:128:16], T.wf[:, o0 + k:o0 + 2048:16], T.idf[:, k:128:16], k == 0, k == 15, 256) for k in range(2 * a, 2 * a + 2)],
+                       ["idf"] + ["wh%d%d" % (s, c) + "x" * x for c in range(2) for x in range(HSPLIT)], ["B%d" % b])
+                got, key, start = land(b, q - q % 2, 2)
+                if HJ == "D":
+                    s = s if lk == 2 else 2 + q
+                    et = T.et[:, 128 * s:128 * s + 128]
+                    cp(et, ps[b][:, 0:128], 128, [], ["B%d" % b, "et%d" % s])
+                    pe([(got, et, T.idb[:], start, True, 128)], ["et%d" % s, "idb"], [key])
+                    if lk == 3:
+                        kept[q - q % 2] = (2, [(et, T.idb[:])], ["et%d" % s, "idb"])
+                else:
+                    et = T.ew[:, 128 * s:128 * s + 128]
+                    act(et, ps[b][:, 0:128], F.Identity, 128, [], ["B%d" % b, "ew%d" % s])
+                    pe([(got, et, T.idf[:], start, True, 512)], ["ew%d" % s, "idf"], [key])
+                offsets(b, 2)
             return
         if eng == "A":
             s = rot["wf"] % 2; rot["wf"] += 1
-            o0, b, et = 1024 * s, 2 + s, T.et[:, 128 * s:128 * s + 128]
-            act(T.wf[:, o0:o0 + 1024], win[:, 0:3072].indirect(src[:, 64 * q:64 * q + 64]), F.Identity, 1024, wk + [sk], ["wf%d" % s], cost="g", bias=-1024.0)
+            c = s if lk == 2 else 2 + q
+            o0, b, et = 1024 * s, bank(), T.et[:, 128 * c:128 * c + 128]
+            m = HSPLIT if lk == 2 and t else 1
+            for a in range(m):
+                act(T.wf[:, o0 + 1024 // m * a:o0 + 1024 // m * (a + 1)], win.indirect(src[:, 64 * q + 64 // m * a:64 * q + 64 // m * (a + 1)]), F.Identity,
+                    1024 // m, wk + [sk], ["wf%d%d" % (s, x) for x in range(HSPLIT) if m == 1 or x == a], cost="g", bias=-SH)
             for a in range(4):
                 pe([(ps[b][:, k:128:8], T.wf[:, o0 + k:o0 + 1024:8], T.idf[:, k:128:8], k == 0, k == 7, 256) for k in range(2 * a, 2 * a + 2)],
-                   ["idf", "wf%d" % s], ["B%d" % b])
-            tt(et, ps[b][:, 0:128], T.par[:], A.mult, 128, ["par"], ["B%d" % b, "et%d" % s])
-            pe([(ps[b][:, 128:192], et, T.pair[:], True, True, 64)], ["et%d" % s, "pair"], ["B%d" % b])
-            ts(dst[:, 64 * q:64 * q + 64], ps[b][:, 128:192], 1024.0, A.add, 64, [], ["B%d" % b, dk])
+                   ["idf"] + ["wf%d%d" % (s, x) for x in range(HSPLIT)], ["B%d" % b])
+            tt(et, ps[b][:, 0:128], T.par[:], A.mult, 128, ["par"], ["B%d" % b, "et%d" % c])
+            got, key, start = land(b, q, 1)
+            pe([(got, et, T.pair[:], start, True, 64)], ["et%d" % c, "pair"], [key])
+            if lk == 3:
+                kept[q] = (1, [(et, T.pair[:])], ["et%d" % c, "pair"])
+            offsets(b, 1)
             return
-        name = "wd%d" % (rot["wd"] % 3); rot["wd"] += 1
-        if eng == "W":
-            ts(T[name][:], win[:, 0:3072].indirect(src[:, 64 * q:64 * q + 64]), -1024.0, A.add, 1024, wk + [sk], [name + "a", name + "b"], cost="g")
+        name = "wd%d" % (rot["wd"] % 3) if lk == 2 else "wk%d" % q
+        rot["wd"] += lk == 2
+        if lk == 3:
+            kept[q] = (1, [(T.dh[:, 128 * k:128 * k + 128], T[name][:, k:1024:16]) for k in range(16)], DH + [name + "a", name + "b"])
+        if eng != "D":
+            ts(T[name][:], win.indirect(src[:, 64 * q:64 * q + 64]), -SH, A.add, 1024, wk + [sk], [name + "a", name + "b"], cost="g")
         for a in range(2 * (eng == "D")):
-            ts(T[name][:, 512 * a:512 * a + 512], win[:, 0:3072].indirect(src[:, 64 * q + 32 * a:64 * q + 32 * a + 32]), -1024.0, A.add, 512,
+            ts(T[name][:, 512 * a:512 * a + 512], win.indirect(src[:, 64 * q + 32 * a:64 * q + 32 * a + 32]), -SH, A.add, 512,
                wk + [sk], [name + "ab"[a]], cost="g")
-        b = (5, 6)[rot["bank"] % 2]; rot["bank"] += 1
-        pe([(ps[b][:, 0:64], T.dh[:, 128 * k:128 * k + 128], T[name][:, k:1024:16], k == 0, k == 15, 64) for k in range(16)],
-           DH + [name + "a", name + "b"], ["B%d" % b])
-        ts(dst[:, 64 * q:64 * q + 64], ps[b][:, 0:64], 1024.0, A.add, 64, [], ["B%d" % b, dk])
+        b = rot["held"] or bank()
+        got, key, start = land(b, q, 1)
+        pe([(got, T.dh[:, 128 * k:128 * k + 128], T[name][:, k:1024:16], k == 0 and start, k == 15, 64) for k in range(16)],
+           DH + [name + "a", name + "b"], [key])
+        offsets(b, 1)
+
+    def early(t):
+        pl, plk = T["pl%d" % t], "pl%d" % t
+        win, wk = (T.w3[:, 2048:3072], ["vd0", "vd1"]) if t else (T.svd[:, 0:1024], ["svd"])
+        if FIRST[t]:
+            cp(T.e1[:, 0:64], win.indirect(pl[:, 32:36]), 64, wk + [plk], ["e10"], cost="g")
+            cp(T.e1[:, 64:256], win.indirect(pl[:, 36:48]), 192, wk + [plk], ["e1"], cost="g")
+        else:
+            cp(T.e1[:], win.indirect(pl[:, 32:48]), 256, wk + [plk], ["e10", "e1"], cost="g")
+        for q, eng in OVER.get(t, (LOOK2,))[0]:
+            look(t, 2, int(q), eng)
 
     def repeats(src, skey, c0, vfk, half):
         off, first = 0, True
@@ -273,200 +423,259 @@ def build_ops(g, T, topo, core):
             pe(mms, ["mt%d" % grp[0], "wb", "th2"], ["B7"])
         act(T.sl[:, 256 * half:256 * half + 256], ps[7][:, 0:256], F.Sign, 256, [], ["B7"] + (["fl"] if half else ["sl0", "sl1"]))
 
-    def to_list(j0, j1, keys, start):
-        pe(start + [(ps[7][:, 0:(j1 - j0) // 16], T.bn[:, 15 - jl:143 - jl], T.sl[:, j0 + jl:j1:16], jl == 0 and not start, jl == 15, 64) for jl in range(16)],
-           ["idh", "jc", "jc0", "bn"] + keys, ["B7"])
+    def to_list(b, j0, j1, keys, start):
+        pe(start + [(ps[b][:, 0:(j1 - j0) // 16], T.bn[:, 15 - jl:143 - jl], T.sl[:, j0 + jl:j1:16], jl == 0 and not start, jl == 15, 64) for jl in range(16)],
+           ["idb", "jc", "jc0"] * bool(start) + ["bn"] + keys, ["B%d" % b])
 
-    def marks(dst, c0, key):
-        act(dst[:, 256:272], ps[7][:, c0:c0 + 16], F.Identity, 16, [], ["B7", key], scale=128.0, bias=2048.0)
+    def marks(dst, c0, key, b=7):
+        ts(dst[:, 256:272], ps[b][:, c0:c0 + 16], 128.0, A.mult, 16, [], ["B%d" % b, key], 2048.0, A.add)
 
     def prepare(t):
         pl, plk, f0, vfk = T["pl%d" % t], "pl%d" % t, 32 * (t % 2), "vpf%d" % (t % 2)
-        cp(T.vpf[:, f0:f0 + 32], pl[:, 16:48], 32, [plk], [vfk])
-        cp(T["vb%d" % t][:], ident.indirect(pl[:, 16:32]), 256, IDK + [plk], ["vb%d" % t], cost="g")
+        vb, vbk, vmk = T["vb%d" % t], "vb%d" % t, "vm%d" % t
+        if t and VBP:
+            cp(T.vpf[:, f0:f0 + 16], pl[:, 32:48], 16, [plk], [vfk])
+            pe([(ps[7][:, jl:256:16], T.lb[:, 128 * jl:128 * jl + 128], vb[:, 272:288], jl == 0, jl == 15, 64) for jl in range(16)], LB + ["vl%d" % t], ["B7"])
+            cp(vb[:, 0:256], ps[7][:, 0:256], 256, [], ["B7", vbk])
+        else:
+            cp(T.vpf[:, f0:f0 + 32 - 16 * bool(t)], pl[:, 32:64 - 16 * bool(t)], 32, [plk], [vfk])
+            cp(vb[:, 0:256], ident.indirect(pl[:, 32:48]), 256, IDK + [plk], [vbk], cost="g")
+        repeats(vb, vbk, f0, vfk, 1)
+        if t and JOIN:
+            return
+        if t:
+            to_list(7, 256, 512, ["fl"], [])
+            marks(vb, 0, vmk)
+        else:
+            cp(T.pb0[:, 0:256], ident.indirect(pl[:, 48:64]), 256, IDK + [plk], ["pb0"], cost="g")
+            repeats(T.pb0, "pb0", 16, vfk, 0)
+            to_list(7, 0, 512, ["sl0", "sl1", "fl"], [])
+            marks(T.pb0, 0, "pm_0")
+            marks(vb, 16, vmk)
+        hand_on(t)
+
+    def hand_on(t):
         if t < NV - 1:
-            send(T["pb%d" % (t + 1)][:], T["vb%d" % t][:], "rb%d" % (t + 1), 65536, ["vb%d" % t], ["pb%d" % (t + 1)])
-        repeats(T["vb%d" % t], "vb%d" % t, f0, vfk, 1)
+            send(T["pb%d" % (t + 1)][:], T["vb%d" % t][:], "rb%d" % (t + 1), 73728, [k + str(t) for k in ("vb", "vm", "vl")],
+                 [k + str(t + 1) for k in ("pb", "pm_", "pq")])
+
+    def advance(z, zk, bw, v, vk, dst, dsh, dk, signs):
+        n = 16 + bool(signs)
+        pe([(ps[6][:, 32:48], T.i37[:], v, True, False, 64)] +
+           [(ps[6][:, 16:17], T.half[:], T.acc[:, h:h + 1], False, False, 256) for h in signs] +
+           [(ps[6][:, 0:16], T[bw][:, 15 - jl:143 - jl], z[:, jl:256:16], False, jl == 15, 64) for jl in range(16)],
+           [bw, "i37", vk, "half"] + zk + ["acc%d" % h for h in signs], ["B6"])
+        cp(T.ui[:, 0:n], ps[6][:, 0:n], n, [], ["B6", "ui"])
+        ts(T.um[:, 0:n], T.ui[:, 0:n], 4095, A.bitwise_and, n, ["ui"], ["um"])
+        tt(T.sq[:], T.um[:, 0:16], T.um[:, 0:16], A.mult, 32, ["um"], ["sq"])
+        if signs:
+            ts(T.abias[:, 0:1], T.um[:, 16:17], -1.0 / 16, A.mult, 1, ["um"], ["abias"])
+        tt(T.sm[:], T.sq[:], ps[6][:, 32:48], A.add, 16, ["sq"], ["B6", "sm"])
+        ts(T.ri[:, 16:32], T.sm[:], 5, A.logical_shift_right, 16, ["sm"], ["vi"], 1023, A.bitwise_and)
+        ts(T.ri[:, 0:16], T.ui[:, 0:16], 7, A.bitwise_and, 16, ["ui"], ["ri"])
+        tt(dsh[:], T.ri[:], T.j8r[:], A.add, 64, ["ri", "vi", "j8r", "j8z"], [dk + "m", dk + "w"])
+        cp(dst[:, 0:32], dsh[:], 16, [dk + "w", dk + "m"], [dk + "n", dk + "v"])
 
     def winners(t, hs):
-        z, zo, zk = T["z%d" % t], T["zo%d" % t], "z%d" % t
+        zo = T["zo%d" % t]
         c0, c1, j0, j1 = 8 * hs[0], 8 * hs[-1] + 8, 128 * hs[0], 128 * hs[-1] + 128
-        n, more = j1 - j0, t < NV - 1 and hs[-1] == 1
+        n, z = j1 - j0, T["z%d" % t][:, j0:j1]
+        more = JOIN and t < NV - 1 and hs[-1] == 1
         c2 = 32 if more else c1
-        to_list(j0, 16 * c2, ["sl%d" % h for h in hs] + ["fl"] * more, [(ps[7][:, 0:c2 - c0], T.idh[:], T.jc[:, c0:c2], True, False, 64)])
-        KU, XS, NL, ZO = ([k + str(h) for h in hs] for k in ("ku", "xs", "nl", "zo%d_" % t))
-        cp(T.ku[:, c0:c1], ps[7][:, 0:c1 - c0], 16, [], ["B7"] + KU)
+        b = NEAR[t] if hs[-1] == 1 else 6
+        to_list(b, j0, 16 * c2, ["sl%d" % h for h in hs] + ["fl"] * more, [(ps[b][:, 0:c2 - c0], T.idb[:], T.jc[:, 0:c2 - c0], True, False, 64)])
+        KU, XS, NL, ZO, Z = ([k + str(h) for h in hs] for k in ("ku", "xs", "nl", "zo%d_" % t, "z%d_" % t))
+        cp(T.ku[:, c0:c1], ps[b][:, 0:c1 - c0], 16, [], ["B%d" % b] + KU)
         if more:
-            marks(T["zo%d" % (t + 1)], c1 - c0, "zos%d" % (t + 1))
-        act(T.xs[:, j0:j1], T.xg[:, 0:4096].indirect(T.ku[:, c0:c1]), F.Identity, n, KU + XG, XS, cost="g")
-        pe([(ps[7][:, 0:n], T.idb[:], T.xs[:, j0:j1], True, False, n), (ps[7][:, 0:n], T.idn[:], z[:, j0:j1], False, True, n)],
-           XS + [zk, "idb", "idn"], ["B7"])
-        act(zo[:, j0:j1], ps[7][:, 0:n], F.Abs, n, [], ["B7"] + ZO)
-        pe([(ps[4][:, 256:256 + n], T.idq[:], T.xs[:, j0:j1], True, False, n), (ps[4][:, 256:256 + n], T.idq[:], z[:, j0:j1], False, True, n)],
-           XS + [zk, "idq"], ["B4"])
-        act(T.nl[:, j0:j1], ps[4][:, 256:256 + n], F.Identity, n, [], ["B4"] + NL, bias=127.75)
+            marks(T["vb%d" % (t + 1)], 16, "vm%d" % (t + 1), 6)
+            hand_on(t + 1)
+        act(T.xs[:, j0:j1], T.xg[:, 16 * j0:16 * j1].indirect(T.ku[:, c0:c1]), F.Identity, n, KU + XG[c0 // 2:c1 // 2], XS, cost="g")
+        pe([(ps[6][:, 0:n], T.idb[:], T.xs[:, j0:j1], True, False, n), (ps[6][:, 0:n], T.idn[:], z, False, False, n),
+            (ps[6][:, 256:256 + n], T.idq[:], T.xs[:, j0:j1], False, False, n), (ps[6][:, 256:256 + n], T.idq[:], z, False, True, n)],
+           XS + Z + ["idb", "idn", "idq"], ["B6"])
+        act(zo[:, j0:j1], ps[6][:, 0:n], F.Abs, n, [], ["B6"] + ZO)
+        if t < NV - 1 and ZSEND == 2:
+            send(T["z%d" % (t + 1)][:, j0:j1], zo[:, j0:j1], "r%s%d" % ("yz"[hs[-1]], t + 1), 256 * n, ZO, ["z%d_%d" % (t + 1, h) for h in hs])
+        elif t < NV - 1 and hs[-1] == 1:
+            send(T["z%d" % (t + 1)][:], zo[:], "rz%d" % (t + 1), 65536, ["zo%d_0" % t, "zo%d_1" % t], ["z%d_0" % (t + 1), "z%d_1" % (t + 1)])
+        act(T.nl[:, j0:j1], ps[6][:, 256:256 + n], F.Identity, n, [], ["B6"] + NL, bias=127.75)
+        for part in [[h] for h in hs] if XSPLIT else [hs]:
+            a, b = 128 * part[0], 128 * part[-1] + 128
+            tt(T.xw[:, 0:8 * b].indirect(T["pl%d" % t][:, a // 16:b // 16]), T.nl[:, a:b], T.m128[:, 0:b - a], A.add, b - a,
+               ["pn%dn" % t, "m128"] + ["nl%d" % h for h in part], ["x0", "x1"][:b // 128], cost="s")
+            if t < NV - 1 and part[0] == 0:
+                if TWICE[t]:
+                    tt(T.xw[:, 2048:3072].indirect(T["pl%d" % t][:, 0:8]), T.nl[:, 0:128], T.m128[:, 0:128], A.add, 128, ["pn%dn" % t, "m128", "nl0"], ["xd"], cost="s")
+                else:
+                    dma("sp", T.xw[:, 2048:3072], T.xw[:, 0:1024], 262144, ["x0"], ["xd"])
+            if t == NV - 1:
+                for a, b in enumerate((2, 3)):
+                    pe([(ps[b][:, 0:256], T[n][:], T.xw[:, 512 * q + 256 * a:512 * q + 256 * a + 256], q == 0, q == 3, 256)
+                        for q, n in enumerate(("idb", "i64", "i4k", "i18")) if q // 2 in part], ["idb", "i64", "i4k", "i18"] + ["x%d" % h for h in part], ["B%d" % b])
 
-    def rests(h):
-        if RB == 2:
-            act(T.rb[:, 128 * h:128 * h + 128], T.t8[:, 0:1024].indirect(T.nu[:, 8 * h:8 * h + 8]), F.Identity, 128, ["t8", "nu"], ["rb%d" % h], cost="g")
-        elif h == RB:
-            act(T.rb[:], T.t8[:, 0:1024].indirect(T.nu[:]), F.Identity, 256, ["t8", "nu"], ["rb0", "rb1"], cost="g")
+    def scatter(t, d, hs, token=False):
+        j0, n = 128 * hs[0], 128 * len(hs)
+        o0 = 32 * (t % 2) + 16 * d + 8 * hs[0]
+        out, keys = (T.w3, T.w2)[d][:, 2048:TK].indirect(T.ou[:, o0:o0 + n // 16]), (["vd0", "vd1"], ["pd0", "pd1"])[d]
+        r = ["ou%d" % (t % 2), "w2t", "w3t"]
+        if not token:
+            a0 = 256 + 2 * j0 + n * d
+            tt(out, T.w3[:, TK + j0:TK + j0 + n], T.a2[:, a0:a0 + n], A.max, n, r + [k + str(h) for k in ("E", "fp") for h in hs], keys, cost="s")
+        elif TOKEN_ENG[d] == "A":
+            act(out, T.w2[:, TK + j0:TK + j0 + n], F.Silu, n, r, keys + ["tok%d" % d], cost="s")
+        else:
+            cp(out, T.w2[:, TK + j0:TK + j0 + n], n, r, keys + ["tok%d" % d], cost="s")
 
-    def lines_out(h):
-        tt(T.xw[:, 1024 * h:1024 * h + 1024].indirect(T.nu[:, 8 * h:8 * h + 8]), T.nl[:, 128 * h:128 * h + 128], T.m128[:], A.add,
-           128, ["nu", "nl%d" % h, "m128"], ["x%d" % h], cost="s")
+    def tail(t, hs):
+        z, vb, pb = (T["%s%d" % (n, t)] for n in ("z", "vb", "pb"))
+        j0, j1, n = 128 * hs[0], 128 * hs[-1] + 128, 128 * len(hs)
+        pk, K = ps[4], lambda *names: [k + str(h) for k in names for h in hs]
+        pe([(pk[:, 256 * a + 128 * h:256 * a + 128 * h + 128], T.oneh[:], T.kc[:, 128 * a:128 * a + 128], a == 0 and h == 0, False, 128)
+            for h in range(2) for a in range(2)], ["oneh", "kc0", "kc"], ["B4"])
+        for h in hs:
+            xk = lambda k: T.xg[:, 2048 * h + k:2048 * h + 2048:16]
+            abk = lambda k: T.ab[:, 2048 * h + 128 * ZR * (k % SETS) + k // SETS:2048 * h + 128 * ZR * (k % SETS + 1):ZR]
+            pe([(pk[:, 256 + 128 * h:384 + 128 * h], z[:, 128 * h:128 * h + 128], T.selz[:, 128:256], False, False, 128)], ["selz1", "z%d_%d" % (t, h)], ["B4"])
+            for q, m in [(2 * h, 2)] if MAXH[t][h] else [(q, 1) for q in ORDER[h]]:
+                for par in range(SETS):
+                    a0 = 2048 * h + 128 * ZR * par + 64 * ZR * (q % 2)
+                    tt(T.ab[:, a0:a0 + 64 * ZR * m], T.xg[:, 1024 * q + par:1024 * (q + m):SETS], zin(q, m), A.max, 32 * ZR * m,
+                       XG[2 * q:2 * (q + m)], [zbank(h)] + ["ab%d%d" % (q + a, par) for a in range(m)])
+            for a in range(2):
+                pe([(pk[:, k:512:16], xk(k), T.sel[:, 48 - 8 * h:80 - 8 * h], False, False, 64) for k in range(8 * a, 8 * a + 8)], ["sel"] + XG[4 * h:4 * h + 4], ["B4"])
+            for par in range(SETS):
+                pe([(pk[:, k:512:16], abk(k), T.sel[:, 8 - 8 * h:40 - 8 * h], False, k == 15 and h == hs[-1], 64) for k in range(par, 16, SETS)],
+                   ["sel"] + ["ab%d%d" % (2 * h + a, par) for a in range(2)], ["B4"])
+        if hs[0] == 0:
+            ts(T.hi[:], T.e3[:], 2048.0, A.is_lt, 128, ["e30", "e31", "e32", "e33", "c11"], ["hi"], col(11), A.subtract)
+            if not REPICK[t]:
+                ts(T.et[:, 256:512], T.e3[:], -SH, A.add, 128, ["e30", "e31", "e32", "e33"], ["et2", "et3"])
+                for h in range(2):
+                    kept[2 * h] = (2, [(T.idb[:], T.et[:, 256 + 128 * h:384 + 128 * h])], ["idb", "et%d" % (2 + h)])
+                    kept.pop(2 * h + 1, None)
+        for a in range(2):
+            pe([(ps[5][:, 256 + jl:256 + n:16], T.lb[:, 128 * jl:128 * jl + 128], T["ph%d" % t][:, j0 // 16:j1 // 16], jl == 0, False, 64)
+                for jl in range(8 * a, 8 * a + 8)], LB + ["pn%dm" % t], ["B5"])
+        for q, (m, pairs, keys) in kept.items():
+            if q // 2 in hs:
+                pe([(ps[5][:, 64 * q - j0:64 * (q + m) - j0], l, x, False, False, 64 * m) for l, x in pairs], keys, ["B5"])
+        pe([(ps[5][:, 0:n], T.ip2[:], T.hi[:, j0:j1], False, False, n)], ["ip2", "hi"], ["B5"])
+        pm, least = T.pm[:, j0:j1], T.pn8[:, j0 // 16:j1 // 16]
+        op("dve", lambda: V.tensor_tensor_scan(pm, T.rst[:, 0:n], pk[:, j0:j1], 0.0, A.add, A.min), ("v", n), ["rst"], ["B4"] + K("pm"))
+        act(T.sg[:, j0:j1], pk[:, 256 + j0:256 + j1], F.Sign, n + 22, ["abias"], ["B4", "acc%d" % hs[0]] + K("sg"), bias=T.abias[:, 0:1],
+            accum_out=T.acc[:, hs[0]:hs[0] + 1])
+        if PN == "D":
+            cp(least, T.pm[:, j0 + 15:j1:16], 16, K("pm"), K("pn"))
+        else:
+            act(least, T.pm[:, j0 + 15:j1:16], F.Identity, 16, K("pm"), K("pn"))
+        tt(T.st[:, 8 + j0:8 + j1], least.indirect(T.mix[:, 0:n // 16]), pm, A.is_equal, n, K("pm", "pn") + ["mix"], K("st"), cost="g")
+        pe([(pk[:, 0:n], T.idb[:], pb[:, j0:j1], True, False, n), (pk[:, n:2 * n], T.idb[:], vb[:, j0:j1], False, False, n)],
+           ["idb", "pb%d" % t, "vb%d" % t], ["B4"])
+        pe([(pk[:, n * a + 128 * h - j0:n * a + 128 * h - j0 + 128], T.sg[:, 128 * h:128 * h + 128], (T.ip2, T.in2)[a][:], False, a == 1 and h == hs[-1], 128)
+            for h in hs for a in range(2)], K("sg") + ["ip2", "in2"], ["B4"])
+        act(T.a2[:, 256 + 2 * j0:256 + 2 * j1], pk[:, 0:2 * n], F.Identity, 2 * n, [], ["B4"] + K("fp"))
+        sT = lambda h, back=0: T.st[:, 8 + 128 * h - back:136 + 128 * h - back]
+        pe([(ps[5][:, c + 128 * h - j0:c + 128 * h - j0 + 128], sT(h, back), (T.ip2, T.in2)[(c == 0) ^ back][:], False, c == 0 and back == 1 and h == hs[-1], 128)
+            for c in (256, 0) for h in hs for back in range(2)], K("st") + ["st0", "stp", "ip2", "in2"], ["B5"])
+        if A2[t] == "A":
+            act(T.a2[:, j0:j1], ps[5][:, 256:256 + n], F.Identity, n, ["c10"], ["B5"] + K("a2"), bias=col(10))
+        else:
+            ts(T.a2[:, j0:j1], ps[5][:, 256:256 + n], col(10), A.add, n, ["c10"], ["B5"] + K("a2"))
+        tt(T.w3[:, TK + j0:TK + j1], ps[5][:, 0:n], T.a2[:, j0:j1], A.max, n, K("a2"), ["B5"] + K("E"))
+        b = NEAR[t] if hs[-1] == 1 else 6
+        pe([(ps[b][:, 128 * h - j0:128 * h - j0 + 128], sT(h), T.idn[:], h == hs[0], h == hs[-1], 128) for h in hs], K("st") + ["idn"], ["B%d" % b])
+        if SL[t] == "A":
+            act(T.sl[:, j0:j1], ps[b][:, 0:n], F.Identity, n, [], ["B%d" % b] + K("sl"))
+        else:
+            cp(T.sl[:, j0:j1], ps[b][:, 0:n], n, [], ["B%d" % b] + K("sl"))
 
     for t in range(NV):
-        z, zo, pl, vb, pb = (T["%s%d" % (n, t)] for n in ("z", "zo", "pl", "vb", "pb"))
-        zk, plk, pbk, vbk, pok = "z%d" % t, "pl%d" % t, "pb%d" % t, "vb%d" % t, "po%d" % t
+        z, zo, pl, ph, vb, pb = (T["%s%d" % (n, t)] for n in ("z", "zo", "pl", "ph", "vb", "pb"))
+        kept.clear()
+        ZK, plk, pnk = ["z%d_0" % t, "z%d_1" % t], "pl%d" % t, "pn%d" % t
         last = t == NV - 1
         look2, look3, lines = OVER.get(t, (LOOK2, LOOK3, LINES))
         f0, vfk = 32 * (t % 2), "vpf%d" % (t % 2)
 
-        if t and FIRST:
-            cp(T.e1[:, 0:64], T.w3[:, 2048:3072].indirect(pl[:, 16:20]), 64, ["vd0", "vd1", plk], ["e10"], cost="g")
-            cp(T.e1[:, 64:256], T.w3[:, 2048:3072].indirect(pl[:, 20:32]), 192, ["vd0", "vd1", plk], ["e1"], cost="g")
-        elif t:
-            cp(T.e1[:], T.w3[:, 2048:3072].indirect(pl[:, 16:32]), 256, ["vd0", "vd1", plk], ["e10", "e1"], cost="g")
-        for a, (q, eng) in enumerate(look2):
-            look(2, int(q), eng)
-            if t and a == 0:
-                lines_out(0)
-                dma("sp", T.xw[:, 2048:3072], T.xw[:, 0:1024], 262144, ["x0"], ["xd"])
-        for q, eng in look3:
-            look(3, int(q), eng)
-        if t:
-            lines_out(1)
-            pe([(ps[4][:, 0:1], T.half[:], T.acc[:, h:h + 1], h == 0, h == 1, 256) for h in range(2)], ["half", "acc0", "acc1"], ["B4"])
-            ts(T.ai[:, 0:1], ps[4][:, 0:1], 1.0 / 256, A.mult, 1, [], ["B4", "ai"], -127.5 / 256, A.add)
-            ts(T.abias[:, 0:1], T.ai[:, 0:1], 256.0, A.mult, 1, ["ai"], ["B4", "abias"], ps[4][:, 0:1], A.subtract)
-
+        tokens = [] if last else list(TOKENS)
         if t == 0:
+            early(0)
+            advance(z, ZK, "bw", vb[:, 272:288], "vl0", pl, ph, pnk, [])
+            send2([(T.pl1[:, 32:48], pl[:, 16:32]), (T.vb1[:, 272:288], ph[:, 16:32])], "rp1", 8192, [pnk + "v", pnk + "w"], ["pl1", "vl1"], 1)
             prepare(0)
-            cp(pb[:], ident.indirect(pl[:, 32:48]), 256, IDK + [plk], [pbk], cost="g")
-            repeats(pb, pbk, 16, vfk, 0)
-            to_list(0, 512, ["sl0", "sl1", "fl"], [])
-            marks(z, 0, "z0s")
-            marks(zo, 16, "zos0")
-        pe([(ps[4][:, 0:16], T.bw[:, 15 - jl:143 - jl], z[:, jl:256:16], jl == 0, jl == 15, 64) for jl in range(16)], ["bw", zk], ["B4"])
-        cp(T.ui[:], ps[4][:, 0:16], 16, [], ["B4", "ui"])
-        ts(T.um[:], T.ui[:], 4095, A.bitwise_and, 16, ["ui"], ["um"])
-        tt(T.sq[:], T.um[:], T.um[:], A.mult, 32, ["um"], ["sq"])
-        act(T.vm[:], T.vpf[:, f0:f0 + 16], F.Identity, 16, [vfk], ["vm"], scale=37.0 * 32)
-        tt(T.sm[:], T.sq[:], T.vm[:], A.add, 32, ["sq", "vm"], ["sm"])
-        ts(T.vi[:], T.sm[:], 5, A.logical_shift_right, 16, ["sm"], ["vi"], 1023, A.bitwise_and)
-        cp(pl[:, 0:16], T.vi[:], 16, ["vi"], [pok])
-        if not last:
-            send(T["pl%d" % (t + 1)][:, 16:48], pl[:, 0:32], "rp%d" % (t + 1), 8192, [pok, plk], ["pl%d" % (t + 1)])
-        ts(T.ri[:], T.ui[:], 7, A.bitwise_and, 16, ["ui"], ["ri"])
-        tt(T.nf[:], T.ri[:], T.j8r[:], A.add, 32, ["ri", "j8r0", "j8r1"], ["nf"])
-
-        for a in range(2):
-            op("pool", lambda a=a, z=z: g.affine_select(T.zz[:, a:512:2], z[:, 0:256], [[0, 256]], A.is_ge, 0.0, 0, 0), ("i", 256), [zk], ["zz%d" % a])
-        turn([(T.pz1[:, 16 * q:16 * q + 16, :, :], T.zz[:, 128 * q:128 * q + 128]) for q in range(4)], ["zz0", "zz1"], "Bz1")
-        if ZT == "D":
-            cp(T.zt[:], T.pz1[:, 0:64, :, :], 256, [], ["Bz1", "zt"])
-        else:
-            act(T.zt[:], T.pz1[:, 0:64, :, :], F.Identity, 512, [], ["Bz1", "zt"])
-        for q in ORDER[0] + ORDER[1]:
-            turn([(T["pz%d" % (q // 2)][:, 64 * (q % 2):64 * (q % 2) + 64, r, :], T.zt[:, 128 * q:128 * q + 128]) for r in range(4)], ["zt"], "Bz%d" % (q // 2))
-
-        cp(T.nu[:], T.nf[:], 16, ["nf"], ["nu"])
-        for a, (c, eng) in enumerate(lines):
-            c = int(c)
-            if a == 4:
-                rests(0)
-            o, gath = T.xg[:, 512 * c:512 * c + 512], T.xw[:, 0:3072].indirect(T.e3[:, 32 * c:32 * c + 32])
-            if eng == "D":
-                cp(o, gath, 512, ["x0", "x1", "xd", "e3%d" % (c // 2)], ["xg%d" % c], cost="g")
-            else:
-                act(o, gath, F.Identity, 512, ["x0", "x1", "xd", "e3%d" % (c // 2)], ["xg%d" % c], cost="g")
-        rests(1)
-
-        pe([(ps[7][:, 0:32], T.idf[:], T.vpf[:, f0:f0 + 32], True, False, 256)] +
-           [(ps[7][:, 16 * a:16 * a + 16], T.idb[:], m[:, 256:272], False, a == 1 and m is z, 64) for m in (zo, z) for a in range(2)],
-           ["idf", "idb", vfk, "zos%d" % t, "z0s" if t == 0 else zk], ["B7"])
+        pe([(ps[7][:, 16 * a:16 * a + 16], T.idb[:], m[:, 272:288], a == 0, False, 64) for a, m in enumerate((vb, pb))] +
+           [(ps[7][:, 16 * a:16 * a + 16], T.idb[:], m[:, 256:272], False, a == 1 and m is pb, 64) for m in (vb, pb) for a in range(2)],
+           ["idb", "vl%d" % t, "pq%d" % t, "vm%d" % t, "pm_%d" % t], ["B7"])
         tt(T.of[:], ps[7][:, 0:32], T.dt[:], A.min, 32, ["dt0", "dt1"], ["B7", "of"])
-        cp(T.ou[:], T.of[:], 32, ["of"], ["ou"])
+        cp(T.ou[:, f0:f0 + 32], T.of[:], 32, ["of"], ["ou%d" % (t % 2)])
+        for hs in TPARTS if tokens else ():
+            scatter(t, 1, hs, True)
+        for q, eng in look3:
+            look(t, 3, int(q), eng)
+        for hs in TPARTS if tokens else ():
+            scatter(t, 0, hs, True)
 
-        for h in range(2):
-            j0, j1 = 128 * h, 128 * h + 128
-            kb = (4, 3)[h]
-            pk, KB = ps[kb], "B%d" % kb
-            E3 = ["e3%d" % (2 * h), "e3%d" % (2 * h + 1)]
-            XH = XG[4 * h:4 * h + 4]
-            pe([(pk[:, 0:256], T.oneh[:], T.kc[:], True, False, 256)], ["oneh", "kc0", "kc"], [KB])
-            xk = lambda k: T.xg[:, 2048 * h + k:2048 * h + 2048:16]
-            abk = lambda k: T.ab[:, 2048 * h + 1024 * (k % 2) + k // 2:2048 * h + 1024 * (k % 2) + 1024:8]
-            pe([(pk[:, 0:256], z[:, j0:j1], T.selz[:], False, False, 256)], ["selz0", "selz1", zk], [KB])
-            for q in ORDER[h]:
-                for par in range(2):
-                    a0 = 2048 * h + 1024 * par + 512 * (q % 2)
-                    tt(T.ab[:, a0:a0 + 512], T.xg[:, 1024 * q + par:1024 * q + 1024:2], T["pz%d" % h][:, 64 * (q % 2):64 * (q % 2) + 64, :, :], A.max, 256,
-                       XG[2 * q:2 * q + 2], ["Bz%d" % h, "ab%d%d" % (q, par)])
+        for hs in ZPARTS[t]:
+            j0, j1, pz, pzk = 128 * hs[0], 128 * hs[-1] + 128, T["pz%d" % (hs[0] * (ZR == 8))], zbank(hs[0])
+            w, o = 128 // ZR, 128 * hs[0] * (ZR == 4)
+            n = j1 - j0
+            ZZ, ZT_ = ["zz%d%d" % (h, a) for a in range(2) for h in hs], ["zt%d" % h for h in hs]
             for a in range(2):
-                pe([(pk[:, k:256:16], xk(k), T.sel[:, 16:32], False, False, 64) for k in range(8 * a, 8 * a + 8)], SEL + XH, [KB])
-            for par in range(2):
-                pe([(pk[:, k:256:16], abk(k), T.sel[:, 0:16], False, k == 15, 64) for k in range(par, 16, 2)],
-                   SEL + ["ab%d%d" % (2 * h + a, par) for a in range(2)], [KB])
-            if not WHOLE:
-                ts(T.ef[:, j0:j1], T.e3[:, j0:j1], -2048.0, A.add, 64, E3, ["ef%d" % h])
-                ts(T.hi[:, j0:j1], T.e3[:, j0:j1], 2048.0, A.is_lt, 64, E3, ["hi%d" % h])
-            elif h == 0:
-                ts(T.ef[:], T.e3[:], -2048.0, A.add, 128, ["e30", "e31", "e32", "e33"], ["ef0", "ef1"])
-                ts(T.hi[:], T.e3[:], 2048.0, A.is_lt, 128, ["e30", "e31", "e32", "e33"], ["hi0", "hi1"])
-            pe([(ps[5][:, 0:128], T.idh[:], T.ef[:, j0:j1], True, False, 128), (ps[5][:, 0:128], T.ip2[:], T.hi[:, j0:j1], False, False, 128)],
-               ["idh", "ip2", "ef%d" % h, "hi%d" % h], ["B5"])
-            pe([(ps[2][:, 0:128], T.idb[:], T.rb[:, j0:j1], True, False, 128), (ps[2][:, 0:128], T.idb[:], T.j8c[:, j0:j1], False, False, 128)],
-               ["idb", "rb%d" % h, "j8c"], ["B2"])
-            pe([(ps[6][:, 128:256], T.idh[:], pb[:, j0:j1], True, False, 128), (ps[6][:, 256:384], T.idh[:], vb[:, j0:j1], False, False, 128)],
-               ["idh", pbk, vbk], ["B6"])
-            pm, ky, sT = T.pm[:, j0:j1], T.ky[:, j0:j1], T.st[:, j0:j1]
-            act(ky, pk[:, 0:128], F.Identity, 128, [], [KB, "ky%d" % h])
-            act(T.sg[:, j0:j1], pk[:, 128:256], F.Sign, 150, ["abias"], [KB, "sg%d" % h, "acc%d" % h], bias=T.abias[:, 0:1], accum_out=T.acc[:, h:h + 1])
-            op("dve", lambda pm=pm, ky=ky: V.tensor_tensor_scan(pm, T.rst[:], ky, 0.0, A.add, A.min), ("v", 128), ["rst", "ky%d" % h], ["pm%d" % h])
-            tt(sT, pm.indirect(T.mix[:]), ky, A.is_equal, 128, ["pm%d" % h, "ky%d" % h, "mix"], ["st%d" % h], cost="g")
-            pe([(ps[6][:, 128:256], T.sg[:, j0:j1], T.ip2[:], False, False, 128), (ps[6][:, 256:384], T.sg[:, j0:j1], T.in2[:], False, True, 128)],
-               ["sg%d" % h, "ip2", "in2"], ["B6"])
-            a0 = 384 * h
-            act(T.a2[:, a0 + 128:a0 + 384], ps[6][:, 128:384], F.Identity, 256, [], ["B6", "fv%d" % h, "fp%d" % h])
-            pe([(ps[2][:, 0:128], sT, T.ip2[:], False, True, 128)], ["st%d" % h, "ip2"], ["B2"])
-            pe([(ps[5][:, 0:128], sT, T.in2[:], False, True, 128)], ["st%d" % h, "in2"], ["B5"])
-            pe([(ps[6][:, 0:128], sT, T.idb[:], True, True, 128)], ["st%d" % h, "idb"], ["B6"])
-            act(T.a2[:, a0:a0 + 128], ps[2][:, 0:128], F.Identity, 128, [], ["B2", "a2%d" % h], bias=-2048.0)
-            act(T.sl[:, j0:j1], ps[6][:, 0:128], F.Identity, 128, ["c0"], ["B6", "sl%d" % h], scale=col(0))
-            tt(T.ep[:, j0:j1], ps[5][:, 0:128], T.a2[:, a0:a0 + 128], A.max, 128, ["a2%d" % h], ["B5", "ep%d" % h])
-            tt(T.w3[:, 2048:3328].indirect(T.ou[:, 8 * h:8 * h + 8]), T.ep[:, j0:j1], T.a2[:, a0 + 128:a0 + 256], A.max, 128,
-               ["ou", "ep%d" % h, "fv%d" % h], ["vd0", "vd1"], cost="s")
-            tt(T.w2[:, 2048:3328].indirect(T.ou[:, 16 + 8 * h:24 + 8 * h]), T.ep[:, j0:j1], T.a2[:, a0 + 256:a0 + 384], A.max, 128,
-               ["ou", "ep%d" % h, "fp%d" % h], ["pd0", "pd1"], cost="s")
-            if last and h == 1:
-                dma("sp", T.yvd[:], T.w3[:, 2048:3072], 524288, ["vd0", "vd1"], [])
-                dma("sp", T.ypd[:], T.w2[:, 2048:3072], 524288, ["pd0", "pd1"], [])
-            if SPLIT_WIN[t]:
-                winners(t, [h])
-            if h == 0 and not last:
-                prepare(t + 1)
-            elif h == 0:
-                act(T.yt[:], ident.indirect(pl[:, 0:16]), F.Identity, 256, IDK + [pok], ["yt"], cost="g")
-                pe([(ps[7][0:8, 0:256], T.i1k[:], vb[:], True, False, 256), (ps[7][0:8, 0:256], T.idf[:, 0:128:16], T.yt[:], False, True, 1024)],
-                   ["i1k", "idf", vbk, "yt"], ["B7"])
-                act(T.yv[0:8, :], ps[7][0:8, 0:256], F.Identity, 256, [], ["B7", "yv"])
-                dma("sp", T.yvp[:], T.yv[0:8, :], 8192, ["yv"], [])
-        if not SPLIT_WIN[t]:
-            winners(t, [0, 1])
-        ZO = ["zo%d_0" % t, "zo%d_1" % t]
+                op("pool", lambda a=a, z=z, j0=j0, j1=j1: g.affine_select(T.zz[:, 2 * j0 + a:2 * j1:2], z[:, j0:j1], [[0, j1 - j0]], A.is_ge, 0.0, 0, 0),
+                   ("i", n), [ZK[h] for h in hs], ZZ[a * len(hs):(a + 1) * len(hs)])
+            turn([(pz[:, o + w * q:o + w * q + w, :, :], T.zz[:, 2 * j0 + 128 * q:2 * j0 + 128 * q + 128]) for q in range(n // 64)], ZZ, pzk)
+            if ZT == "D":
+                cp(T.zt[:, 2 * j0:2 * j1], pz[:, o:o + 2 * n // ZR, :, :], n, [], [pzk] + ZT_)
+            else:
+                act(T.zt[:, 2 * j0:2 * j1], pz[:, o:o + 2 * n // ZR, :, :], F.Identity, 2 * n, [], [pzk] + ZT_)
+            for q in [q for h in hs for q in ORDER[h]]:
+                turn([(zin(q, 1, r), T.zt[:, 128 * q:128 * q + 128]) for r in range(ZR // 2)], ["zt%d" % (q // 2)], zbank(q // 2))
+
+        for a, (c, n, eng) in enumerate(lines):
+            c, n = int(c), int(n)
+            o, gath = T.xg[:, 512 * c:512 * (c + n)], T.xw[:, 0:3072].indirect(T.e3[:, 32 * c:32 * (c + n)])
+            r = ["x0", "x1", "xd"] + ["e3%d" % q for q in range(c // 2, (c + n + 1) // 2)]
+            if tokens and t and a >= AFTER:
+                r += ["tok0", "tok1"]
+            if eng == "D":
+                cp(o, gath, 512 * n, r, XG[c:c + n], cost="g")
+            else:
+                act(o, gath, F.Identity, 512 * n, r, XG[c:c + n], cost="g")
+
         if not last:
-            send(T["z%d" % (t + 1)][:], zo[:], "rz%d" % (t + 1), 69632, ZO + ["zos%d" % t], ["z%d" % (t + 1)])
+            prepare(t + 1)
         else:
-            dma("act", T.yz[:], zo[:, 0:256], 65536, ZO, [])
-            for h in range(2):
-                lines_out(h)
-                for a, b in enumerate((3, 5)):
-                    pe([(ps[b][:, 0:256], T[n][:], T.xw[:, 512 * q + 256 * a:512 * q + 256 * a + 256], q == 0, q == 3, 256)
-                        for q, n in enumerate(("idb", "i64", "i4k", "i18")) if q // 2 == h], ["idb", "i64", "i4k", "i18", "x%d" % h], ["B%d" % b])
-            act(T.yxs[:, 0:256], ps[3][:, 0:256], F.Identity, 256, [], ["B3", "yx0"])
-            cp(T.yxs[:, 256:512], ps[5][:, 0:256], 256, [], ["B5", "yx1"])
+            pe([(ps[7][0:8, 0:256], T.i1k[:], vb[:, 0:256], True, False, 256)] +
+               [(ps[7][0:8, jl:256:16], T.lb[:, 128 * jl:128 * jl + 128:16], ph[:, 16:32], False, jl == 15, 16) for jl in range(16)],
+               LB + ["i1k", "vb%d" % t, pnk + "w"], ["B7"])
+            act(T.yv[0:8, :], ps[7][0:8, 0:256], F.Identity, 256, [], ["B7", "yv"])
+            dma("sp", T.yvp[:], T.yv[0:8, :], 8192, ["yv"], [])
+
+        for hs in TAILS[t]:
+            if tokens and hs[0] == tokens[0]:
+                early(t + 1)
+            tail(t, hs)
+            for d, y in enumerate((T.yvd, T.ypd)):
+                scatter(t, d, hs)
+                if last and hs[-1] == 1:
+                    dma("sp", y[:], (T.w3, T.w2)[d][:, 2048:3072], 524288, (["vd0", "vd1"], ["pd0", "pd1"])[d], [])
+            for part in WINS[t]:
+                if part[-1] in hs:
+                    winners(t, part)
+        if not last:
+            if not tokens:
+                early(t + 1)
+            so, sh, sok = T["so%d" % (t + 1)], T["sh%d" % (t + 1)], "so%d" % (t + 1)
+            advance(zo, ["zo%d_0" % t, "zo%d_1" % t], "bw2", ph[:, 16:32], pnk + "w", so, sh, sok, [hs[0] for hs in TAILS[t]])
+            if t + 2 < NV:
+                send2([(T["pl%d" % (t + 2)][:, 32:48], so[:, 16:32]), (T["vb%d" % (t + 2)][:, 272:288], sh[:, 16:32])], "rp%d" % (t + 2), 8192,
+                      [sok + "v", sok + "w"], ["pl%d" % (t + 2), "vl%d" % (t + 2)], 2)
+            send2([(T["pl%d" % (t + 1)][:, 0:32], so[:]), (T["ph%d" % (t + 1)][:], sh[:])], "ra%d" % (t + 1), 16384,
+                  [sok + k for k in "nvmw"], ["pn%d%s" % (t + 1, k) for k in "nvmw"], 1)
+        else:
+            dma("act", T.yz[:], zo[:], 65536, ["zo%d_0" % t, "zo%d_1" % t], [])
+            act(T.yxs[:, 0:256], ps[2][:, 0:256], F.Identity, 256, [], ["B2", "yx0"])
+            cp(T.yxs[:, 256:512], ps[3][:, 0:256], 256, [], ["B3", "yx1"])
             dma("sp", T.yx[:], T.yxs[:], 262144, ["yx0", "yx1"], [])
     return ops
 
@@ -504,40 +713,119 @@ def tables(ops, pred, m):
                      i=150 + 2 * n * m["cy"], d=60.0, r=1000.0)[c]
         eng.append(ENG.index(o["eng"]))
         hold.append(x)
-        lat.append(m["dma"] if c == "d" else m["far"] + n / 60.0 if c == "r" else x)
+        lat.append(m["dma"] if c == "d" else m["far"] + n / (12.0 * REMOTE_ENGINES) if c == "r" else x)
         wire.append(0.0 if c != "d" else n / m["rate"])
     return eng, hold, lat, wire, [[(j, m["hop"] if sem else 0.0) for j, sem in p.items()] for p in pred]
 
 
-def play(seq, tab, a=0, base=None):
-    eng, hold, lat, wire, inn = tab
-    free, last, w = [0.0] * 5, [-1] * 5, 0.0
-    if base is None:
-        done, why = [0.0] * len(seq), [None] * len(seq)
-    else:
-        done, why = base[1][:], base[2][:]
-        for i in seq[:a]:
+def chains(seq, tab, state, a, b):
+    eng, hold, full, wire, pre, suc = tab
+    r, q, why = state
+    last, w, seen = [-1] * 5, -1, 0
+    for k in range(a - 1, -1, -1):
+        i = seq[k]
+        if last[eng[i]] < 0:
             last[eng[i]] = i
-            if wire[i]:
-                w = done[i]
-        for e, i in enumerate(last):
-            if i >= 0:
-                free[e] = why[i][2]
+            seen += 1
+        if w < 0 and wire[i]:
+            w = i
+            seen += 1
+        if seen == 6:
+            break
     for i in seq[a:]:
         e = eng[i]
-        s, y, q = free[e], last[e], True
-        for j, h in inn[i]:
-            x = done[j] + h
+        p = last[e]
+        s, y, same = (r[p] + hold[p], p, True) if p >= 0 else (0.0, -1, True)
+        for j, x in pre[i]:
+            x += r[j]
             if x > s:
-                s, y, q = x, j, False
-        free[e] = x = s + hold[i]
-        last[e] = i
-        d = s + lat[i]
+                s, y, same = x, j, False
         if wire[i]:
-            d = w = (w if w > d else d) + wire[i]
-        done[i] = d
-        why[i] = (y, q, x)
-    return max(done), done, why
+            if w >= 0 and r[w] + wire[w] > s:
+                s, y, same = r[w] + wire[w], w, True
+            w = i
+        r[i] = s
+        why[i] = (y, same)
+        last[e] = i
+    nxt, w, seen = [-1.0] * 5, -1.0, 0
+    for i in seq[b + 1:]:
+        if nxt[eng[i]] < 0:
+            nxt[eng[i]] = q[i]
+            seen += 1
+        if w < 0 and wire[i]:
+            w = q[i]
+            seen += 1
+        if seen == 6:
+            break
+    for i in seq[b::-1]:
+        e = eng[i]
+        s = nxt[e] + hold[i]
+        if full[i] > s:
+            s = full[i]
+        for j, x in suc[i]:
+            x += q[j]
+            if x > s:
+                s = x
+        if wire[i]:
+            if w + wire[i] > s:
+                s = w + wire[i]
+            w = s
+        q[i] = nxt[e] = s
+
+
+def through(seq, mid, a, b, pos, tab, state):
+    eng, hold, full, wire, pre, suc = tab
+    r, q, why = state
+    free, w, used, wired = [0.0] * 5, 0.0, 0, False
+    for i in mid:
+        used |= 1 << eng[i]
+        if wire[i]:
+            wired = True
+    need, look = used, wired
+    for k in range(a - 1, -1, -1):
+        i = seq[k]
+        m = 1 << eng[i]
+        if need & m:
+            need ^= m
+            free[eng[i]] = r[i] + hold[i]
+        if look and wire[i]:
+            w, look = r[i] + wire[i], False
+        if not need and not look:
+            break
+    new, out = {}, 0.0
+    for i in mid:
+        e = eng[i]
+        s = free[e]
+        for j, x in pre[i]:
+            x += new[j] if j in new else r[j]
+            if x > s:
+                s = x
+        if wire[i]:
+            if w > s:
+                s = w
+            w = s + wire[i]
+        new[i] = s
+        free[e] = s + hold[i]
+        t = full[i]
+        for j, x in suc[i]:
+            if pos[j] > b and x + q[j] > t:
+                t = x + q[j]
+        if s + t > out:
+            out = s + t
+    for k in range(b + 1, len(seq)):
+        i = seq[k]
+        m = 1 << eng[i]
+        if used & m:
+            used ^= m
+            if free[eng[i]] + q[i] > out:
+                out = free[eng[i]] + q[i]
+        if wired and wire[i]:
+            wired = False
+            if w + q[i] > out:
+                out = w + q[i]
+        if not used and not wired:
+            break
+    return out
 
 
 def first_order(ops, pred, tab):
@@ -547,6 +835,9 @@ def first_order(ops, pred, tab):
     for i in range(n):
         for j, h in inn[i]:
             succ[j].append((i, h))
+    rest = [0.0] * n
+    for i in range(n - 1, -1, -1):
+        rest[i] = lat[i] + wire[i] + max([h + rest[j] for j, h in succ[i]], default=0.0)
     left = [len(p) for p in pred]
     ready, free, w = [0.0] * n, [0.0] * 5, 0.0
     cand = [[i for i in range(n) if not left[i] and eng[i] == e] for e in range(5)]
@@ -556,7 +847,7 @@ def first_order(ops, pred, tab):
         for e in range(5):
             if cand[e]:
                 t0 = max(free[e], min(ready[j] for j in cand[e]))
-                i = min(j for j in cand[e] if ready[j] <= t0 + 120.0)
+                i = max((j for j in cand[e] if ready[j] <= t0), key=lambda j: rest[j])
                 t0 = max(t0, ready[i])
                 if best is None or t0 < best[0]:
                     best = (t0, e, i)
@@ -576,30 +867,44 @@ def first_order(ops, pred, tab):
 
 
 def improve(seq, pred, tabs, tries, hot, cold, rng):
-    eng, n = tabs[0][0], len(seq)
-    succ = [[] for _ in range(n)]
-    for i, p in enumerate(pred):
-        for j in p:
-            succ[j].append(i)
-    res = [play(seq, t) for t in tabs]
-    cur = sum(r[0] for r in res)
-    best, paths = (cur, seq), None
+    n, seq, full = len(seq), list(seq), []
+    for eng, hold, lat, wire, inn in tabs:
+        pre = [[(j, lat[j] + wire[j] + h) for j, h in p] for p in inn]
+        suc = [[] for _ in range(n)]
+        for i in range(n):
+            for j, x in pre[i]:
+                suc[j].append((i, x))
+        full.append((eng, hold, [a + b for a, b in zip(lat, wire)], wire, pre, suc))
+    succ = [[j for j, _ in l] for l in full[0][5]]
+    ends = [i for i in range(n) if not succ[i]]
+    states = [([0.0] * n, [0.0] * n, [None] * n) for _ in tabs]
+    pos = [0] * n
+    best, fresh, a, b = (1e18, seq), True, 0, n - 1
     for k, r in enumerate(rng.random((tries, 5)).tolist()):
-        if paths is None:
-            pos = [0] * n
-            for a, i in enumerate(seq):
-                pos[i] = a
-            paths = []
-            for tot, done, why in res:
-                i, p = done.index(tot), []
+        if fresh:
+            for c in range(a, b + 1):
+                pos[seq[c]] = c
+            paths, tots, fresh = [], [], False
+            for t, s in zip(full, states):
+                chains(seq, t, s, a, b)
+                tot, i = max((s[0][i] + t[2][i], i) for i in ends)
+                p, why = [], s[2]
                 while i >= 0:
                     y = why[i][0]
                     if why[i][1] and y >= 0:
                         p.append((i, y))
                     i = y
                 paths.append(p)
+                tots.append(tot)
+            cur = sum(tots)
+            if cur < best[0]:
+                best = (cur, seq[:])
         p = paths[int(r[0] * len(paths))]
         i, y = p[int(r[1] * len(p))]
+        if k % FREE == 0:
+            b = 1 + int(r[1] * (n - 1))
+            i = seq[b]
+            y = next((seq[c] for c in range(b - 1, -1, -1) if eng[seq[c]] == eng[i]), i)
         a, b = pos[y], pos[i]
         more = int(-1.5 * math.log(1.0 - r[2]))
         if r[3] < 0.5:
@@ -613,7 +918,7 @@ def improve(seq, pred, tabs, tries, hot, cold, rng):
                     front.append(j)
                 else:
                     back.append(j)
-            new = seq[:a] + front[::-1] + back[::-1] + seq[b + 1:]
+            mid = front[::-1] + back[::-1]
         else:
             while more and b < n - 1:
                 b += 1
@@ -625,19 +930,13 @@ def improve(seq, pred, tabs, tries, hot, cold, rng):
                     back.append(j)
                 else:
                     front.append(j)
-            new = seq[:a] + front + back + seq[b + 1:]
+            mid = front + back
+        if mid == seq[a:b + 1]:
+            continue
         limit = cur - len(tabs) * hot * (cold / hot) ** (k / tries) * math.log(1.0 - r[4])
-        out, tot = [], 0.0
-        for t, old in zip(tabs, res):
-            out.append(play(new, t, a, old))
-            tot += out[-1][0]
-            if out[-1][0] > old[0] + 2500.0:
-                break
-        else:
-            if tot <= limit:
-                seq, res, cur, paths = new, out, tot, None
-                if cur < best[0]:
-                    best = (cur, seq)
+        if sum(max(through(seq, mid, a, b, pos, t, s), x - 1.0) for t, s, x in zip(full, states, tots)) <= limit:
+            seq[a:b + 1] = mid
+            fresh = True
     return best[1]
 
 

import math
import numpy as np
from concourse.bass import DstId, RemoteDMATransfer
from concourse.mybir import AluOpType as A, AxisListType, ActivationFunctionType as F

NV = 4
LOOK2 = ("0W", "1A", "2W", "3A")
LOOK3 = ("0A", "1W", "2A", "3W")
LINES = ("02A", "22A", "42A", "62A")
ORDER = ((0, 1), (2, 3))
ZT = "D"
HJ = "D"
FIRST = (1, 0, 0, 0)
BOTH, EACH = ([0, 1],), ([0], [1])
TAILS = (BOTH, BOTH, BOTH, EACH)
WINS = (BOTH, BOTH, BOTH, EACH)
TOKENS = (0, 1)
PN = "D"
TOKEN_ENG = "AA"
PICK = (2, 3)
ZSEND = 1
ZPARTS = (BOTH, BOTH, BOTH, BOTH)
AFTER = 9
HSPLIT = 2
MAXH = ((0, 0),) * 4
REPICK = (0, 0, 0, 0)
TWICE = (0, 0, 0)
NEAR = (6, 6, 6, 7)
ZR = 8
JOIN = 0
VBP = 0
PIECE = 1100
A2, SL = "AAAA", "AAAA"
TPARTS = BOTH
XSPLIT = 0
CONST = dict(dh="DDPP", ids="P", w3="P")
SH = 1536.0
TK = 3328
OVER = {0: (("0A", "1W", "2A", "3A"), LOOK3, LINES), 3: (LOOK2, LOOK3, ("02A", "22A", "42A", "61A", "71D"))}
BETA = 1.7
SEED = 2
FREE = 10 ** 9
REMOTE_ENGINES = 8
MODELS = [dict(cy=0.95, fix=45, g=1.56, s=3.8, pe=0.48, hop=90.0, far=3000.0, dma=1800.0, rate=300.0),
          dict(cy=0.95, fix=45, g=1.15, s=5.0, pe=0.53, hop=120.0, far=4000.0, dma=2200.0, rate=220.0),
          dict(cy=0.95, fix=45, g=1.95, s=2.5, pe=0.43, hop=70.0, far=2500.0, dma=1500.0, rate=350.0),
          dict(cy=0.8, fix=45, g=2.0, s=5.5, pe=0.4, hop=65.0, far=2300.0, dma=1300.0, rate=420.0)]
ROUNDS = ((1, 60000, 220.0, 30.0), (4, 65000, 60.0, 4.0), (4, 80000, 35.0, 3.0))

f32, bf, f16, i32, u16 = "float32", "bfloat16", "float16", "int32", "uint16"
SCRATCH = {}
for _n, _c, _d in [
    ("svd", 1024, i32), ("spd", 1024, i32), ("w2", 3584, f32), ("w3", 3584, f32), ("xw", 3072, bf),
    ("vpi", 32, i32), ("wti", 16, i32), ("z0", 256, bf), ("bw2", 144, bf),
    ("e1", 256, u16), ("e2", 256, u16), ("e3", 256, u16), ("hi", 256, bf),
    ("wd0", 1024, f16), ("wd1", 1024, f16), ("wd2", 1024, f16), ("wk0", 1024, f16), ("wk1", 1024, f16), ("wk2", 1024, f16), ("wk3", 1024, f16), ("wf", 6144, f32),
    ("xg", 4096, bf), ("ab", 4096, bf), ("pm", 256, f32), ("pn8", 16, f32), ("st", 272, bf), ("sg", 256, bf), ("acc", 8, f32),
    ("a2", 768, f32), ("sl", 512, bf), ("ku", 16, u16), ("xs", 256, bf), ("nl", 256, bf),
    ("mt", 2176, bf), ("vpf", 64, f32),
    ("ui", 24, i32), ("um", 24, i32), ("ri", 32, i32), ("i37", 128, bf),
    ("sq", 16, i32), ("sm", 16, i32),
    ("of", 32, f32), ("ou", 64, u16), ("abias", 8, f32),
    ("yv", 256, f32), ("yxs", 512, f32),
    ("pi", 8, i32), ("pj", 8, i32), ("col", 16, f32), ("row", 256, f32), ("m16", 16, f32), ("idb", 128, bf), ("idn", 128, bf),
    ("idq", 128, bf), ("ip2", 128, bf), ("in2", 128, bf), ("i64", 128, bf), ("i4k", 128, bf), ("i18", 128, bf),
    ("dh", 2048, bf), ("lb", 2048, bf), ("zr", 512, bf), ("bn", 144, bf), ("bw", 144, bf), ("blk", 128, f32), ("wb", 128, bf),
    ("sel", 80, bf), ("selz", 256, bf), ("zt", 512, bf), ("zz", 512, bf), ("idf", 128, f32), ("et", 768, f16),
    ("b8", 128, f32), ("par", 128, f32), ("pair", 64, f16), ("th2", 256, bf), ("oneh", 128, bf),
    ("half", 128, f32), ("kc", 256, f16), ("rst", 256, f32),
    ("mix", 16, u16), ("jl", 16, f32), ("dt", 32, f32), ("j8r", 32, f32), ("jc", 32, f16),
    ("m128", 256, bf), ("i1k", 8, bf), ("big", 256, f32), ("pw", 64, f32),
]:
    SCRATCH[_n] = ("sbuf", [128, _c], _d)
for _t in range(NV):
    SCRATCH["zo%d" % _t] = ("sbuf", [128, 256], bf)
    SCRATCH["vb%d" % _t] = ("sbuf", [128, 288], f16)
    SCRATCH["pb%d" % _t] = ("sbuf", [128, 288], f16)
    SCRATCH["pl%d" % _t] = ("sbuf", [128, 64], u16)
    SCRATCH["ph%d" % _t] = ("sbuf", [128, 32], f16)
    if _t:
        SCRATCH["z%d" % _t] = ("sbuf", [128, 256], bf)
        SCRATCH["so%d" % _t] = ("sbuf", [128, 32], u16)
        SCRATCH["sh%d" % _t] = ("sbuf", [128, 32], f16)
for _b in range(ZR // 4, 8):
    SCRATCH["ps%d" % _b] = ("psum", [128, 512], f32)
for _b in range(ZR // 4):
    SCRATCH["pz%d" % _b] = ("psum", [128, 1024 // ZR, ZR // 2, 2], bf)

ENG = ("pe", "dve", "act", "pool", "sp")
SEMAPHORES = ["q_" + e for e in ENG[:4]] + ["d%d" % i for i in range(24)] + ["sent", "rw"] + \
             ["r%s%d" % (k, t) for k in "apbyz" for t in range(1, NV)]


def build_ops(g, T, topo, core):
    ops = []
    V, S, P = g.vector, g.scalar, g.tensor
    ps = {b: T["ps%d" % b] for b in range(ZR // 4, 8)}
    ndma = [0]

    def op(eng, fn, cost, r, w, kind="c", sem=None):
        ops.append(dict(eng=eng, fn=fn, cost=cost, r=list(r), w=list(w), kind=kind, sem=sem))

    def ts(out, in0, s1, o0, n, r, w, s2=None, o1=None, cost="v"):
        if o1 is None:
            op("dve", lambda: V.tensor_scalar(out, in0, s1, None, o0), (cost, n), r, w)
        else:
            op("dve", lambda: V.tensor_scalar(out, in0, s1, s2, o0, o1), (cost, n), r, w)

    def tt(out, in0, in1, o, n, r, w, cost="v"):
        op("dve", lambda: V.tensor_tensor(out, in0, in1, o), (cost, n), r, w)

    def cp(out, in_, n, r, w, cost="v"):
        op("dve", lambda: V.tensor_copy(out, in_), (cost, n), r, w)

    def ms(out, val, n, w):
        op("dve", lambda: V.memset(out, val), ("v", n), [], w)

    def act(out, in_, func, n, r, w, cost="v", **kw):
        op("act", lambda: S.activation(out, in_, func, **kw), (cost, n), r, w)

    def many(eng, fns, n, r, w):
        def fn():
            last = None
            for f in fns:
                last = f()
            return last
        op(eng, fn, ("m", n), r, w)

    def pe(mms, r, w):
        if len(mms) > 1 and sum(m[5] for m in mms) > PIECE:
            pe(mms[:len(mms) // 2], r, w)
            pe(mms[len(mms) // 2:], r, w)
            return

        def fn():
            last = None
            for o, l, x, s0, s1, c in mms:
                last = P.matmul(o, l, x, s0, s1)
            return last
        op("pe", fn, ("p", sum(m[5] for m in mms)), r, w)

    def turn(pairs, r, bank):
        def fn():
            last = None
            for o, x in pairs:
                last = P.transpose(o, x, T.idb[:])
            return last
        op("pe", fn, ("p", 128 * len(pairs)), r + ["idb"], [bank])

    def iota(out, pattern, base, cm, n, w, flag=True):
        if flag:
            op("pool", lambda: g.iota(out, pattern, base, cm, allow_small_or_imprecise_dtypes=True), ("i", n), [], w)
        else:
            op("pool", lambda: g.iota(out, pattern, base, cm), ("i", n), [], w)

    def mark(out, pattern, base, val, n, w):
        op("pool", lambda: g.affine_select(out, T.zr[:, 0:n], pattern, A.not_equal, val, base, 1), ("i", n), ["zr"], w)

    def dma(eng, out, in_, nbytes, r, w):
        q = g.sync if eng == "sp" else g.scalar
        op(eng, lambda: q.dma_start(out, in_), ("d", nbytes), r, w, kind="dma", sem="d%d" % ndma[0])
        ndma[0] += 1

    def send(dst, src, sem, nbytes, r, w, ahead=1):
        to = T.cores[(T.rank_of(core) + ahead) % len(T.cores)]
        rid, pid, _ = topo.addr(to)
        mask = sum(1 << e for e in topo.engines(core, to)[:REMOTE_ENGINES])
        op("pool", lambda: g.remote_dma(dst, src, T.sem[sem], T.sem.sent, pid, rid, mask), ("r", nbytes), r, w, kind="send", sem=sem)

    def send2(pairs, sem, nbytes, r, w, ahead):
        to = T.cores[(T.rank_of(core) + ahead) % len(T.cores)]
        rid, pid, _ = topo.addr(to)
        some = topo.engines(core, to)[:REMOTE_ENGINES]
        moves = [RemoteDMATransfer(dst_ids=[DstId(rid=rid, pnc=pid)], dma_engine_mask=sum(1 << e for e in some[a::2]), remote_sem=T.sem[sem], src=x, dst=y)
                 for a, (y, x) in enumerate(pairs)]
        op("pool", lambda: g.remote_dma_fused(moves, local_sem=T.sem.sent), ("r", nbytes), r, w, kind="send", sem=sem)

    dma("sp", T.vpi[:, 0:16], T.vn[:], 8192, [], ["vpi0"])
    dma("act", T.vpi[:, 16:32], T.pn[:], 8192, [], ["vpi1"])
    dma("sp", T.svd[:], T.vdir[:], 524288, [], ["svd"])
    dma("sp", T.spd[:, 0:768], T.pdir[:, 0:768], 393216, [], ["spd0"])
    dma("sp", T.spd[:, 768:1024], T.pdir[:, 768:1024], 131072, [], ["spd1"])
    dma("act", T.wti[:, 0:1], T.wt[:], 512, [], ["wti0"])
    dma("act", T.wti[:, 8:9], T.th[:], 512, [], ["wti1"])
    dma("sp", T.z0[:], T.z[:], 65536, [], ["z0_0", "z0_1"])
    dma("sp", T.xw[:, 0:2048], T.xl[:], 524288, [], ["x0", "x1"])
    dma("sp", T.xw[:, 2048:3072], T.xl[:, 0:1024], 262144, [], ["xd"])

    col = lambda c: T.col[:, c:c + 1]
    iota(T.pi[:, 0:1], [[0, 1]], 0, 1, 1, ["pi"], flag=False)
    iota(T.row[:], [[1, 256]], 0, 0, 256, ["row"])
    iota(T.w2[:, 0:512], [[1, 512]], 0, 0, 512, ["w2a"])
    iota(T.blk[:], [[16, 8], [0, 16]], 0, 0, 128, ["blk"])
    iota(T.b8[:], [[0, 8], [1, 2], [0, 8]], 0, 0, 128, ["b8"])
    ms(T.zr[:], 0.0, 256, ["zr"])
    mark(T.idb[:], [[-1, 128]], 0, 1.0, 128, ["idb"])
    act(T.w2[:, 512:1024], T.w2[:, 0:512], F.Identity, 512, ["w2a"], ["w2b"], bias=512.0)
    act(T.w2[:, 1024:2048], T.w2[:, 0:1024], F.Identity, 1024, ["w2a", "w2b"], ["w2c"], bias=1024.0)
    act(T.big[:], T.zr[:, 0:256], F.Silu, 256 + 1400, ["zr"], ["big"], bias=65536.0)
    for a, k in enumerate("ab"):
        if CONST["w3"][a % len(CONST["w3"])] == "P":
            iota(T.w3[:, 1024 * a:1024 * a + 1024], [[1, 1024]], 1024 * a, 0, 1024, ["w3" + k])
        else:
            act(T.w3[:, 1024 * a:1024 * a + 1024], T.w2[:, 0:1024], F.Identity, 1024, ["w2a", "w2b"], ["w3" + k], bias=1024.0 * a)
    for c, bits in enumerate((15, 112, 1, 126)):
        ts(T.pj[:, c:c + 1], T.pi[:, 0:1], bits, A.bitwise_and, 1, ["pi"], ["pj%d" % c])
    cp(T.col[:, 0:4], T.pj[:, 0:4], 4, ["pj%d" % c for c in range(4)], ["c0"])
    ts(T.m16[:], T.row[:, 0:16], col(0), A.is_equal, 16, ["row", "c0"], ["m16"])
    cp(T.pl0[:, 32:64], T.vpi[:], 32, ["vpi0", "vpi1"], ["pl0"])
    cp(T.vb0[:, 272:288], T.vpi[:, 0:16], 16, ["vpi0"], ["vl0"])
    cp(T.pb0[:, 272:288], T.vpi[:, 16:32], 16, ["vpi1"], ["pq0"])
    cp(T.w2[:, 2048:2816], T.spd[:, 0:768], 768, ["spd0"], ["pd0"])
    cp(T.w2[:, 2816:3072], T.spd[:, 768:1024], 256, ["spd1"], ["pd1"])
    for a in range(2):
        cp(T.w3[:, 2048 + 512 * a:2560 + 512 * a], T.svd[:, 512 * a:512 * a + 512], 512, ["svd"], ["vd%d" % a])
    for a in range(4):
        if CONST["dh"][a % len(CONST["dh"])] == "P":
            mark(T.dh[:, 512 * a:512 * a + 512], [[128, 4], [-16, 8], [-129, 16]], 512 * a, 1.0, 512, ["dh%d" % a])
        else:
            many("dve", [(lambda k=k: V.tensor_scalar(T.dh[:, 128 * k:128 * k + 128], T.idb[:], T.m16[:, k:k + 1], None, A.mult))
                         for k in range(4 * a, 4 * a + 4)], [64] * 4, ["idb", "m16"], ["dh%d" % a])
    DH = ["dh%d" % a for a in range(4)]
    act(T.idf[:], T.idb[:], F.Identity, 128, ["idb"], ["idf"])
    ts(T.par[:], T.b8[:], col(2), A.is_equal, 128, ["b8", "c0"], ["par"])
    ts(T.pair[:], T.row[:, 0:128:2], col(3), A.is_equal, 64, ["row", "c0"], ["pair"])
    ts(col(5), col(1), 15.0, A.add, 1, ["c0"], ["c5"])
    ts(T.bn[:], T.row[:, 0:144], col(5), A.is_equal, 144, ["row", "c5"], ["bn"])
    ms(T.pw[:, 0:16], 1.0 / BETA, 16, ["pw0"])
    ms(T.pw[:, 16:32], 0.0, 16, ["pw1"])
    op("dve", lambda: V.tensor_tensor_scan(T.pw[:, 32:48], T.pw[:, 0:16], T.pw[:, 16:32], BETA ** 9, A.mult, A.add), ("v", 16), ["pw0", "pw1"], ["pw2"])
    tt(T.pw[:, 48:64], T.pw[:, 32:48], T.m16[:], A.mult, 32, ["pw2", "m16"], ["pw3"])
    op("dve", lambda: V.tensor_reduce(col(6), T.pw[:, 48:64], AxisListType.X, A.add), ("v", 16), ["pw3"], ["c6"])
    ts(T.wb[:], T.blk[:], col(1), A.is_equal, 128, ["blk", "c0", "c6"], ["wb"], col(6), A.mult)
    scale = [2.0 ** (97 - 13 * jh) for jh in range(16)]
    many("act", [(lambda jh=jh: S.activation(T.th2[:, 16 * jh:16 * jh + 16], T.m16[:], F.Identity, scale=-2.56 * scale[jh]))
                 for jh in range(16)], [16] * 16, ["m16"], ["th2"])
    cp(T.col[:, 7:9], T.wti[:, 0:9:8], 2, ["wti0", "wti1"], ["c7"])
    act(T.bw[:], T.bn[:], F.Identity, 144, ["bn", "c7"], ["bw"], scale=col(7))
    send(T.bw2[:], T.bw[:], "rw", 36864, ["bw"], ["bw2"], -1)
    for name, val in (("i37", 37.0 * 32), ("ip2", 2048.0), ("in2", -2048.0), ("idn", -1.0), ("idq", 0.5), ("i64", 64.0), ("i4k", 4096.0), ("i18", 262144.0)):
        if CONST["ids"] == "P":
            mark(T[name][:], [[-1, 128]], 0, val, 128, [name])
        else:
            act(T[name][:], T.idb[:], F.Identity, 128, ["idb"], [name], scale=val)
    for a in range(4):
        mark(T.lb[:, 512 * a:512 * a + 512], [[-1, 4], [-16, 8], [0, 16]], -4 * a, 1.0, 512, ["lb%d" % a])
    LB = ["lb%d" % a for a in range(4)]
    iota(T.w2[:, 3072:3584], [[1, 512]], 3072, 0, 512, ["w2t"])
    iota(T.w3[:, 3072:3584], [[1, 512]], 3072, 0, 512, ["w3t", "E0", "E1"])
    ts(T.selz[:, 128:256], T.blk[:], col(1), A.is_equal, 128, ["blk", "c0"], ["selz1"], -1.0, A.mult)
    act(T.selz[:, 0:128], T.selz[:, 128:256], F.Identity, 128, ["selz1"], ["selz0"], scale=16.0)
    ms(T.sel[:], 0.0, 40, ["sel"])
    many("act", [(lambda w=w, a=a: S.activation(T.sel[:, 40 * w + 16 * a + 8:40 * w + 16 * a + 16], T.selz[:, 128 * a:128 * a + 128:16], F.Identity,
                                                scale=(-2.0, 1.0)[w])) for w in range(2) for a in range(2)], [21] * 4, ["selz0", "selz1"], ["sel"])
    act(T.half[:], T.big[:, 0:128], F.Identity, 128, ["big"], ["half"], scale=8.0 / 65536)
    iota(T.oneh[:], [[0, 128]], 1, 0, 128, ["oneh"])
    ms(T.st[:, 7:8], 1.0, 1, ["stp"])
    act(col(11), T.m16[:, 0:1], F.Identity, 1, ["m16"], ["c11"], bias=1.0 - SH / 2048)
    act(col(10), T.m16[:, 0:1], F.Identity, 1, ["m16"], ["c10"], scale=2048.0, bias=-2048.0)
    act(col(9), col(8), F.Identity, 1, ["c7"], ["c9"], scale=-1.0, bias=0.5)
    ts(T.kc[:, 0:128], T.idb[:], col(0), A.mult, 64, ["idb", "c0"], ["kc0"])
    ts(T.kc[:, 128:256], T.idb[:], col(9), A.mult, 64, ["idb", "c9"], ["kc"])
    op("pool", lambda: g.affine_select(T.rst[:], T.big[:], [[0, 16], [1, 16]], A.is_equal, 0.0, 0, 0), ("i", 256), ["big"], ["rst"])
    cp(T.mix[:], T.row[:, 0:16], 16, ["row"], ["mix"])
    ts(T.jl[:], T.row[:, 0:16], 16.0, A.mult, 16, ["row", "c0"], ["jl"], col(0), A.add)
    for a in range(2):
        act(T.dt[:, 16 * a:16 * a + 16], T.jl[:], F.Identity, 16, ["jl"], ["dt%d" % a], bias=1024.0)
    act(T.j8r[:, 0:16], T.jl[:], F.Identity, 16, ["jl"], ["j8r"], scale=8.0)
    ms(T.j8r[:, 16:32], 0.0, 16, ["j8z"])
    ts(T.jc[:, 0:16], T.jl[:], 16.0, A.mult, 16, ["jl"], ["jc"], 16.0, A.add)
    ts(T.jc[:, 16:32], T.jl[:], 0.0, A.mult, 16, ["jl"], ["jc0"])
    iota(T.m128[:], [[0, 256]], -128, 0, 256, ["m128"])
    mark(T.i1k[:], [[-16, 8]], 0, 1024.0, 8, ["i1k"])
    ms(T.abias[:, 0:1], 0.0, 1, ["abias"])

    W2I, W3I = ["w2a", "w2b", "w2c"], ["w3a", "w3b"]
    ident = T.w2[:, 0:1024]
    IDK = ["w2a", "w2b"]
    XG = ["xg%d" % c for c in range(8)]
    rot = dict(wd=0, wf=0, wh=0, wv=0, bank=0, held=0)

    kept = {}

    SETS = 16 // ZR
    zbank = lambda h: "Bz%d" % (h * (ZR == 8))

    def zin(q, m, r=slice(None)):
        c = 64 * (q % 2 if ZR == 8 else q)
        return T["pz%d" % (q // 2 * (ZR == 8))][:, c:c + 64 * m, r, :]

    def bank():
        rot["bank"] += 1
        return PICK[rot["bank"] % len(PICK)]

    def look(t, lk, q, eng):
        win, wk = (T.w2, W2I + ["pd0", "pd1"]) if lk == 2 else (T.w3, W3I + ["vd0", "vd1"])
        if t and TOKENS:
            win, wk = win[:, 0:3584], wk + (["w2t"] if lk == 2 else ["w3t", "E0", "E1"])
        else:
            win = win[:, 0:3072]
        src, sk = (T.e1, "e1" if q else "e10") if lk == 2 else (T.e2, "e2%d" % q)
        dst, dk = (T.e2, "e2%d" % q) if lk == 2 else (T.e3, "e3%d" % q)
        defer, eng = eng.islower(), eng.upper()

        def land(b, c, n):
            if rot["held"]:
                b = rot["held"]
            return ps[b][:, 256 + 64 * (c % 2):256 + 64 * (c % 2 + n)], "B%d" % b, True

        def offsets(b, n):
            if defer:
                rot["held"] = b
                return
            if rot["held"]:
                b, n = rot["held"], 2
            rot["held"] = 0
            c = q - q % n
            got, key = ps[b][:, 256 + 64 * (c % 2):256 + 64 * (c % 2 + n)], "B%d" % b
            ts(dst[:, 64 * c:64 * (c + n)], got, SH, A.add, 64 * n, [], [key] + [dk[:2] + str(c + a) for a in range(n)])

        both = [sk, sk if lk == 2 and q > 1 else sk[:2] + str(q ^ 1) if lk == 3 else "e1"]
        if eng == "V":
            s = rot["wv"] % 2; rot["wv"] += 1
            o0 = 2048 * s
            ts(T.wv[:, o0:o0 + 2048], win.indirect(src[:, 64 * q:64 * q + 128]), -SH, A.add, 2048, wk + both, ["wv%d" % s], cost="g")
            b = bank()
            got, key, start = land(b, q, 2)
            for a in range(2):
                pe([(got, T.dh[:, 128 * k:128 * k + 128], T.wv[:, o0 + k:o0 + 2048:16], k == 0, k == 15, 128) for k in range(8 * a, 8 * a + 8)],
                   DH + ["wv%d" % s], [key])
            offsets(b, 2)
            return
        if eng in "HJG":
            s = rot["wh"] % 2
            o0 = 2048 + 2048 * s
            if eng == "G":
                act(T.wf[:, o0:o0 + 2048], win.indirect(src[:, 64 * q:64 * q + 128]), F.Identity, 2048, wk + both, ["wh%d0" % s, "wh%d1" % s], cost="g", bias=-SH)
            else:
                for a in range(HSPLIT):
                    n = 64 // HSPLIT
                    c = 64 * (q % 2) + n * a
                    act(T.wf[:, o0 + 16 * c:o0 + 16 * (c + n)], win.indirect(src[:, 64 * q + n * a:64 * q + n * a + n]), F.Identity, 16 * n, wk + [sk],
                        ["wh%d%d" % (s, q % 2) + "x" * a], cost="g", bias=-SH)
            if eng != "H":
                rot["wh"] += 1
                b = bank()
                for a in range(8):
                    pe([(ps[b][:, k:128:16], T.wf[:, o0 + k:o0 + 2048:16], T.idf[:, k:128:16], k == 0, k == 15, 256) for k in range(2 * a, 2 * a + 2)],
                       ["idf"] + ["wh%d%d" % (s, c) + "x" * x for c in range(2) for x in range(HSPLIT)], ["B%d" % b])
                got, key, start = land(b, q - q % 2, 2)
                if HJ == "D":
                    s = s if lk == 2 else 2 + q
                    et = T.et[:, 128 * s:128 * s + 128]
                    cp(et, ps[b][:, 0:128], 128, [], ["B%d" % b, "et%d" % s])
                    pe([(got, et, T.idb[:], start, True, 128)], ["et%d" % s, "idb"], [key])
                    if lk == 3:
                        kept[q - q % 2] = (2, [(et, T.idb[:])], ["et%d" % s, "idb"])
                else:
                    et = T.ew[:, 128 * s:128 * s + 128]
                    act(et, ps[b][:, 0:128], F.Identity, 128, [], ["B%d" % b, "ew%d" % s])
                    pe([(got, et, T.idf[:], start, True, 512)], ["ew%d" % s, "idf"], [key])
                offsets(b, 2)
            return
        if eng == "A":
            s = rot["wf"] % 2; rot["wf"] += 1
            c = s if lk == 2 else 2 + q
            o0, b, et = 1024 * s, bank(), T.et[:, 128 * c:128 * c + 128]
            m = HSPLIT if lk == 2 and t else 1
            for a in range(m):
                act(T.wf[:, o0 + 1024 // m * a:o0 + 1024 // m * (a + 1)], win.indirect(src[:, 64 * q + 64 // m * a:64 * q + 64 // m * (a + 1)]), F.Identity,
                    1024 // m, wk + [sk], ["wf%d%d" % (s, x) for x in range(HSPLIT) if m == 1 or x == a], cost="g", bias=-SH)
            for a in range(4):
                pe([(ps[b][:, k:128:8], T.wf[:, o0 + k:o0 + 1024:8], T.idf[:, k:128:8], k == 0, k == 7, 256) for k in range(2 * a, 2 * a + 2)],
                   ["idf"] + ["wf%d%d" % (s, x) for x in range(HSPLIT)], ["B%d" % b])
            tt(et, ps[b][:, 0:128], T.par[:], A.mult, 128, ["par"], ["B%d" % b, "et%d" % c])
            got, key, start = land(b, q, 1)
            pe([(got, et, T.pair[:], start, True, 64)], ["et%d" % c, "pair"], [key])
            if lk == 3:
                kept[q] = (1, [(et, T.pair[:])], ["et%d" % c, "pair"])
            offsets(b, 1)
            return
        name = "wd%d" % (rot["wd"] % 3) if lk == 2 else "wk%d" % q
        rot["wd"] += lk == 2
        if lk == 3:
            kept[q] = (1, [(T.dh[:, 128 * k:128 * k + 128], T[name][:, k:1024:16]) for k in range(16)], DH + [name + "a", name + "b"])
        if eng != "D":
            ts(T[name][:], win.indirect(src[:, 64 * q:64 * q + 64]), -SH, A.add, 1024, wk + [sk], [name + "a", name + "b"], cost="g")
        for a in range(2 * (eng == "D")):
            ts(T[name][:, 512 * a:512 * a + 512], win.indirect(src[:, 64 * q + 32 * a:64 * q + 32 * a + 32]), -SH, A.add, 512,
               wk + [sk], [name + "ab"[a]], cost="g")
        b = rot["held"] or bank()
        got, key, start = land(b, q, 1)
        pe([(got, T.dh[:, 128 * k:128 * k + 128], T[name][:, k:1024:16], k == 0 and start, k == 15, 64) for k in range(16)],
           DH + [name + "a", name + "b"], [key])
        offsets(b, 1)

    def early(t):
        pl, plk = T["pl%d" % t], "pl%d" % t
        win, wk = (T.w3[:, 2048:3072], ["vd0", "vd1"]) if t else (T.svd[:, 0:1024], ["svd"])
        if FIRST[t]:
            cp(T.e1[:, 0:64], win.indirect(pl[:, 32:36]), 64, wk + [plk], ["e10"], cost="g")
            cp(T.e1[:, 64:256], win.indirect(pl[:, 36:48]), 192, wk + [plk], ["e1"], cost="g")
        else:
            cp(T.e1[:], win.indirect(pl[:, 32:48]), 256, wk + [plk], ["e10", "e1"], cost="g")
        for q, eng in OVER.get(t, (LOOK2,))[0]:
            look(t, 2, int(q), eng)

    def repeats(src, skey, c0, vfk, half):
        off, first = 0, True
        for grp in ((0, 1), (2, 3, 4), (5, 6, 7), (8, 9, 10, 11), (12, 13, 14, 15)):
            fns, mms, n = [], [], []
            if first:
                mms.append((ps[7][:, 0:256], T.wb[:], T.th2[:], True, False, 256))
                first = False
            for jh in grp:
                wd = 256 - 16 * jh
                m = T.mt[:, off:off + wd]
                fns.append(lambda jh=jh, m=m: V.tensor_scalar(m, src[:, 16 * jh:256], T.vpf[:, c0 + jh:c0 + jh + 1], scale[jh], A.is_equal, A.mult))
                mms.append((ps[7][:, 16 * jh:256], T.wb[:], m, False, jh == 15, max(64, wd)))
                n.append(wd // 2)
                off += wd
            many("dve", fns, n, [skey, vfk], ["mt%d" % grp[0]])
            pe(mms, ["mt%d" % grp[0], "wb", "th2"], ["B7"])
        act(T.sl[:, 256 * half:256 * half + 256], ps[7][:, 0:256], F.Sign, 256, [], ["B7"] + (["fl"] if half else ["sl0", "sl1"]))

    def to_list(b, j0, j1, keys, start):
        pe(start + [(ps[b][:, 0:(j1 - j0) // 16], T.bn[:, 15 - jl:143 - jl], T.sl[:, j0 + jl:j1:16], jl == 0 and not start, jl == 15, 64) for jl in range(16)],
           ["idb", "jc", "jc0"] * bool(start) + ["bn"] + keys, ["B%d" % b])

    def marks(dst, c0, key, b=7):
        ts(dst[:, 256:272], ps[b][:, c0:c0 + 16], 128.0, A.mult, 16, [], ["B%d" % b, key], 2048.0, A.add)

    def prepare(t):
        pl, plk, f0, vfk = T["pl%d" % t], "pl%d" % t, 32 * (t % 2), "vpf%d" % (t % 2)
        vb, vbk, vmk = T["vb%d" % t], "vb%d" % t, "vm%d" % t
        if t and VBP:
            cp(T.vpf[:, f0:f0 + 16], pl[:, 32:48], 16, [plk], [vfk])
            pe([(ps[7][:, jl:256:16], T.lb[:, 128 * jl:128 * jl + 128], vb[:, 272:288], jl == 0, jl == 15, 64) for jl in range(16)], LB + ["vl%d" % t], ["B7"])
            cp(vb[:, 0:256], ps[7][:, 0:256], 256, [], ["B7", vbk])
        else:
            cp(T.vpf[:, f0:f0 + 32 - 16 * bool(t)], pl[:, 32:64 - 16 * bool(t)], 32, [plk], [vfk])
            cp(vb[:, 0:256], ident.indirect(pl[:, 32:48]), 256, IDK + [plk], [vbk], cost="g")
        repeats(vb, vbk, f0, vfk, 1)
        if t and JOIN:
            return
        if t:
            to_list(7, 256, 512, ["fl"], [])
            marks(vb, 0, vmk)
        else:
            cp(T.pb0[:, 0:256], ident.indirect(pl[:, 48:64]), 256, IDK + [plk], ["pb0"], cost="g")
            repeats(T.pb0, "pb0", 16, vfk, 0)
            to_list(7, 0, 512, ["sl0", "sl1", "fl"], [])
            marks(T.pb0, 0, "pm_0")
            marks(vb, 16, vmk)
        hand_on(t)

    def hand_on(t):
        if t < NV - 1:
            send(T["pb%d" % (t + 1)][:], T["vb%d" % t][:], "rb%d" % (t + 1), 73728, [k + str(t) for k in ("vb", "vm", "vl")],
                 [k + str(t + 1) for k in ("pb", "pm_", "pq")])

    def advance(z, zk, bw, v, vk, dst, dsh, dk, signs):
        n = 16 + bool(signs)
        pe([(ps[6][:, 32:48], T.i37[:], v, True, False, 64)] +
           [(ps[6][:, 16:17], T.half[:], T.acc[:, h:h + 1], False, False, 256) for h in signs] +
           [(ps[6][:, 0:16], T[bw][:, 15 - jl:143 - jl], z[:, jl:256:16], False, jl == 15, 64) for jl in range(16)],
           [bw, "i37", vk, "half"] + zk + ["acc%d" % h for h in signs], ["B6"])
        cp(T.ui[:, 0:n], ps[6][:, 0:n], n, [], ["B6", "ui"])
        ts(T.um[:, 0:n], T.ui[:, 0:n], 4095, A.bitwise_and, n, ["ui"], ["um"])
        tt(T.sq[:], T.um[:, 0:16], T.um[:, 0:16], A.mult, 32, ["um"], ["sq"])
        if signs:
            ts(T.abias[:, 0:1], T.um[:, 16:17], -1.0 / 16, A.mult, 1, ["um"], ["abias"])
        tt(T.sm[:], T.sq[:], ps[6][:, 32:48], A.add, 16, ["sq"], ["B6", "sm"])
        ts(T.ri[:, 16:32], T.sm[:], 5, A.logical_shift_right, 16, ["sm"], ["vi"], 1023, A.bitwise_and)
        ts(T.ri[:, 0:16], T.ui[:, 0:16], 7, A.bitwise_and, 16, ["ui"], ["ri"])
        tt(dsh[:], T.ri[:], T.j8r[:], A.add, 64, ["ri", "vi", "j8r", "j8z"], [dk + "m", dk + "w"])
        cp(dst[:, 0:32], dsh[:], 16, [dk + "w", dk + "m"], [dk + "n", dk + "v"])

    def winners(t, hs):
        zo = T["zo%d" % t]
        c0, c1, j0, j1 = 8 * hs[0], 8 * hs[-1] + 8, 128 * hs[0], 128 * hs[-1] + 128
        n, z = j1 - j0, T["z%d" % t][:, j0:j1]
        more = JOIN and t < NV - 1 and hs[-1] == 1
        c2 = 32 if more else c1
        b = NEAR[t] if hs[-1] == 1 else 6
        to_list(b, j0, 16 * c2, ["sl%d" % h for h in hs] + ["fl"] * more, [(ps[b][:, 0:c2 - c0], T.idb[:], T.jc[:, 0:c2 - c0], True, False, 64)])
        KU, XS, NL, ZO, Z = ([k + str(h) for h in hs] for k in ("ku", "xs", "nl", "zo%d_" % t, "z%d_" % t))
        cp(T.ku[:, c0:c1], ps[b][:, 0:c1 - c0], 16, [], ["B%d" % b] + KU)
        if more:
            marks(T["vb%d" % (t + 1)], 16, "vm%d" % (t + 1), 6)
            hand_on(t + 1)
        act(T.xs[:, j0:j1], T.xg[:, 16 * j0:16 * j1].indirect(T.ku[:, c0:c1]), F.Identity, n, KU + XG[c0 // 2:c1 // 2], XS, cost="g")
        pe([(ps[6][:, 0:n], T.idb[:], T.xs[:, j0:j1], True, False, n), (ps[6][:, 0:n], T.idn[:], z, False, False, n),
            (ps[6][:, 256:256 + n], T.idq[:], T.xs[:, j0:j1], False, False, n), (ps[6][:, 256:256 + n], T.idq[:], z, False, True, n)],
           XS + Z + ["idb", "idn", "idq"], ["B6"])
        act(zo[:, j0:j1], ps[6][:, 0:n], F.Abs, n, [], ["B6"] + ZO)
        if t < NV - 1 and ZSEND == 2:
            send(T["z%d" % (t + 1)][:, j0:j1], zo[:, j0:j1], "r%s%d" % ("yz"[hs[-1]], t + 1), 256 * n, ZO, ["z%d_%d" % (t + 1, h) for h in hs])
        elif t < NV - 1 and hs[-1] == 1:
            send(T["z%d" % (t + 1)][:], zo[:], "rz%d" % (t + 1), 65536, ["zo%d_0" % t, "zo%d_1" % t], ["z%d_0" % (t + 1), "z%d_1" % (t + 1)])
        act(T.nl[:, j0:j1], ps[6][:, 256:256 + n], F.Identity, n, [], ["B6"] + NL, bias=127.75)
        for part in [[h] for h in hs] if XSPLIT else [hs]:
            a, b = 128 * part[0], 128 * part[-1] + 128
            tt(T.xw[:, 0:8 * b].indirect(T["pl%d" % t][:, a // 16:b // 16]), T.nl[:, a:b], T.m128[:, 0:b - a], A.add, b - a,
               ["pn%dn" % t, "m128"] + ["nl%d" % h for h in part], ["x0", "x1"][:b // 128], cost="s")
            if t < NV - 1 and part[0] == 0:
                if TWICE[t]:
                    tt(T.xw[:, 2048:3072].indirect(T["pl%d" % t][:, 0:8]), T.nl[:, 0:128], T.m128[:, 0:128], A.add, 128, ["pn%dn" % t, "m128", "nl0"], ["xd"], cost="s")
                else:
                    dma("sp", T.xw[:, 2048:3072], T.xw[:, 0:1024], 262144, ["x0"], ["xd"])
            if t == NV - 1:
                for a, b in enumerate((2, 3)):
                    pe([(ps[b][:, 0:256], T[n][:], T.xw[:, 512 * q + 256 * a:512 * q + 256 * a + 256], q == 0, q == 3, 256)
                        for q, n in enumerate(("idb", "i64", "i4k", "i18")) if q // 2 in part], ["idb", "i64", "i4k", "i18"] + ["x%d" % h for h in part], ["B%d" % b])

    def scatter(t, d, hs, token=False):
        j0, n = 128 * hs[0], 128 * len(hs)
        o0 = 32 * (t % 2) + 16 * d + 8 * hs[0]
        out, keys = (T.w3, T.w2)[d][:, 2048:TK].indirect(T.ou[:, o0:o0 + n // 16]), (["vd0", "vd1"], ["pd0", "pd1"])[d]
        r = ["ou%d" % (t % 2), "w2t", "w3t"]
        if not token:
            a0 = 256 + 2 * j0 + n * d
            tt(out, T.w3[:, TK + j0:TK + j0 + n], T.a2[:, a0:a0 + n], A.max, n, r + [k + str(h) for k in ("E", "fp") for h in hs], keys, cost="s")
        elif TOKEN_ENG[d] == "A":
            act(out, T.w2[:, TK + j0:TK + j0 + n], F.Silu, n, r, keys + ["tok%d" % d], cost="s")
        else:
            cp(out, T.w2[:, TK + j0:TK + j0 + n], n, r, keys + ["tok%d" % d], cost="s")

    def tail(t, hs):
        z, vb, pb = (T["%s%d" % (n, t)] for n in ("z", "vb", "pb"))
        j0, j1, n = 128 * hs[0], 128 * hs[-1] + 128, 128 * len(hs)
        pk, K = ps[4], lambda *names: [k + str(h) for k in names for h in hs]
        pe([(pk[:, 256 * a + 128 * h:256 * a + 128 * h + 128], T.oneh[:], T.kc[:, 128 * a:128 * a + 128], a == 0 and h == 0, False, 128)
            for h in range(2) for a in range(2)], ["oneh", "kc0", "kc"], ["B4"])
        for h in hs:
            xk = lambda k: T.xg[:, 2048 * h + k:2048 * h + 2048:16]
            abk = lambda k: T.ab[:, 2048 * h + 128 * ZR * (k % SETS) + k // SETS:2048 * h + 128 * ZR * (k % SETS + 1):ZR]
            pe([(pk[:, 256 + 128 * h:384 + 128 * h], z[:, 128 * h:128 * h + 128], T.selz[:, 128:256], False, False, 128)], ["selz1", "z%d_%d" % (t, h)], ["B4"])
            for q, m in [(2 * h, 2)] if MAXH[t][h] else [(q, 1) for q in ORDER[h]]:
                for par in range(SETS):
                    a0 = 2048 * h + 128 * ZR * par + 64 * ZR * (q % 2)
                    tt(T.ab[:, a0:a0 + 64 * ZR * m], T.xg[:, 1024 * q + par:1024 * (q + m):SETS], zin(q, m), A.max, 32 * ZR * m,
                       XG[2 * q:2 * (q + m)], [zbank(h)] + ["ab%d%d" % (q + a, par) for a in range(m)])
            for a in range(2):
                pe([(pk[:, k:512:16], xk(k), T.sel[:, 48 - 8 * h:80 - 8 * h], False, False, 64) for k in range(8 * a, 8 * a + 8)], ["sel"] + XG[4 * h:4 * h + 4], ["B4"])
            for par in range(SETS):
                pe([(pk[:, k:512:16], abk(k), T.sel[:, 8 - 8 * h:40 - 8 * h], False, k == 15 and h == hs[-1], 64) for k in range(par, 16, SETS)],
                   ["sel"] + ["ab%d%d" % (2 * h + a, par) for a in range(2)], ["B4"])
        if hs[0] == 0:
            ts(T.hi[:], T.e3[:], 2048.0, A.is_lt, 128, ["e30", "e31", "e32", "e33", "c11"], ["hi"], col(11), A.subtract)
            if not REPICK[t]:
                ts(T.et[:, 256:512], T.e3[:], -SH, A.add, 128, ["e30", "e31", "e32", "e33"], ["et2", "et3"])
                for h in range(2):
                    kept[2 * h] = (2, [(T.idb[:], T.et[:, 256 + 128 * h:384 + 128 * h])], ["idb", "et%d" % (2 + h)])
                    kept.pop(2 * h + 1, None)
        for a in range(2):
            pe([(ps[5][:, 256 + jl:256 + n:16], T.lb[:, 128 * jl:128 * jl + 128], T["ph%d" % t][:, j0 // 16:j1 // 16], jl == 0, False, 64)
                for jl in range(8 * a, 8 * a + 8)], LB + ["pn%dm" % t], ["B5"])
        for q, (m, pairs, keys) in kept.items():
            if q // 2 in hs:
                pe([(ps[5][:, 64 * q - j0:64 * (q + m) - j0], l, x, False, False, 64 * m) for l, x in pairs], keys, ["B5"])
        pe([(ps[5][:, 0:n], T.ip2[:], T.hi[:, j0:j1], False, False, n)], ["ip2", "hi"], ["B5"])
        pm, least = T.pm[:, j0:j1], T.pn8[:, j0 // 16:j1 // 16]
        op("dve", lambda: V.tensor_tensor_scan(pm, T.rst[:, 0:n], pk[:, j0:j1], 0.0, A.add, A.min), ("v", n), ["rst"], ["B4"] + K("pm"))
        act(T.sg[:, j0:j1], pk[:, 256 + j0:256 + j1], F.Sign, n + 22, ["abias"], ["B4", "acc%d" % hs[0]] + K("sg"), bias=T.abias[:, 0:1],
            accum_out=T.acc[:, hs[0]:hs[0] + 1])
        if PN == "D":
            cp(least, T.pm[:, j0 + 15:j1:16], 16, K("pm"), K("pn"))
        else:
            act(least, T.pm[:, j0 + 15:j1:16], F.Identity, 16, K("pm"), K("pn"))
        tt(T.st[:, 8 + j0:8 + j1], least.indirect(T.mix[:, 0:n // 16]), pm, A.is_equal, n, K("pm", "pn") + ["mix"], K("st"), cost="g")
        pe([(pk[:, 0:n], T.idb[:], pb[:, j0:j1], True, False, n), (pk[:, n:2 * n], T.idb[:], vb[:, j0:j1], False, False, n)],
           ["idb", "pb%d" % t, "vb%d" % t], ["B4"])
        pe([(pk[:, n * a + 128 * h - j0:n * a + 128 * h - j0 + 128], T.sg[:, 128 * h:128 * h + 128], (T.ip2, T.in2)[a][:], False, a == 1 and h == hs[-1], 128)
            for h in hs for a in range(2)], K("sg") + ["ip2", "in2"], ["B4"])
        act(T.a2[:, 256 + 2 * j0:256 + 2 * j1], pk[:, 0:2 * n], F.Identity, 2 * n, [], ["B4"] + K("fp"))
        sT = lambda h, back=0: T.st[:, 8 + 128 * h - back:136 + 128 * h - back]
        pe([(ps[5][:, c + 128 * h - j0:c + 128 * h - j0 + 128], sT(h, back), (T.ip2, T.in2)[(c == 0) ^ back][:], False, c == 0 and back == 1 and h == hs[-1], 128)
            for c in (256, 0) for h in hs for back in range(2)], K("st") + ["st0", "stp", "ip2", "in2"], ["B5"])
        if A2[t] == "A":
            act(T.a2[:, j0:j1], ps[5][:, 256:256 + n], F.Identity, n, ["c10"], ["B5"] + K("a2"), bias=col(10))
        else:
            ts(T.a2[:, j0:j1], ps[5][:, 256:256 + n], col(10), A.add, n, ["c10"], ["B5"] + K("a2"))
        tt(T.w3[:, TK + j0:TK + j1], ps[5][:, 0:n], T.a2[:, j0:j1], A.max, n, K("a2"), ["B5"] + K("E"))
        b = NEAR[t] if hs[-1] == 1 else 6
        pe([(ps[b][:, 128 * h - j0:128 * h - j0 + 128], sT(h), T.idn[:], h == hs[0], h == hs[-1], 128) for h in hs], K("st") + ["idn"], ["B%d" % b])
        if SL[t] == "A":
            act(T.sl[:, j0:j1], ps[b][:, 0:n], F.Identity, n, [], ["B%d" % b] + K("sl"))
        else:
            cp(T.sl[:, j0:j1], ps[b][:, 0:n], n, [], ["B%d" % b] + K("sl"))

    for t in range(NV):
        z, zo, pl, ph, vb, pb = (T["%s%d" % (n, t)] for n in ("z", "zo", "pl", "ph", "vb", "pb"))
        kept.clear()
        ZK, plk, pnk = ["z%d_0" % t, "z%d_1" % t], "pl%d" % t, "pn%d" % t
        last = t == NV - 1
        look2, look3, lines = OVER.get(t, (LOOK2, LOOK3, LINES))
        f0, vfk = 32 * (t % 2), "vpf%d" % (t % 2)

        tokens = [] if last else list(TOKENS)
        if t == 0:
            early(0)
            advance(z, ZK, "bw", vb[:, 272:288], "vl0", pl, ph, pnk, [])
            send2([(T.pl1[:, 32:48], pl[:, 16:32]), (T.vb1[:, 272:288], ph[:, 16:32])], "rp1", 8192, [pnk + "v", pnk + "w"], ["pl1", "vl1"], 1)
            prepare(0)
        pe([(ps[7][:, 16 * a:16 * a + 16], T.idb[:], m[:, 272:288], a == 0, False, 64) for a, m in enumerate((vb, pb))] +
           [(ps[7][:, 16 * a:16 * a + 16], T.idb[:], m[:, 256:272], False, a == 1 and m is pb, 64) for m in (vb, pb) for a in range(2)],
           ["idb", "vl%d" % t, "pq%d" % t, "vm%d" % t, "pm_%d" % t], ["B7"])
        tt(T.of[:], ps[7][:, 0:32], T.dt[:], A.min, 32, ["dt0", "dt1"], ["B7", "of"])
        cp(T.ou[:, f0:f0 + 32], T.of[:], 32, ["of"], ["ou%d" % (t % 2)])
        for hs in TPARTS if tokens else ():
            scatter(t, 1, hs, True)
        for q, eng in look3:
            look(t, 3, int(q), eng)
        for hs in TPARTS if tokens else ():
            scatter(t, 0, hs, True)

        for hs in ZPARTS[t]:
            j0, j1, pz, pzk = 128 * hs[0], 128 * hs[-1] + 128, T["pz%d" % (hs[0] * (ZR == 8))], zbank(hs[0])
            w, o = 128 // ZR, 128 * hs[0] * (ZR == 4)
            n = j1 - j0
            ZZ, ZT_ = ["zz%d%d" % (h, a) for a in range(2) for h in hs], ["zt%d" % h for h in hs]
            for a in range(2):
                op("pool", lambda a=a, z=z, j0=j0, j1=j1: g.affine_select(T.zz[:, 2 * j0 + a:2 * j1:2], z[:, j0:j1], [[0, j1 - j0]], A.is_ge, 0.0, 0, 0),
                   ("i", n), [ZK[h] for h in hs], ZZ[a * len(hs):(a + 1) * len(hs)])
            turn([(pz[:, o + w * q:o + w * q + w, :, :], T.zz[:, 2 * j0 + 128 * q:2 * j0 + 128 * q + 128]) for q in range(n // 64)], ZZ, pzk)
            if ZT == "D":
                cp(T.zt[:, 2 * j0:2 * j1], pz[:, o:o + 2 * n // ZR, :, :], n, [], [pzk] + ZT_)
            else:
                act(T.zt[:, 2 * j0:2 * j1], pz[:, o:o + 2 * n // ZR, :, :], F.Identity, 2 * n, [], [pzk] + ZT_)
            for q in [q for h in hs for q in ORDER[h]]:
                turn([(zin(q, 1, r), T.zt[:, 128 * q:128 * q + 128]) for r in range(ZR // 2)], ["zt%d" % (q // 2)], zbank(q // 2))

        for a, (c, n, eng) in enumerate(lines):
            c, n = int(c), int(n)
            o, gath = T.xg[:, 512 * c:512 * (c + n)], T.xw[:, 0:3072].indirect(T.e3[:, 32 * c:32 * (c + n)])
            r = ["x0", "x1", "xd"] + ["e3%d" % q for q in range(c // 2, (c + n + 1) // 2)]
            if tokens and t and a >= AFTER:
                r += ["tok0", "tok1"]
            if eng == "D":
                cp(o, gath, 512 * n, r, XG[c:c + n], cost="g")
            else:
                act(o, gath, F.Identity, 512 * n, r, XG[c:c + n], cost="g")

        if not last:
            prepare(t + 1)
        else:
            pe([(ps[7][0:8, 0:256], T.i1k[:], vb[:, 0:256], True, False, 256)] +
               [(ps[7][0:8, jl:256:16], T.lb[:, 128 * jl:128 * jl + 128:16], ph[:, 16:32], False, jl == 15, 16) for jl in range(16)],
               LB + ["i1k", "vb%d" % t, pnk + "w"], ["B7"])
            act(T.yv[0:8, :], ps[7][0:8, 0:256], F.Identity, 256, [], ["B7", "yv"])
            dma("sp", T.yvp[:], T.yv[0:8, :], 8192, ["yv"], [])

        for hs in TAILS[t]:
            if tokens and hs[0] == tokens[0]:
                early(t + 1)
            tail(t, hs)
            for d, y in enumerate((T.yvd, T.ypd)):
                scatter(t, d, hs)
                if last and hs[-1] == 1:
                    dma("sp", y[:], (T.w3, T.w2)[d][:, 2048:3072], 524288, (["vd0", "vd1"], ["pd0", "pd1"])[d], [])
            for part in WINS[t]:
                if part[-1] in hs:
                    winners(t, part)
        if not last:
            if not tokens:
                early(t + 1)
            so, sh, sok = T["so%d" % (t + 1)], T["sh%d" % (t + 1)], "so%d" % (t + 1)
            advance(zo, ["zo%d_0" % t, "zo%d_1" % t], "bw2", ph[:, 16:32], pnk + "w", so, sh, sok, [hs[0] for hs in TAILS[t]])
            if t + 2 < NV:
                send2([(T["pl%d" % (t + 2)][:, 32:48], so[:, 16:32]), (T["vb%d" % (t + 2)][:, 272:288], sh[:, 16:32])], "rp%d" % (t + 2), 8192,
                      [sok + "v", sok + "w"], ["pl%d" % (t + 2), "vl%d" % (t + 2)], 2)
            send2([(T["pl%d" % (t + 1)][:, 0:32], so[:]), (T["ph%d" % (t + 1)][:], sh[:])], "ra%d" % (t + 1), 16384,
                  [sok + k for k in "nvmw"], ["pn%d%s" % (t + 1, k) for k in "nvmw"], 1)
        else:
            dma("act", T.yz[:], zo[:], 65536, ["zo%d_0" % t, "zo%d_1" % t], [])
            act(T.yxs[:, 0:256], ps[2][:, 0:256], F.Identity, 256, [], ["B2", "yx0"])
            cp(T.yxs[:, 256:512], ps[3][:, 0:256], 256, [], ["B3", "yx1"])
            dma("sp", T.yx[:], T.yxs[:], 262144, ["yx0", "yx1"], [])
    return ops


def depends(ops):
    writer, readers, pred = {}, {}, []
    for i, o in enumerate(ops):
        d = {}
        for k in o["r"] + o["w"]:
            if k in writer:
                j = writer[k]
                d[j] = d.get(j, False) or ops[j]["eng"] != o["eng"] or (o["eng"] != "pe" and k[0] != "B")
        for k in o["w"]:
            for j in readers.get(k, ()):
                d[j] = d.get(j, False) or ops[j]["eng"] != "pe" or o["eng"] != "pe"
        d.pop(i, None)
        for k in o["r"]:
            readers.setdefault(k, []).append(i)
        for k in o["w"]:
            writer[k] = i
            readers[k] = []
        pred.append(d)
    return pred


def tables(ops, pred, m):
    eng, hold, lat, wire = [], [], [], []
    for o in ops:
        c, n = o["cost"]
        fix = m["fix"] * (1.3 if o["eng"] == "act" else 1.0)
        if c == "m":
            x = sum(max(64, fix + a) for a in n) * m["cy"]
        else:
            x = dict(v=max(64, fix + n) * m["cy"], g=(1.3 * fix + n * m["g"]) * m["cy"], s=(1.3 * fix + n * m["s"]) * m["cy"], p=n * m["pe"],
                     i=150 + 2 * n * m["cy"], d=60.0, r=1000.0)[c]
        eng.append(ENG.index(o["eng"]))
        hold.append(x)
        lat.append(m["dma"] if c == "d" else m["far"] + n / (12.0 * REMOTE_ENGINES) if c == "r" else x)
        wire.append(0.0 if c != "d" else n / m["rate"])
    return eng, hold, lat, wire, [[(j, m["hop"] if sem else 0.0) for j, sem in p.items()] for p in pred]


def chains(seq, tab, state, a, b):
    eng, hold, full, wire, pre, suc = tab
    r, q, why = state
    last, w, seen = [-1] * 5, -1, 0
    for k in range(a - 1, -1, -1):
        i = seq[k]
        if last[eng[i]] < 0:
            last[eng[i]] = i
            seen += 1
        if w < 0 and wire[i]:
            w = i
            seen += 1
        if seen == 6:
            break
    for i in seq[a:]:
        e = eng[i]
        p = last[e]
        s, y, same = (r[p] + hold[p], p, True) if p >= 0 else (0.0, -1, True)
        for j, x in pre[i]:
            x += r[j]
            if x > s:
                s, y, same = x, j, False
        if wire[i]:
            if w >= 0 and r[w] + wire[w] > s:
                s, y, same = r[w] + wire[w], w, True
            w = i
        r[i] = s
        why[i] = (y, same)
        last[e] = i
    nxt, w, seen = [-1.0] * 5, -1.0, 0
    for i in seq[b + 1:]:
        if nxt[eng[i]] < 0:
            nxt[eng[i]] = q[i]
            seen += 1
        if w < 0 and wire[i]:
            w = q[i]
            seen += 1
        if seen == 6:
            break
    for i in seq[b::-1]:
        e = eng[i]
        s = nxt[e] + hold[i]
        if full[i] > s:
            s = full[i]
        for j, x in suc[i]:
            x += q[j]
            if x > s:
                s = x
        if wire[i]:
            if w + wire[i] > s:
                s = w + wire[i]
            w = s
        q[i] = nxt[e] = s


def through(seq, mid, a, b, pos, tab, state):
    eng, hold, full, wire, pre, suc = tab
    r, q, why = state
    free, w, used, wired = [0.0] * 5, 0.0, 0, False
    for i in mid:
        used |= 1 << eng[i]
        if wire[i]:
            wired = True
    need, look = used, wired
    for k in range(a - 1, -1, -1):
        i = seq[k]
        m = 1 << eng[i]
        if need & m:
            need ^= m
            free[eng[i]] = r[i] + hold[i]
        if look and wire[i]:
            w, look = r[i] + wire[i], False
        if not need and not look:
            break
    new, out = {}, 0.0
    for i in mid:
        e = eng[i]
        s = free[e]
        for j, x in pre[i]:
            x += new[j] if j in new else r[j]
            if x > s:
                s = x
        if wire[i]:
            if w > s:
                s = w
            w = s + wire[i]
        new[i] = s
        free[e] = s + hold[i]
        t = full[i]
        for j, x in suc[i]:
            if pos[j] > b and x + q[j] > t:
                t = x + q[j]
        if s + t > out:
            out = s + t
    for k in range(b + 1, len(seq)):
        i = seq[k]
        m = 1 << eng[i]
        if used & m:
            used ^= m
            if free[eng[i]] + q[i] > out:
                out = free[eng[i]] + q[i]
        if wired and wire[i]:
            wired = False
            if w + q[i] > out:
                out = w + q[i]
        if not used and not wired:
            break
    return out


def first_order(ops, pred, tab):
    eng, hold, lat, wire, inn = tab
    n = len(ops)
    succ = [[] for _ in range(n)]
    for i in range(n):
        for j, h in inn[i]:
            succ[j].append((i, h))
    rest = [0.0] * n
    for i in range(n - 1, -1, -1):
        rest[i] = lat[i] + wire[i] + max([h + rest[j] for j, h in succ[i]], default=0.0)
    left = [len(p) for p in pred]
    ready, free, w = [0.0] * n, [0.0] * 5, 0.0
    cand = [[i for i in range(n) if not left[i] and eng[i] == e] for e in range(5)]
    seq = []
    for _ in range(n):
        best = None
        for e in range(5):
            if cand[e]:
                t0 = max(free[e], min(ready[j] for j in cand[e]))
                i = max((j for j in cand[e] if ready[j] <= t0), key=lambda j: rest[j])
                t0 = max(t0, ready[i])
                if best is None or t0 < best[0]:
                    best = (t0, e, i)
        s, e, i = best
        cand[e].remove(i)
        seq.append(i)
        free[e] = s + hold[i]
        d = s + lat[i]
        if wire[i]:
            d = w = max(w, d) + wire[i]
        for j, h in succ[i]:
            ready[j] = max(ready[j], d + h)
            left[j] -= 1
            if not left[j]:
                cand[eng[j]].append(j)
    return seq


def improve(seq, pred, tabs, tries, hot, cold, rng):
    n, seq, full = len(seq), list(seq), []
    for eng, hold, lat, wire, inn in tabs:
        pre = [[(j, lat[j] + wire[j] + h) for j, h in p] for p in inn]
        suc = [[] for _ in range(n)]
        for i in range(n):
            for j, x in pre[i]:
                suc[j].append((i, x))
        full.append((eng, hold, [a + b for a, b in zip(lat, wire)], wire, pre, suc))
    succ = [[j for j, _ in l] for l in full[0][5]]
    ends = [i for i in range(n) if not succ[i]]
    states = [([0.0] * n, [0.0] * n, [None] * n) for _ in tabs]
    pos = [0] * n
    best, fresh, a, b = (1e18, seq), True, 0, n - 1
    for k, r in enumerate(rng.random((tries, 5)).tolist()):
        if fresh:
            for c in range(a, b + 1):
                pos[seq[c]] = c
            paths, tots, fresh = [], [], False
            for t, s in zip(full, states):
                chains(seq, t, s, a, b)
                tot, i = max((s[0][i] + t[2][i], i) for i in ends)
                p, why = [], s[2]
                while i >= 0:
                    y = why[i][0]
                    if why[i][1] and y >= 0:
                        p.append((i, y))
                    i = y
                paths.append(p)
                tots.append(tot)
            cur = sum(tots)
            if cur < best[0]:
                best = (cur, seq[:])
        p = paths[int(r[0] * len(paths))]
        i, y = p[int(r[1] * len(p))]
        if k % FREE == 0:
            b = 1 + int(r[1] * (n - 1))
            i = seq[b]
            y = next((seq[c] for c in range(b - 1, -1, -1) if eng[seq[c]] == eng[i]), i)
        a, b = pos[y], pos[i]
        more = int(-1.5 * math.log(1.0 - r[2]))
        if r[3] < 0.5:
            while more and a > 0:
                a -= 1
                more -= eng[seq[a]] == eng[i]
            want, front, back = {i}, [], []
            for j in seq[b:a - 1 if a else None:-1]:
                if j in want:
                    want.update(pred[j])
                    front.append(j)
                else:
                    back.append(j)
            mid = front[::-1] + back[::-1]
        else:
            while more and b < n - 1:
                b += 1
                more -= eng[seq[b]] == eng[i]
            want, front, back = {y}, [], []
            for j in seq[a:b + 1]:
                if j in want:
                    want.update(succ[j])
                    back.append(j)
                else:
                    front.append(j)
            mid = front + back
        if mid == seq[a:b + 1]:
            continue
        limit = cur - len(tabs) * hot * (cold / hot) ** (k / tries) * math.log(1.0 - r[4])
        if sum(max(through(seq, mid, a, b, pos, t, s), x - 1.0) for t, s, x in zip(full, states, tots)) <= limit:
            seq[a:b + 1] = mid
            fresh = True
    return best[1]


def arrange(ops, pred):
    tabs = [tables(ops, pred, m) for m in MODELS]
    rng = np.random.default_rng(SEED)
    seq = first_order(ops, pred, tabs[0])
    for count, tries, hot, cold in ROUNDS:
        seq = improve(seq, pred, tabs[:count], tries, hot, cold, rng)
    return seq


PLAN = {}


def rank_program(g, core, T, topo):
    if T.rank_of(core) is None:
        return
    ops = build_ops(g, T, topo, core)
    if "seq" not in PLAN:
        PLAN["pred"] = depends(ops)
        PLAN["seq"] = arrange(ops, PLAN["pred"])
    pred, seq = PLAN["pred"], PLAN["seq"]
    queue = dict(pe=g.tensor, dve=g.vector, act=g.scalar, pool=g, sp=g.sync)
    place = {i: k for k, i in enumerate(seq)}
    name = lambda j: ops[j]["eng"] if ops[j]["kind"] == "c" else ops[j]["sem"]
    known = {e: {} for e in ENG}
    knew, waits, marked = {}, {}, set()
    for i in seq:
        mine = known[ops[i]["eng"]]
        waits[i] = []
        for j in sorted((j for j, sem in pred[i].items() if sem), key=lambda j: -place[j]):
            if mine.get(name(j), -1) < place[j]:
                waits[i].append(j)
                marked.add(j)
                mine[name(j)] = place[j]
                if ops[j]["kind"] != "send":
                    for key, val in knew[j].items():
                        mine[key] = max(mine.get(key, -1), val)
        knew[i] = dict(mine)
    signal, total = {}, {}
    for i in seq:
        o = ops[i]
        if o["kind"] == "dma":
            signal[i] = (o["sem"], 16)
        elif o["kind"] == "send":
            signal[i] = (o["sem"], REMOTE_ENGINES)
            total["sent"] = total.get("sent", 0) + REMOTE_ENGINES
        elif i in marked:
            signal[i] = ("q_" + o["eng"], total.get("q_" + o["eng"], 0) + 1)
        else:
            continue
        total[signal[i][0]] = signal[i][1]
    for e in ENG:
        for i in seq:
            if ops[i]["eng"] != e:
                continue
            for j in waits[i]:
                queue[e].wait_ge(T.sem[signal[j][0]], signal[j][1])
            ins = ops[i]["fn"]()
            if ops[i]["kind"] == "dma":
                ins.then_inc(T.sem[signal[i][0]], 16)
            elif ops[i]["kind"] == "c" and i in marked:
                ins.then_inc(T.sem[signal[i][0]], 1)
    for key, val in total.items():
        g.wait_ge(T.sem[key], val)
